import numpy as np
import ml_dtypes


def mxq(x, axis, fmt="e4m3"):
    dtype, down = {"e4m3": (ml_dtypes.float8_e4m3fn, 7), "e5m2": (ml_dtypes.float8_e5m2, 14)}[fmt]
    v = np.moveaxis(np.asarray(x, np.float32).astype(ml_dtypes.bfloat16).astype(np.float64), axis, -1)
    blocks = v.reshape(v.shape[:-1] + (-1, 32))
    amax = np.abs(blocks).max(-1, keepdims=True)
    byte = np.maximum(np.where(amax > 0, np.frexp(amax)[1] - 1 + 127, 0) - down, 1)
    scale = np.exp2(byte - 127.0)
    codes = (blocks / scale).astype(np.float32).astype(dtype).astype(np.float64)
    return np.moveaxis((codes * scale).reshape(v.shape), -1, axis)


WIDE = False


def mx_kscale(k):
    if not WIDE:
        return np.ones(k)
    levels = np.array([10, -10, 5, -5, 0])
    if k % 512:
        return np.exp2(np.random.permutation(np.resize(levels, k // 32))).repeat(32)
    a = np.empty((k // 512, 16))
    for p in range(k // 512):
        a[p, :8] = np.random.permutation(np.resize(levels, 8))
        for g in range(8):
            far = levels[np.abs(levels - a[p, g]) >= 10]
            a[p, g + 8] = far[np.random.randint(len(far))]
    return np.exp2(a.ravel()).repeat(32)


def f64(x):
    return np.asarray(x).astype(np.float64)


def striped(idx):
    return np.tile(idx.reshape(-1, 16).T, (8, 1)).astype(np.uint16)


def unstriped(offs):
    return offs[:16].T.reshape(-1).astype(np.int64)


def pack_weight(w):
    k, n = w.shape
    w = f64(np.asarray(w, np.float32).astype(ml_dtypes.bfloat16)).reshape(k // 32, 32, n)
    amax = np.abs(w).max(1)
    byte = np.clip(np.where(amax > 0, np.frexp(amax)[1] - 1 + 127 - 7, 1), 1, 254)
    scaled = (w * np.exp2(127.0 - byte)[:, None, :]).reshape(k, n).astype(np.float32)
    words = np.ascontiguousarray(scaled.reshape(k // 512, 128, 4, n).transpose(0, 1, 3, 2)).astype(ml_dtypes.float8_e4m3fn).view(np.uint8)
    return words, np.ascontiguousarray(byte.astype(np.uint8).reshape(k // 512, 16, n))


def unpack_weight(words, scales):
    g, p, n, _ = words.shape
    vals = np.ascontiguousarray(words).view(ml_dtypes.float8_e4m3fn).astype(np.float64) * np.repeat(np.exp2(scales.astype(np.float64) - 127.0), 8, axis=1)[..., None]
    return vals.transpose(0, 1, 3, 2).reshape(g * 512, n)


E2M1 = np.array([0.0, 0.5, 1.0, 1.5, 2.0, 3.0, 4.0, 6.0, -0.0, -0.5, -1.0, -1.5, -2.0, -3.0, -4.0, -6.0])


def pack_fp4(w):
    k, n = w.shape
    w = f64(np.asarray(w, np.float32).astype(ml_dtypes.bfloat16)).reshape(k // 32, 32, n)
    amax = np.abs(w).max(1)
    mant, ex = np.frexp(amax / 6.0)
    byte = np.clip(np.where(amax > 0, np.where(mant > 0.5, ex, ex - 1) + 127, 1), 1, 254)
    scaled = (w * np.exp2(127.0 - byte)[:, None, :]).reshape(k, n).astype(np.float32)
    c = np.ascontiguousarray(scaled.reshape(k // 512, 128, 4, n).transpose(0, 1, 3, 2)).astype(ml_dtypes.float4_e2m1fn).view(np.uint8) & 0xF
    words = (c[..., 0::2] | (c[..., 1::2] << 4)).reshape(k // 512, 128, 2 * n)
    return np.ascontiguousarray(words), np.ascontiguousarray(byte.astype(np.uint8).reshape(k // 512, 16, n))


def unpack_fp4(words, scales):
    g, _, n = scales.shape
    words = np.ascontiguousarray(words).reshape(g, 128, n, 2)
    nib = np.empty((g, 128, n, 4), np.uint8)
    nib[..., 0::2] = words & 0xF
    nib[..., 1::2] = words >> 4
    vals = E2M1[nib] * np.repeat(np.exp2(scales.astype(np.float64) - 127.0), 8, axis=1)[..., None]
    return vals.transpose(0, 1, 3, 2).reshape(g * 512, n)


def relu(v):
    return np.maximum(v, 0.0)


K, T, S, D, V, H, N, U = 512, 2048, 512, 4, 512, 512, 128, 1024
P = 2 ** 7


def setup_inputs():
    n = np.random.standard_normal
    s = mx_kscale(K)[:, None]
    u = mx_kscale(H)
    packed_xT = pack_weight(n((K, T)) * s)
    packed_w2 = pack_fp4(n((H, N)) / np.sqrt(H) / u[:, None])
    return {
        "x_words": packed_xT[0],
        "x_scales": packed_xT[1],
        "w1": (n((K, H)) / np.sqrt(K) / s * u).astype(np.float32),
        "w2_words": packed_w2[0],
        "w2_scales": packed_w2[1],
        "gate": np.tile(np.random.uniform(0.2, 0.6, (D, 1, V)), (1, P, 1)).astype(np.float32),
        "emb": (0.5 * n((H, U)) * u[:, None]).astype(np.float32),
        "offs": striped(np.random.permutation(T)[:S]),
        "cell": striped(np.random.permutation(U)[:S]),
        "pos1": striped(np.random.permutation(U)[:V]),
        "pos2": striped(np.random.permutation(U)[:V]),
        "pos3": striped(np.random.permutation(U)[:V]),
        "pos4": striped(np.random.permutation(U)[:V]),
    }


def reference(x_words, x_scales, w1, w2_words, w2_scales, gate, emb, offs, cell, pos1, pos2, pos3, pos4):
    xq = unpack_weight(x_words, x_scales)[:, unstriped(offs)]
    up = np.zeros((H, U))
    up[:, unstriped(cell)] = relu(mxq(f64(w1), 0, "e4m3").T @ xq)
    z = up + f64(emb)
    y = relu(unpack_fp4(w2_words, w2_scales).T @ mxq(z, 0, "e4m3"))
    return y[:, unstriped(pos1)] * f64(gate)[0, :1] + y[:, unstriped(pos2)] * f64(gate)[1, :1] + y[:, unstriped(pos3)] * f64(gate)[2, :1] + y[:, unstriped(pos4)] * f64(gate)[3, :1]

@@ -1,0 +1,178 @@
+from contextlib import ExitStack
+
+import concourse.mybir as mybir
+
+K, T, S, D, V, H, N, U = 512, 2048, 512, 4, 512, 512, 128, 1024
+FLOPS = 2 * K * H * S + 2 * H * N * U
+
+F32 = mybir.dt.float32
+BF16 = mybir.dt.bfloat16
+I32 = mybir.dt.int32
+U32 = mybir.dt.uint32
+U16 = mybir.dt.uint16
+U8 = mybir.dt.uint8
+FP8X4 = mybir.dt.float8_e4m3fn_x4
+FP4X4 = mybir.dt.float4_e2m1fn_x4
+ADD = mybir.AluOpType.add
+MULT = mybir.AluOpType.mult
+RELU = mybir.ActivationFunctionType.Relu
+
+P = 128
+PACK = 4
+LANES = 16
+CHUNKS = 4
+CW = U // CHUNKS
+
+
+def tile_picked_devox_relu_p_kernel(
+    tc, x_words, x_scales, w1, w2_words, w2_scales, gate, emb, offs, cell, pos1, pos2, pos3, pos4, out
+):
+    nc = tc.nc
+    with ExitStack() as ctx:
+        lists = ctx.enter_context(tc.tile_pool(name="lists", bufs=1))
+        keep = ctx.enter_context(tc.tile_pool(name="keep", bufs=1))
+        psum = ctx.enter_context(tc.psum_pool(name="psum", bufs=1))
+
+        def load_list(name, src):
+            t = lists.tile([P, S // LANES], U16, name=name)
+            nc.sync.dma_start(t[:], src)
+            return t
+
+        def load_scale_rows(queue, plane, src):
+            for q in range(4):
+                queue.dma_start(
+                    plane[32 * q : 32 * q + 4, :].bitcast(I32), src[0, 4 * q : 4 * q + 4, :].bitcast(I32)
+                )
+
+        offs_t = load_list("offs_t", offs)
+        xs_all = keep.tile([P, T], U8, name="xs_all", align_bytes=64)
+        nc.gpsimd.memset(xs_all[:].bitcast(I32), 0)
+        load_scale_rows(nc.scalar, xs_all, x_scales)
+
+        w1_rows = w1.rearrange("(p j) c -> p j c", j=PACK)
+        half = H // 2
+        w1_raw = []
+        for a in range(2):
+            raw = keep.tile([P, PACK, half], F32, name=f"w1_raw{a}", tag=f"stage{a}")
+            nc.sync.dma_start(raw[:], w1_rows[:, :, a * half : (a + 1) * half])
+            w1_raw.append(raw)
+        xw_all = keep.tile([P, T], U32, name="xw_all", tag="stage2")
+        nc.sync.dma_start(xw_all[:].bitcast(I32), x_words[0].rearrange("p n t -> p (n t)").bitcast(I32))
+        cell_t = load_list("cell_t", cell)
+
+        ups = []
+        for t in range(PACK):
+            up = keep.tile([P, U], F32, name=f"up{t}")
+            nc.vector.memset(up[:], 0.0)
+            ups.append(up)
+
+        w1_bf = keep.tile([P, PACK, P, PACK], BF16, name="w1_bf", align_bytes=64)
+        dealt = w1_bf[:].rearrange("p t (g e) j -> p g j e t", e=2)
+        for a in range(2):
+            nc.scalar.copy(
+                dealt[:, a * 32 : (a + 1) * 32],
+                w1_raw[a][:].rearrange("p j (g e t) -> p g j e t", e=2, t=PACK),
+            )
+        xs_g = keep.tile([P, S], U8, name="xs_g", align_bytes=64)
+        nc.vector.tensor_copy(xs_g[:], xs_all[:].indirect(offs_t[:]))
+        w1_q = keep.tile([P, H], U32, name="w1_q", align_bytes=64)
+        w1_s = keep.tile([P, H], U8, name="w1_s", align_bytes=64)
+        nc.vector.quantize_mx(
+            out=w1_q[:].bitcast(FP8X4), scales=w1_s[:], in_=w1_bf[:].rearrange("p t m j -> p (t m j)")
+        )
+        xw_g = [keep.tile([P, 256], U32, name=f"xw_g{a}", align_bytes=64) for a in range(2)]
+        for a in range(2):
+            nc.vector.tensor_copy(xw_g[a][:], xw_all[:].indirect(offs_t[:, a * 16 : (a + 1) * 16]))
+
+        emb_rows = emb.rearrange("(p t) c -> p t c", t=PACK)
+        emb1 = keep.tile([P, U], F32, name="emb1", tag="stage1")
+        nc.sync.dma_start(emb1[:], emb_rows[:, 1, :])
+        emb0 = keep.tile([P, U], F32, name="emb0", tag="stage0")
+        nc.sync.dma_start(emb0[:], emb_rows[:, 0, :])
+        emb23 = keep.tile([P, 2, U], F32, name="emb23", tag="stage2")
+        nc.sync.dma_start(emb23[:], emb_rows[:, 2:4, :])
+        embs = [emb0[:], emb1[:], emb23[:, 0, :], emb23[:, 1, :]]
+        pos_t = [load_list(f"pos{d}_t", src) for d, src in enumerate((pos1, pos2, pos3, pos4))]
+        w2_q = keep.tile([P, 2 * N], U8, name="w2_q", align_bytes=64)
+        nc.sync.dma_start(w2_q[:].bitcast(I32), w2_words[0].bitcast(I32))
+        w2_s = keep.tile([P, N], U8, name="w2_s", align_bytes=64)
+        nc.vector.memset(w2_s[:].bitcast(I32), 0)
+        load_scale_rows(nc.sync, w2_s, w2_scales)
+
+        pieces = [(0, 0, 256), (0, 256, 512), (1, 0, 512), (2, 0, 512), (3, 0, 512)]
+        for i, (t, lo, hi) in enumerate(pieces):
+            acc = psum.tile([P, hi - lo], F32, name=f"h_acc{i}", tag=f"bank{i}")
+            for c0 in range(lo, hi, 256):
+                nc.tensor.matmul_mx(
+                    out=acc[:, c0 - lo : c0 - lo + 256],
+                    lhsT=w1_q[:, t * P : (t + 1) * P].bitcast(FP8X4),
+                    lhsT_scale=w1_s[:, t * P : (t + 1) * P],
+                    rhs=xw_g[c0 // 256][:].bitcast(FP8X4),
+                    rhs_scale=xs_g[:, c0 : c0 + 256],
+                    start=True,
+                    stop=True,
+                )
+            h = keep.tile([P, hi - lo], F32, name=f"h{i}")
+            nc.scalar.activation(h[:], acc[:], RELU)
+            nc.vector.tensor_copy(ups[t][:].indirect(cell_t[:, lo // LANES : hi // LANES]), h[:])
+
+        z01 = keep.tile([P, 2, U], BF16, name="z01")
+        for t in (0, 1):
+            nc.gpsimd.tensor_tensor(z01[:, t, :], ups[t][:], embs[t], ADD)
+        gates = []
+        for a in range(2):
+            g = keep.tile([P, 2, V], F32, name=f"gate{a}", tag=f"stage{a}")
+            nc.sync.dma_start(g[:], gate[2 * a : 2 * a + 2].rearrange("d p v -> p d v"))
+            gates += [g[:, 0, :], g[:, 1, :]]
+
+        z_bf = [keep.tile([P, CW, 2, 2], BF16, name=f"z_bf{c}", align_bytes=64) for c in range(CHUNKS)]
+        z23 = [keep.tile([P, 2, CW], BF16, name=f"z23_{c}") for c in range(CHUNKS)]
+        for c in range(CHUNKS):
+            cols = slice(c * CW, (c + 1) * CW)
+            nc.scalar.copy(z_bf[c][:, :, 0, :], z01[:, :, cols].rearrange("p e c -> p c e"))
+        for c in range(CHUNKS):
+            cols = slice(c * CW, (c + 1) * CW)
+            nc.gpsimd.tensor_tensor(z23[c][:, 0, :], ups[2][:, cols], embs[2][:, cols], ADD)
+        for c in range(CHUNKS):
+            cols = slice(c * CW, (c + 1) * CW)
+            nc.vector.tensor_tensor(z23[c][:, 1, :], ups[3][:, cols], embs[3][:, cols], ADD)
+        for c in range(CHUNKS):
+            pair = z23[c][:].rearrange("p e c -> p c e")
+            if c < 2:
+                nc.scalar.copy(z_bf[c][:, :, 1, :], pair)
+            else:
+                nc.vector.tensor_copy(z_bf[c][:, :, 1, :], pair)
+
+        y = keep.tile([P, U], F32, name="y")
+        for c in range(CHUNKS):
+            z_q = keep.tile([P, CW], U32, name=f"z_q{c}", align_bytes=64)
+            z_s = keep.tile([P, CW], U8, name=f"z_s{c}", align_bytes=64)
+            nc.vector.quantize_mx(
+                out=z_q[:].bitcast(FP8X4), scales=z_s[:], in_=z_bf[c][:].rearrange("p c a e -> p (c a e)")
+            )
+            acc = psum.tile([P, CW], F32, name=f"y_acc{c}", tag=f"bank{(5 + c) % 8}")
+            nc.tensor.matmul_mx(
+                out=acc[:],
+                lhsT=w2_q[:].bitcast(FP4X4),
+                lhsT_scale=w2_s[:],
+                rhs=z_q[:].bitcast(FP8X4),
+                rhs_scale=z_s[:],
+                start=True,
+                stop=True,
+            )
+            nc.scalar.activation(y[:, c * CW : (c + 1) * CW], acc[:], RELU)
+
+        terms = [keep.tile([P, V], F32, name=f"term{d}") for d in range(D)]
+        sum01 = keep.tile([P, V], F32, name="sum01")
+        sum012 = keep.tile([P, V], F32, name="sum012")
+        for d in range(3):
+            nc.vector.tensor_tensor(terms[d][:], y[:].indirect(pos_t[d][:]), gates[d], MULT)
+        nc.vector.tensor_tensor(sum01[:], terms[0][:], terms[1][:], ADD)
+        nc.vector.tensor_tensor(terms[3][:, 0:256], y[:].indirect(pos_t[3][:, 0:16]), gates[3][:, 0:256], MULT)
+        nc.vector.tensor_tensor(sum012[:], sum01[:], terms[2][:], ADD)
+        nc.vector.tensor_tensor(terms[3][:, 256:512], y[:].indirect(pos_t[3][:, 16:32]), gates[3][:, 256:512], MULT)
+        for a in range(2):
+            cols = slice(a * 256, (a + 1) * 256)
+            res = keep.tile([P, 256], F32, name=f"res{a}")
+            nc.vector.tensor_tensor(res[:], sum012[:, cols], terms[3][:, cols], ADD)
+            nc.sync.dma_start(out[:, cols], res[:])

@@ -1,6 +1,7 @@
 from contextlib import ExitStack
 
 import concourse.mybir as mybir
+from concourse.masks import make_identity
 
 K, T, S, D, V, H, N, U = 512, 2048, 512, 4, 512, 512, 128, 1024
 FLOPS = 2 * K * H * S + 2 * H * N * U
@@ -44,10 +45,8 @@ def tile_picked_devox_relu_p_kernel(
                     plane[32 * q : 32 * q + 4, :].bitcast(I32), src[0, 4 * q : 4 * q + 4, :].bitcast(I32)
                 )
 
-        offs_t = load_list("offs_t", offs)
         xs_all = keep.tile([P, T], U8, name="xs_all", align_bytes=64)
         nc.gpsimd.memset(xs_all[:].bitcast(I32), 0)
-        load_scale_rows(nc.scalar, xs_all, x_scales)
 
         w1_rows = w1.rearrange("(p j) c -> p j c", j=PACK)
         half = H // 2
@@ -56,6 +55,9 @@ def tile_picked_devox_relu_p_kernel(
             raw = keep.tile([P, PACK, half], F32, name=f"w1_raw{a}", tag=f"stage{a}")
             nc.sync.dma_start(raw[:], w1_rows[:, :, a * half : (a + 1) * half])
             w1_raw.append(raw)
+            if a == 0:
+                offs_t = load_list("offs_t", offs)
+                load_scale_rows(nc.sync, xs_all, x_scales)
         xw_all = keep.tile([P, T], U32, name="xw_all", tag="stage2")
         nc.sync.dma_start(xw_all[:].bitcast(I32), x_words[0].rearrange("p n t -> p (n t)").bitcast(I32))
         cell_t = load_list("cell_t", cell)
@@ -99,21 +101,26 @@ def tile_picked_devox_relu_p_kernel(
         nc.vector.memset(w2_s[:].bitcast(I32), 0)
         load_scale_rows(nc.sync, w2_s, w2_scales)
 
-        pieces = [(0, 0, 256), (0, 256, 512), (1, 0, 512), (2, 0, 512), (3, 0, 512)]
+        pieces = [(0, 0, 128), (1, 0, 256), (0, 128, 512), (1, 256, 512), (2, 0, 512), (3, 0, 512)]
         for i, (t, lo, hi) in enumerate(pieces):
             acc = psum.tile([P, hi - lo], F32, name=f"h_acc{i}", tag=f"bank{i}")
-            for c0 in range(lo, hi, 256):
+            for c0, c1 in ((lo, min(hi, 256)), (max(lo, 256), hi)):
+                if c0 >= c1:
+                    continue
                 nc.tensor.matmul_mx(
-                    out=acc[:, c0 - lo : c0 - lo + 256],
+                    out=acc[:, c0 - lo : c1 - lo],
                     lhsT=w1_q[:, t * P : (t + 1) * P].bitcast(FP8X4),
                     lhsT_scale=w1_s[:, t * P : (t + 1) * P],
-                    rhs=xw_g[c0 // 256][:].bitcast(FP8X4),
-                    rhs_scale=xs_g[:, c0 : c0 + 256],
+                    rhs=xw_g[c0 // 256][:, c0 % 256 : c0 % 256 + c1 - c0].bitcast(FP8X4),
+                    rhs_scale=xs_g[:, c0:c1],
                     start=True,
                     stop=True,
                 )
             h = keep.tile([P, hi - lo], F32, name=f"h{i}")
-            nc.scalar.activation(h[:], acc[:], RELU)
+            if i == 0:
+                nc.vector.tensor_scalar_max(h[:], acc[:], 0.0)
+            else:
+                nc.scalar.activation(h[:], acc[:], RELU)
             nc.vector.tensor_copy(ups[t][:].indirect(cell_t[:, lo // LANES : hi // LANES]), h[:])
 
         z01 = keep.tile([P, 2, U], BF16, name="z01")
@@ -125,32 +132,39 @@ def tile_picked_devox_relu_p_kernel(
             nc.sync.dma_start(g[:], gate[2 * a : 2 * a + 2].rearrange("d p v -> p d v"))
             gates += [g[:, 0, :], g[:, 1, :]]
 
-        z_bf = [keep.tile([P, CW, 2, 2], BF16, name=f"z_bf{c}", align_bytes=64) for c in range(CHUNKS)]
-        z23 = [keep.tile([P, 2, CW], BF16, name=f"z23_{c}") for c in range(CHUNKS)]
-        for c in range(CHUNKS):
-            cols = slice(c * CW, (c + 1) * CW)
-            nc.scalar.copy(z_bf[c][:, :, 0, :], z01[:, :, cols].rearrange("p e c -> p c e"))
-        for c in range(CHUNKS):
-            cols = slice(c * CW, (c + 1) * CW)
-            nc.gpsimd.tensor_tensor(z23[c][:, 0, :], ups[2][:, cols], embs[2][:, cols], ADD)
-        for c in range(CHUNKS):
-            cols = slice(c * CW, (c + 1) * CW)
-            nc.vector.tensor_tensor(z23[c][:, 1, :], ups[3][:, cols], embs[3][:, cols], ADD)
-        for c in range(CHUNKS):
-            pair = z23[c][:].rearrange("p e c -> p c e")
-            if c < 2:
-                nc.scalar.copy(z_bf[c][:, :, 1, :], pair)
+        chunks = [(0, 2, nc.scalar), (2, 4, nc.scalar), (4, 5, nc.scalar), (5, 7, nc.vector), (7, 8, nc.vector)]
+        z_bf = [
+            keep.tile([P, hi - lo, P, 2, 2], BF16, name=f"z_bf{c}", align_bytes=64)
+            for c, (lo, hi, eng) in enumerate(chunks)
+        ]
+        z01_b = z01[:].rearrange("p e (b c) -> p b c e", c=P)
+        for c, (lo, hi, eng) in enumerate(chunks):
+            nc.scalar.copy(z_bf[c][:, :, :, 0, :], z01_b[:, lo:hi])
+        z23_row = keep.tile([P, 2 * U], BF16, name="z23_row")
+        z23 = z23_row[:].rearrange("p (b e c) -> p b e c", e=2, c=P)
+        up_b = [ups[t][:].rearrange("p (b c) -> p b c", c=P) for t in (2, 3)]
+        emb_b = [embs[t].rearrange("p (b c) -> p b c", c=P) for t in (2, 3)]
+        nc.gpsimd.tensor_tensor(z23[:, :, 0, :], up_b[0], emb_b[0], ADD)
+        for lo, hi in ((0, 2), (2, 5), (5, 8)):
+            nc.vector.tensor_tensor(z23[:, lo:hi, 1, :], up_b[1][:, lo:hi], emb_b[1][:, lo:hi], ADD)
+        for c, (lo, hi, eng) in enumerate(chunks):
+            pair = z23[:, lo:hi].rearrange("p b e c -> p b c e")
+            if c < 3:
+                nc.scalar.copy(z_bf[c][:, :, :, 1, :], pair)
             else:
-                nc.vector.tensor_copy(z_bf[c][:, :, 1, :], pair)
+                nc.vector.tensor_copy(z_bf[c][:, :, :, 1, :], pair)
 
         y = keep.tile([P, U], F32, name="y")
-        for c in range(CHUNKS):
-            z_q = keep.tile([P, CW], U32, name=f"z_q{c}", align_bytes=64)
-            z_s = keep.tile([P, CW], U8, name=f"z_s{c}", align_bytes=64)
+        late = []
+        for i, c in enumerate((0, 1, 3, 4, 2)):
+            lo, hi, eng = chunks[c]
+            w = (hi - lo) * P
+            z_q = keep.tile([P, w], U32, name=f"z_q{c}", align_bytes=64)
+            z_s = keep.tile([P, w], U8, name=f"z_s{c}", align_bytes=64)
             nc.vector.quantize_mx(
-                out=z_q[:].bitcast(FP8X4), scales=z_s[:], in_=z_bf[c][:].rearrange("p c a e -> p (c a e)")
+                out=z_q[:].bitcast(FP8X4), scales=z_s[:], in_=z_bf[c][:].rearrange("p b c a e -> p (b c a e)")
             )
-            acc = psum.tile([P, CW], F32, name=f"y_acc{c}", tag=f"bank{(5 + c) % 8}")
+            acc = psum.tile([P, w], F32, name=f"y_acc{c}", tag=f"bank{(6 + i) % 8}")
             nc.tensor.matmul_mx(
                 out=acc[:],
                 lhsT=w2_q[:].bitcast(FP4X4),
@@ -160,19 +174,46 @@ def tile_picked_devox_relu_p_kernel(
                 start=True,
                 stop=True,
             )
-            nc.scalar.activation(y[:, c * CW : (c + 1) * CW], acc[:], RELU)
+            if i < 3:
+                nc.scalar.activation(y[:, lo * P : hi * P], acc[:], RELU)
+            else:
+                late.append((y[:, lo * P : hi * P], acc))
+        for dst, acc in late:
+            nc.vector.tensor_scalar_max(dst, acc[:], 0.0)
 
-        terms = [keep.tile([P, V], F32, name=f"term{d}") for d in range(D)]
-        sum01 = keep.tile([P, V], F32, name="sum01")
-        sum012 = keep.tile([P, V], F32, name="sum012")
-        for d in range(3):
-            nc.vector.tensor_tensor(terms[d][:], y[:].indirect(pos_t[d][:]), gates[d], MULT)
-        nc.vector.tensor_tensor(sum01[:], terms[0][:], terms[1][:], ADD)
-        nc.vector.tensor_tensor(terms[3][:, 0:256], y[:].indirect(pos_t[3][:, 0:16]), gates[3][:, 0:256], MULT)
-        nc.vector.tensor_tensor(sum012[:], sum01[:], terms[2][:], ADD)
-        nc.vector.tensor_tensor(terms[3][:, 256:512], y[:].indirect(pos_t[3][:, 16:32]), gates[3][:, 256:512], MULT)
-        for a in range(2):
-            cols = slice(a * 256, (a + 1) * 256)
-            res = keep.tile([P, 256], F32, name=f"res{a}")
-            nc.vector.tensor_tensor(res[:], sum012[:, cols], terms[3][:, cols], ADD)
-            nc.sync.dma_start(out[:, cols], res[:])
+        ident = keep.tile([P, P], F32, name="ident")
+        make_identity(nc, ident[:])
+        nb = 2
+        wa = nb * P
+        turned = [psum.tile([P, P], F32, name=f"turned{b}", tag=f"bank{3 + b}") for b in range(nb)]
+        for d in range(D):
+            term = keep.tile([P, wa], F32, name=f"term_a{d}")
+            nc.vector.tensor_tensor(term[:], y[:].indirect(pos_t[d][:, 0 : wa // LANES]), gates[d][:, 0:wa], MULT)
+            for b in range(nb):
+                nc.tensor.matmul(
+                    turned[b][:], term[:, b * P : (b + 1) * P], ident[:], start=(d == 0), stop=(d == D - 1), is_transpose=True
+                )
+        back = psum.tile([P, wa], F32, name="back", tag="bank5")
+        for b in range(nb):
+            sum_t = keep.tile([P, P], F32, name=f"sum_t{b}")
+            nc.scalar.copy(sum_t[:], turned[b][:])
+            nc.tensor.transpose(back[:, b * P : (b + 1) * P], sum_t[:], ident[:])
+        res_a = keep.tile([P, wa], F32, name="res_a")
+        nc.scalar.copy(res_a[:], back[:])
+        nc.scalar.dma_start(out[:, 0:wa], res_a[:])
+
+        wb = V - wa
+        terms = [keep.tile([P, wb], F32, name=f"term_b{d}") for d in range(D)]
+        sums = [keep.tile([P, wb], F32, name=f"sum_b{d}") for d in range(D - 1)]
+
+        def gather_b(d):
+            nc.vector.tensor_tensor(terms[d][:], y[:].indirect(pos_t[d][:, wa // LANES :]), gates[d][:, wa:], MULT)
+
+        gather_b(0)
+        gather_b(1)
+        gather_b(2)
+        nc.vector.tensor_tensor(sums[0][:], terms[0][:], terms[1][:], ADD)
+        gather_b(3)
+        nc.vector.tensor_tensor(sums[1][:], sums[0][:], terms[2][:], ADD)
+        nc.vector.tensor_tensor(sums[2][:], sums[1][:], terms[3][:], ADD)
+        nc.sync.dma_start(out[:, wa:], sums[2][:])

@@ -49,11 +49,10 @@ def tile_picked_devox_relu_p_kernel(
         nc.gpsimd.memset(xs_all[:].bitcast(I32), 0)
 
         w1_rows = w1.rearrange("(p j) c -> p j c", j=PACK)
-        half = H // 2
         w1_raw = []
         for a in range(2):
-            raw = keep.tile([P, PACK, half], F32, name=f"w1_raw{a}", tag=f"stage{a}")
-            nc.sync.dma_start(raw[:], w1_rows[:, :, a * half : (a + 1) * half])
+            raw = keep.tile([P, 2, H], F32, name=f"w1_raw{a}", tag=f"stage{a}")
+            nc.sync.dma_start(raw[:], w1_rows[:, 2 * a : 2 * a + 2, :])
             w1_raw.append(raw)
             if a == 0:
                 offs_t = load_list("offs_t", offs)
@@ -63,20 +62,19 @@ def tile_picked_devox_relu_p_kernel(
         cell_t = load_list("cell_t", cell)
 
         ups = []
-        for t in range(PACK):
+        for t in range(PACK - 1):
             up = keep.tile([P, U], F32, name=f"up{t}")
             nc.vector.memset(up[:], 0.0)
             ups.append(up)
+        ups.append(ups[0])
 
         w1_bf = keep.tile([P, PACK, P, PACK], BF16, name="w1_bf", align_bytes=64)
         dealt = w1_bf[:].rearrange("p t (g e) j -> p g j e t", e=2)
-        for a in range(2):
-            nc.scalar.copy(
-                dealt[:, a * 32 : (a + 1) * 32],
-                w1_raw[a][:].rearrange("p j (g e t) -> p g j e t", e=2, t=PACK),
-            )
+        w1_src = [raw[:].rearrange("p j (g e t) -> p g j e t", e=2, t=PACK) for raw in w1_raw]
+        nc.scalar.copy(dealt[:, :, 0:2], w1_src[0])
         xs_g = keep.tile([P, S], U8, name="xs_g", align_bytes=64)
         nc.vector.tensor_copy(xs_g[:], xs_all[:].indirect(offs_t[:]))
+        nc.vector.tensor_copy(dealt[:, :, 2:4], w1_src[1])
         w1_q = keep.tile([P, H], U32, name="w1_q", align_bytes=64)
         w1_s = keep.tile([P, H], U8, name="w1_s", align_bytes=64)
         nc.vector.quantize_mx(
@@ -87,13 +85,11 @@ def tile_picked_devox_relu_p_kernel(
             nc.vector.tensor_copy(xw_g[a][:], xw_all[:].indirect(offs_t[:, a * 16 : (a + 1) * 16]))
 
         emb_rows = emb.rearrange("(p t) c -> p t c", t=PACK)
-        emb1 = keep.tile([P, U], F32, name="emb1", tag="stage1")
-        nc.sync.dma_start(emb1[:], emb_rows[:, 1, :])
-        emb0 = keep.tile([P, U], F32, name="emb0", tag="stage0")
-        nc.sync.dma_start(emb0[:], emb_rows[:, 0, :])
+        emb01 = keep.tile([P, 2, U], F32, name="emb01", tag="stage1")
+        nc.sync.dma_start(emb01[:], emb_rows[:, 0:2, :])
         emb23 = keep.tile([P, 2, U], F32, name="emb23", tag="stage2")
         nc.sync.dma_start(emb23[:], emb_rows[:, 2:4, :])
-        embs = [emb0[:], emb1[:], emb23[:, 0, :], emb23[:, 1, :]]
+        embs = [emb01[:, 0, :], emb01[:, 1, :], emb23[:, 0, :], emb23[:, 1, :]]
         pos_t = [load_list(f"pos{d}_t", src) for d, src in enumerate((pos1, pos2, pos3, pos4))]
         w2_q = keep.tile([P, 2 * N], U8, name="w2_q", align_bytes=64)
         nc.sync.dma_start(w2_q[:].bitcast(I32), w2_words[0].bitcast(I32))
@@ -101,7 +97,11 @@ def tile_picked_devox_relu_p_kernel(
         nc.vector.memset(w2_s[:].bitcast(I32), 0)
         load_scale_rows(nc.sync, w2_s, w2_scales)
 
-        pieces = [(0, 0, 128), (1, 0, 256), (0, 128, 512), (1, 256, 512), (2, 0, 512), (3, 0, 512)]
+        z01_row = keep.tile([P, 2 * U], BF16, name="z01_row")
+        z01 = z01_row[:].rearrange("p (b e c) -> p b e c", e=2, c=P)
+        up_b = [up[:].rearrange("p (b c) -> p b c", c=P) for up in ups]
+        emb_b = [e.rearrange("p (b c) -> p b c", c=P) for e in embs]
+        pieces = [(0, 0, 128), (1, 0, 128), (0, 128, 512), (1, 128, 512), (2, 0, 512), (3, 0, 512)]
         for i, (t, lo, hi) in enumerate(pieces):
             acc = psum.tile([P, hi - lo], F32, name=f"h_acc{i}", tag=f"bank{i}")
             for c0, c1 in ((lo, min(hi, 256)), (max(lo, 256), hi)):
@@ -122,31 +122,29 @@ def tile_picked_devox_relu_p_kernel(
             else:
                 nc.scalar.activation(h[:], acc[:], RELU)
             nc.vector.tensor_copy(ups[t][:].indirect(cell_t[:, lo // LANES : hi // LANES]), h[:])
+            if hi == S and t == 0:
+                nc.gpsimd.tensor_tensor(z01[:, :, 0, :], up_b[0], emb_b[0], ADD)
+            if hi == S and t == 1:
+                for b0 in (0, 4):
+                    nc.gpsimd.tensor_tensor(z01[:, b0 : b0 + 4, 1, :], up_b[1][:, b0 : b0 + 4], emb_b[1][:, b0 : b0 + 4], ADD)
 
-        z01 = keep.tile([P, 2, U], BF16, name="z01")
-        for t in (0, 1):
-            nc.gpsimd.tensor_tensor(z01[:, t, :], ups[t][:], embs[t], ADD)
-        gates = []
-        for a in range(2):
-            g = keep.tile([P, 2, V], F32, name=f"gate{a}", tag=f"stage{a}")
-            nc.sync.dma_start(g[:], gate[2 * a : 2 * a + 2].rearrange("d p v -> p d v"))
-            gates += [g[:, 0, :], g[:, 1, :]]
+        gate_t = keep.tile([P, D, V], F32, name="gate_t", tag="stage1")
+        nc.sync.dma_start(gate_t[:], gate.rearrange("d p v -> p d v"))
+        gates = [gate_t[:, d, :] for d in range(D)]
 
         chunks = [(0, 2, nc.scalar), (2, 4, nc.scalar), (4, 5, nc.scalar), (5, 7, nc.vector), (7, 8, nc.vector)]
         z_bf = [
             keep.tile([P, hi - lo, P, 2, 2], BF16, name=f"z_bf{c}", align_bytes=64)
             for c, (lo, hi, eng) in enumerate(chunks)
         ]
-        z01_b = z01[:].rearrange("p e (b c) -> p b c e", c=P)
+        z01_b = z01.rearrange("p b e c -> p b c e")
         for c, (lo, hi, eng) in enumerate(chunks):
             nc.scalar.copy(z_bf[c][:, :, :, 0, :], z01_b[:, lo:hi])
         z23_row = keep.tile([P, 2 * U], BF16, name="z23_row")
         z23 = z23_row[:].rearrange("p (b e c) -> p b e c", e=2, c=P)
-        up_b = [ups[t][:].rearrange("p (b c) -> p b c", c=P) for t in (2, 3)]
-        emb_b = [embs[t].rearrange("p (b c) -> p b c", c=P) for t in (2, 3)]
-        nc.gpsimd.tensor_tensor(z23[:, :, 0, :], up_b[0], emb_b[0], ADD)
-        for lo, hi in ((0, 2), (2, 5), (5, 8)):
-            nc.vector.tensor_tensor(z23[:, lo:hi, 1, :], up_b[1][:, lo:hi], emb_b[1][:, lo:hi], ADD)
+        nc.gpsimd.tensor_tensor(z23[:, :, 0, :], up_b[2], emb_b[2], ADD)
+        for lo, hi in ((0, 2), (5, 8), (2, 5)):
+            nc.vector.tensor_tensor(z23[:, lo:hi, 1, :], up_b[3][:, lo:hi], emb_b[3][:, lo:hi], ADD)
         for c, (lo, hi, eng) in enumerate(chunks):
             pair = z23[:, lo:hi].rearrange("p b e c -> p b c e")
             if c < 3:

@@ -20,9 +20,18 @@ RELU = mybir.ActivationFunctionType.Relu
 
 P = 128
 PACK = 4
-LANES = 16
-CHUNKS = 4
-CW = U // CHUNKS
+PER_COLUMN = 16
+QUADRANT = 32
+BANKS = 8
+HALF_S = S // 2
+HALF_V = V // 2
+
+H_PIECES = [(0, 0, P), (1, 0, P), (0, P, S), (1, P, S), (2, 0, S), (3, 0, S)]
+Z_CHUNKS = [(0, 2), (2, 4), (4, 5), (5, 7), (7, 8)]
+SCALAR_CHUNKS = 3
+LAST_ADDS = [(0, 2), (5, 8), (2, 5)]
+Z_ORDER = [0, 1, 3, 4, 2]
+VECTOR_RELUS = 2
 
 
 def tile_picked_devox_relu_p_kernel(
@@ -35,183 +44,179 @@ def tile_picked_devox_relu_p_kernel(
         psum = ctx.enter_context(tc.psum_pool(name="psum", bufs=1))
 
         def load_list(name, src):
-            t = lists.tile([P, S // LANES], U16, name=name)
-            nc.sync.dma_start(t[:], src)
-            return t
+            tile = lists.tile([P, S // PER_COLUMN], U16, name=name)
+            nc.sync.dma_start(tile[:], src)
+            return tile
 
-        def load_scale_rows(queue, plane, src):
-            for q in range(4):
-                queue.dma_start(
-                    plane[32 * q : 32 * q + 4, :].bitcast(I32), src[0, 4 * q : 4 * q + 4, :].bitcast(I32)
+        def entries(list_tile, lo, hi):
+            return list_tile[:, lo // PER_COLUMN : hi // PER_COLUMN]
+
+        def load_scale_rows(plane, src):
+            for q in range(P // QUADRANT):
+                nc.sync.dma_start(
+                    plane[QUADRANT * q : QUADRANT * q + PACK, :].bitcast(I32),
+                    src[0, PACK * q : PACK * (q + 1), :].bitcast(I32),
                 )
 
         xs_all = keep.tile([P, T], U8, name="xs_all", align_bytes=64)
         nc.gpsimd.memset(xs_all[:].bitcast(I32), 0)
-
         w1_rows = w1.rearrange("(p j) c -> p j c", j=PACK)
-        w1_raw = []
-        for a in range(2):
-            raw = keep.tile([P, 2, H], F32, name=f"w1_raw{a}", tag=f"stage{a}")
-            nc.sync.dma_start(raw[:], w1_rows[:, 2 * a : 2 * a + 2, :])
-            w1_raw.append(raw)
-            if a == 0:
-                offs_t = load_list("offs_t", offs)
-                load_scale_rows(nc.sync, xs_all, x_scales)
+        w1_lo = keep.tile([P, 2, H], F32, name="w1_lo")
+        nc.sync.dma_start(w1_lo[:], w1_rows[:, 0:2, :])
+        offs_t = load_list("offs_t", offs)
+        load_scale_rows(xs_all, x_scales)
+        w1_hi = keep.tile([P, 2, H], F32, name="w1_hi", tag="stage1")
+        nc.sync.dma_start(w1_hi[:], w1_rows[:, 2:4, :])
         xw_all = keep.tile([P, T], U32, name="xw_all", tag="stage2")
         nc.sync.dma_start(xw_all[:].bitcast(I32), x_words[0].rearrange("p n t -> p (n t)").bitcast(I32))
         cell_t = load_list("cell_t", cell)
 
-        ups = []
+        windows = []
         for t in range(PACK - 1):
-            up = keep.tile([P, U], F32, name=f"up{t}")
-            nc.vector.memset(up[:], 0.0)
-            ups.append(up)
-        ups.append(ups[0])
+            window = keep.tile([P, U], F32, name=f"window{t}")
+            nc.vector.memset(window[:], 0.0)
+            windows.append(window)
+        windows.append(windows[0])
 
         w1_bf = keep.tile([P, PACK, P, PACK], BF16, name="w1_bf", align_bytes=64)
         dealt = w1_bf[:].rearrange("p t (g e) j -> p g j e t", e=2)
-        w1_src = [raw[:].rearrange("p j (g e t) -> p g j e t", e=2, t=PACK) for raw in w1_raw]
-        nc.scalar.copy(dealt[:, :, 0:2], w1_src[0])
-        xs_g = keep.tile([P, S], U8, name="xs_g", align_bytes=64)
-        nc.vector.tensor_copy(xs_g[:], xs_all[:].indirect(offs_t[:]))
-        nc.vector.tensor_copy(dealt[:, :, 2:4], w1_src[1])
-        w1_q = keep.tile([P, H], U32, name="w1_q", align_bytes=64)
-        w1_s = keep.tile([P, H], U8, name="w1_s", align_bytes=64)
+        nc.scalar.copy(dealt[:, :, 0:2], w1_lo[:].rearrange("p j (g e t) -> p g j e t", e=2, t=PACK))
+        xs_picked = keep.tile([P, S], U8, name="xs_picked", align_bytes=64)
+        nc.vector.tensor_copy(xs_picked[:], xs_all[:].indirect(offs_t[:]))
+        nc.vector.tensor_copy(dealt[:, :, 2:4], w1_hi[:].rearrange("p j (g e t) -> p g j e t", e=2, t=PACK))
+        w1_codes = keep.tile([P, H], U32, name="w1_codes", align_bytes=64)
+        w1_scales = keep.tile([P, H], U8, name="w1_scales", align_bytes=64)
         nc.vector.quantize_mx(
-            out=w1_q[:].bitcast(FP8X4), scales=w1_s[:], in_=w1_bf[:].rearrange("p t m j -> p (t m j)")
+            out=w1_codes[:].bitcast(FP8X4), scales=w1_scales[:], in_=w1_bf[:].rearrange("p t m j -> p (t m j)")
         )
-        xw_g = [keep.tile([P, 256], U32, name=f"xw_g{a}", align_bytes=64) for a in range(2)]
+        xw_picked = [keep.tile([P, HALF_S], U32, name=f"xw_picked{a}", align_bytes=64) for a in range(2)]
         for a in range(2):
-            nc.vector.tensor_copy(xw_g[a][:], xw_all[:].indirect(offs_t[:, a * 16 : (a + 1) * 16]))
+            nc.vector.tensor_copy(xw_picked[a][:], xw_all[:].indirect(entries(offs_t, a * HALF_S, (a + 1) * HALF_S)))
 
         emb_rows = emb.rearrange("(p t) c -> p t c", t=PACK)
         emb01 = keep.tile([P, 2, U], F32, name="emb01", tag="stage1")
         nc.sync.dma_start(emb01[:], emb_rows[:, 0:2, :])
         emb23 = keep.tile([P, 2, U], F32, name="emb23", tag="stage2")
         nc.sync.dma_start(emb23[:], emb_rows[:, 2:4, :])
-        embs = [emb01[:, 0, :], emb01[:, 1, :], emb23[:, 0, :], emb23[:, 1, :]]
         pos_t = [load_list(f"pos{d}_t", src) for d, src in enumerate((pos1, pos2, pos3, pos4))]
-        w2_q = keep.tile([P, 2 * N], U8, name="w2_q", align_bytes=64)
-        nc.sync.dma_start(w2_q[:].bitcast(I32), w2_words[0].bitcast(I32))
-        w2_s = keep.tile([P, N], U8, name="w2_s", align_bytes=64)
-        nc.vector.memset(w2_s[:].bitcast(I32), 0)
-        load_scale_rows(nc.sync, w2_s, w2_scales)
+        w2_codes = keep.tile([P, 2 * N], U8, name="w2_codes", align_bytes=64)
+        nc.sync.dma_start(w2_codes[:].bitcast(I32), w2_words[0].bitcast(I32))
+        w2_plane = keep.tile([P, N], U8, name="w2_plane", align_bytes=64)
+        nc.vector.memset(w2_plane[:].bitcast(I32), 0)
+        load_scale_rows(w2_plane, w2_scales)
 
+        window_b = [window[:].rearrange("p (b c) -> p b c", c=P) for window in windows]
+        emb_b = [pair[:, e, :].rearrange("p (b c) -> p b c", c=P) for pair in (emb01, emb23) for e in range(2)]
         z01_row = keep.tile([P, 2 * U], BF16, name="z01_row")
         z01 = z01_row[:].rearrange("p (b e c) -> p b e c", e=2, c=P)
-        up_b = [up[:].rearrange("p (b c) -> p b c", c=P) for up in ups]
-        emb_b = [e.rearrange("p (b c) -> p b c", c=P) for e in embs]
-        pieces = [(0, 0, 128), (1, 0, 128), (0, 128, 512), (1, 128, 512), (2, 0, 512), (3, 0, 512)]
-        for i, (t, lo, hi) in enumerate(pieces):
-            acc = psum.tile([P, hi - lo], F32, name=f"h_acc{i}", tag=f"bank{i}")
-            for c0, c1 in ((lo, min(hi, 256)), (max(lo, 256), hi)):
-                if c0 >= c1:
-                    continue
+
+        for i, (t, lo, hi) in enumerate(H_PIECES):
+            h_acc = psum.tile([P, hi - lo], F32, name=f"h_acc{i}", tag=f"bank{i}")
+            for a in range(lo // HALF_S, (hi - 1) // HALF_S + 1):
+                c0, c1 = max(lo, a * HALF_S), min(hi, (a + 1) * HALF_S)
                 nc.tensor.matmul_mx(
-                    out=acc[:, c0 - lo : c1 - lo],
-                    lhsT=w1_q[:, t * P : (t + 1) * P].bitcast(FP8X4),
-                    lhsT_scale=w1_s[:, t * P : (t + 1) * P],
-                    rhs=xw_g[c0 // 256][:, c0 % 256 : c0 % 256 + c1 - c0].bitcast(FP8X4),
-                    rhs_scale=xs_g[:, c0:c1],
+                    out=h_acc[:, c0 - lo : c1 - lo],
+                    lhsT=w1_codes[:, t * P : (t + 1) * P].bitcast(FP8X4),
+                    lhsT_scale=w1_scales[:, t * P : (t + 1) * P],
+                    rhs=xw_picked[a][:, c0 - a * HALF_S : c1 - a * HALF_S].bitcast(FP8X4),
+                    rhs_scale=xs_picked[:, c0:c1],
                     start=True,
                     stop=True,
                 )
             h = keep.tile([P, hi - lo], F32, name=f"h{i}")
             if i == 0:
-                nc.vector.tensor_scalar_max(h[:], acc[:], 0.0)
+                nc.vector.tensor_scalar_max(h[:], h_acc[:], 0.0)
             else:
-                nc.scalar.activation(h[:], acc[:], RELU)
-            nc.vector.tensor_copy(ups[t][:].indirect(cell_t[:, lo // LANES : hi // LANES]), h[:])
+                nc.scalar.activation(h[:], h_acc[:], RELU)
+            nc.vector.tensor_copy(windows[t][:].indirect(entries(cell_t, lo, hi)), h[:])
             if hi == S and t == 0:
-                nc.gpsimd.tensor_tensor(z01[:, :, 0, :], up_b[0], emb_b[0], ADD)
+                nc.gpsimd.tensor_tensor(z01[:, :, 0, :], window_b[0], emb_b[0], ADD)
             if hi == S and t == 1:
-                for b0 in (0, 4):
-                    nc.gpsimd.tensor_tensor(z01[:, b0 : b0 + 4, 1, :], up_b[1][:, b0 : b0 + 4], emb_b[1][:, b0 : b0 + 4], ADD)
+                for blocks in (slice(0, U // P // 2), slice(U // P // 2, U // P)):
+                    nc.gpsimd.tensor_tensor(z01[:, blocks, 1, :], window_b[1][:, blocks], emb_b[1][:, blocks], ADD)
 
         gate_t = keep.tile([P, D, V], F32, name="gate_t", tag="stage1")
         nc.sync.dma_start(gate_t[:], gate.rearrange("d p v -> p d v"))
-        gates = [gate_t[:, d, :] for d in range(D)]
 
-        chunks = [(0, 2, nc.scalar), (2, 4, nc.scalar), (4, 5, nc.scalar), (5, 7, nc.vector), (7, 8, nc.vector)]
         z_bf = [
             keep.tile([P, hi - lo, P, 2, 2], BF16, name=f"z_bf{c}", align_bytes=64)
-            for c, (lo, hi, eng) in enumerate(chunks)
+            for c, (lo, hi) in enumerate(Z_CHUNKS)
         ]
-        z01_b = z01.rearrange("p b e c -> p b c e")
-        for c, (lo, hi, eng) in enumerate(chunks):
-            nc.scalar.copy(z_bf[c][:, :, :, 0, :], z01_b[:, lo:hi])
+        for c, (lo, hi) in enumerate(Z_CHUNKS):
+            nc.scalar.copy(z_bf[c][:, :, :, 0, :], z01[:, lo:hi].rearrange("p b e c -> p b c e"))
         z23_row = keep.tile([P, 2 * U], BF16, name="z23_row")
         z23 = z23_row[:].rearrange("p (b e c) -> p b e c", e=2, c=P)
-        nc.gpsimd.tensor_tensor(z23[:, :, 0, :], up_b[2], emb_b[2], ADD)
-        for lo, hi in ((0, 2), (5, 8), (2, 5)):
-            nc.vector.tensor_tensor(z23[:, lo:hi, 1, :], up_b[3][:, lo:hi], emb_b[3][:, lo:hi], ADD)
-        for c, (lo, hi, eng) in enumerate(chunks):
-            pair = z23[:, lo:hi].rearrange("p b e c -> p b c e")
-            if c < 3:
-                nc.scalar.copy(z_bf[c][:, :, :, 1, :], pair)
-            else:
-                nc.vector.tensor_copy(z_bf[c][:, :, :, 1, :], pair)
+        nc.gpsimd.tensor_tensor(z23[:, :, 0, :], window_b[2], emb_b[2], ADD)
+        for lo, hi in LAST_ADDS:
+            nc.vector.tensor_tensor(z23[:, lo:hi, 1, :], window_b[3][:, lo:hi], emb_b[3][:, lo:hi], ADD)
+        for c, (lo, hi) in enumerate(Z_CHUNKS):
+            copy = nc.scalar.copy if c < SCALAR_CHUNKS else nc.vector.tensor_copy
+            copy(z_bf[c][:, :, :, 1, :], z23[:, lo:hi].rearrange("p b e c -> p b c e"))
 
         y = keep.tile([P, U], F32, name="y")
-        late = []
-        for i, c in enumerate((0, 1, 3, 4, 2)):
-            lo, hi, eng = chunks[c]
-            w = (hi - lo) * P
-            z_q = keep.tile([P, w], U32, name=f"z_q{c}", align_bytes=64)
-            z_s = keep.tile([P, w], U8, name=f"z_s{c}", align_bytes=64)
+        y_accs = []
+        for i, c in enumerate(Z_ORDER):
+            lo, hi = Z_CHUNKS[c]
+            width = (hi - lo) * P
+            z_codes = keep.tile([P, width], U32, name=f"z_codes{c}", align_bytes=64)
+            z_scales = keep.tile([P, width], U8, name=f"z_scales{c}", align_bytes=64)
             nc.vector.quantize_mx(
-                out=z_q[:].bitcast(FP8X4), scales=z_s[:], in_=z_bf[c][:].rearrange("p b c a e -> p (b c a e)")
+                out=z_codes[:].bitcast(FP8X4),
+                scales=z_scales[:],
+                in_=z_bf[c][:].rearrange("p b c a e -> p (b c a e)"),
             )
-            acc = psum.tile([P, w], F32, name=f"y_acc{c}", tag=f"bank{(6 + i) % 8}")
+            y_acc = psum.tile([P, width], F32, name=f"y_acc{c}", tag=f"bank{(len(H_PIECES) + i) % BANKS}")
             nc.tensor.matmul_mx(
-                out=acc[:],
-                lhsT=w2_q[:].bitcast(FP4X4),
-                lhsT_scale=w2_s[:],
-                rhs=z_q[:].bitcast(FP8X4),
-                rhs_scale=z_s[:],
+                out=y_acc[:],
+                lhsT=w2_codes[:].bitcast(FP4X4),
+                lhsT_scale=w2_plane[:],
+                rhs=z_codes[:].bitcast(FP8X4),
+                rhs_scale=z_scales[:],
                 start=True,
                 stop=True,
             )
-            if i < 3:
-                nc.scalar.activation(y[:, lo * P : hi * P], acc[:], RELU)
-            else:
-                late.append((y[:, lo * P : hi * P], acc))
-        for dst, acc in late:
-            nc.vector.tensor_scalar_max(dst, acc[:], 0.0)
+            y_accs.append((y[:, lo * P : hi * P], y_acc))
+            if i < len(Z_ORDER) - VECTOR_RELUS:
+                nc.scalar.activation(y[:, lo * P : hi * P], y_acc[:], RELU)
+        for y_cols, y_acc in y_accs[-VECTOR_RELUS:]:
+            nc.vector.tensor_scalar_max(y_cols, y_acc[:], 0.0)
 
         ident = keep.tile([P, P], F32, name="ident")
         make_identity(nc, ident[:])
-        nb = 2
-        wa = nb * P
-        turned = [psum.tile([P, P], F32, name=f"turned{b}", tag=f"bank{3 + b}") for b in range(nb)]
+
+        def gather_term(d, lo, hi):
+            term = keep.tile([P, hi - lo], F32, name=f"term{d}_{lo}")
+            nc.vector.tensor_tensor(term[:], y[:].indirect(entries(pos_t[d], lo, hi)), gate_t[:, d, lo:hi], MULT)
+            return term
+
+        blocks_lo = HALF_V // P
+        turned = [psum.tile([P, P], F32, name=f"turned{b}", tag=f"bank{3 + b}") for b in range(blocks_lo)]
         for d in range(D):
-            term = keep.tile([P, wa], F32, name=f"term_a{d}")
-            nc.vector.tensor_tensor(term[:], y[:].indirect(pos_t[d][:, 0 : wa // LANES]), gates[d][:, 0:wa], MULT)
-            for b in range(nb):
+            term = gather_term(d, 0, HALF_V)
+            for b in range(blocks_lo):
                 nc.tensor.matmul(
-                    turned[b][:], term[:, b * P : (b + 1) * P], ident[:], start=(d == 0), stop=(d == D - 1), is_transpose=True
+                    turned[b][:],
+                    term[:, b * P : (b + 1) * P],
+                    ident[:],
+                    start=(d == 0),
+                    stop=(d == D - 1),
+                    is_transpose=True,
                 )
-        back = psum.tile([P, wa], F32, name="back", tag="bank5")
-        for b in range(nb):
-            sum_t = keep.tile([P, P], F32, name=f"sum_t{b}")
-            nc.scalar.copy(sum_t[:], turned[b][:])
-            nc.tensor.transpose(back[:, b * P : (b + 1) * P], sum_t[:], ident[:])
-        res_a = keep.tile([P, wa], F32, name="res_a")
-        nc.scalar.copy(res_a[:], back[:])
-        nc.scalar.dma_start(out[:, 0:wa], res_a[:])
+        sum_lo = psum.tile([P, HALF_V], F32, name="sum_lo", tag="bank5")
+        for b in range(blocks_lo):
+            turned_sb = keep.tile([P, P], F32, name=f"turned_sb{b}")
+            nc.scalar.copy(turned_sb[:], turned[b][:])
+            nc.tensor.transpose(sum_lo[:, b * P : (b + 1) * P], turned_sb[:], ident[:])
+        res_lo = keep.tile([P, HALF_V], F32, name="res_lo")
+        nc.scalar.copy(res_lo[:], sum_lo[:])
+        nc.scalar.dma_start(out[:, 0:HALF_V], res_lo[:])
 
-        wb = V - wa
-        terms = [keep.tile([P, wb], F32, name=f"term_b{d}") for d in range(D)]
-        sums = [keep.tile([P, wb], F32, name=f"sum_b{d}") for d in range(D - 1)]
-
-        def gather_b(d):
-            nc.vector.tensor_tensor(terms[d][:], y[:].indirect(pos_t[d][:, wa // LANES :]), gates[d][:, wa:], MULT)
-
-        gather_b(0)
-        gather_b(1)
-        gather_b(2)
-        nc.vector.tensor_tensor(sums[0][:], terms[0][:], terms[1][:], ADD)
-        gather_b(3)
-        nc.vector.tensor_tensor(sums[1][:], sums[0][:], terms[2][:], ADD)
-        nc.vector.tensor_tensor(sums[2][:], sums[1][:], terms[3][:], ADD)
-        nc.sync.dma_start(out[:, wa:], sums[2][:])
+        terms_hi = [gather_term(d, HALF_V, V) for d in range(D - 1)]
+        sum01 = keep.tile([P, HALF_V], F32, name="sum01")
+        nc.vector.tensor_tensor(sum01[:], terms_hi[0][:], terms_hi[1][:], ADD)
+        term3_hi = gather_term(D - 1, HALF_V, V)
+        sum012 = keep.tile([P, HALF_V], F32, name="sum012")
+        nc.vector.tensor_tensor(sum012[:], sum01[:], terms_hi[2][:], ADD)
+        res_hi = keep.tile([P, HALF_V], F32, name="res_hi")
+        nc.vector.tensor_tensor(res_hi[:], sum012[:], term3_hi[:], ADD)
+        nc.sync.dma_start(out[:, HALF_V:], res_hi[:])

@@ -189,34 +189,30 @@ def tile_picked_devox_relu_p_kernel(
             nc.vector.tensor_tensor(term[:], y[:].indirect(entries(pos_t[d], lo, hi)), gate_t[:, d, lo:hi], MULT)
             return term
 
-        blocks_lo = HALF_V // P
-        turned = [psum.tile([P, P], F32, name=f"turned{b}", tag=f"bank{3 + b}") for b in range(blocks_lo)]
-        for d in range(D):
-            term = gather_term(d, 0, HALF_V)
-            for b in range(blocks_lo):
-                nc.tensor.matmul(
-                    turned[b][:],
-                    term[:, b * P : (b + 1) * P],
-                    ident[:],
-                    start=(d == 0),
-                    stop=(d == D - 1),
-                    is_transpose=True,
-                )
-        sum_lo = psum.tile([P, HALF_V], F32, name="sum_lo", tag="bank5")
-        for b in range(blocks_lo):
-            turned_sb = keep.tile([P, P], F32, name=f"turned_sb{b}")
-            nc.scalar.copy(turned_sb[:], turned[b][:])
-            nc.tensor.transpose(sum_lo[:, b * P : (b + 1) * P], turned_sb[:], ident[:])
-        res_lo = keep.tile([P, HALF_V], F32, name="res_lo")
-        nc.scalar.copy(res_lo[:], sum_lo[:])
-        nc.scalar.dma_start(out[:, 0:HALF_V], res_lo[:])
-
-        terms_hi = [gather_term(d, HALF_V, V) for d in range(D - 1)]
-        sum01 = keep.tile([P, HALF_V], F32, name="sum01")
-        nc.vector.tensor_tensor(sum01[:], terms_hi[0][:], terms_hi[1][:], ADD)
-        term3_hi = gather_term(D - 1, HALF_V, V)
-        sum012 = keep.tile([P, HALF_V], F32, name="sum012")
-        nc.vector.tensor_tensor(sum012[:], sum01[:], terms_hi[2][:], ADD)
-        res_hi = keep.tile([P, HALF_V], F32, name="res_hi")
-        nc.vector.tensor_tensor(res_hi[:], sum012[:], term3_hi[:], ADD)
-        nc.sync.dma_start(out[:, HALF_V:], res_hi[:])
+        groups = [(0, V - P), (V - P, V)]
+        turned = [psum.tile([P, P], F32, name=f"turned{b}", tag=f"bank{3 + b}") for b in range(V // P)]
+        for lo, hi in groups:
+            for d in range(D - 1):
+                term = gather_term(d, lo, hi)
+                for b in range(lo // P, hi // P):
+                    nc.tensor.matmul(
+                        turned[b][:],
+                        term[:, b * P - lo : (b + 1) * P - lo],
+                        ident[:],
+                        start=(d == 0),
+                        stop=(d == D - 2),
+                        is_transpose=True,
+                    )
+        partial = []
+        for a, (lo, hi) in enumerate(groups):
+            back = psum.tile([P, hi - lo], F32, name=f"back{a}", tag=f"bank{1 + a}")
+            for b in range(lo // P, hi // P):
+                turned_sb = keep.tile([P, P], F32, name=f"turned_sb{b}")
+                nc.scalar.copy(turned_sb[:], turned[b][:])
+                nc.tensor.transpose(back[:, b * P - lo : (b + 1) * P - lo], turned_sb[:], ident[:])
+            partial.append(back)
+        last_terms = [gather_term(D - 1, lo, hi) for lo, hi in groups]
+        for a, (lo, hi) in enumerate(groups):
+            res = keep.tile([P, hi - lo], F32, name=f"res{a}")
+            nc.vector.tensor_tensor(res[:], partial[a][:], last_terms[a][:], ADD)
+            nc.sync.dma_start(out[:, lo:hi], res[:])

@@ -27,11 +27,11 @@ HALF_S = S // 2
 HALF_V = V // 2
 
 H_PIECES = [(0, 0, P), (1, 0, P), (0, P, S), (1, P, S), (2, 0, S), (3, 0, S)]
-Z_CHUNKS = [(0, 2), (2, 4), (4, 5), (5, 7), (7, 8)]
-SCALAR_CHUNKS = 3
-LAST_ADDS = [(0, 2), (5, 8), (2, 5)]
-Z_ORDER = [0, 1, 3, 4, 2]
-VECTOR_RELUS = 2
+Z_CHUNKS = [(0, 1), (1, 3), (3, 5), (5, 6), (6, 8)]
+SCALAR_CHUNKS = 4
+LAST_ADDS = [(0, 1), (1, 3), (6, 8), (3, 6)]
+Z_ORDER = [0, 4, 1, 2, 3]
+VECTOR_RELUS = (0, 4, 1, 3)
 
 
 def tile_picked_devox_relu_p_kernel(
@@ -176,9 +176,10 @@ def tile_picked_devox_relu_p_kernel(
                 stop=True,
             )
             y_accs.append((y[:, lo * P : hi * P], y_acc))
-            if i < len(Z_ORDER) - VECTOR_RELUS:
+            if c not in VECTOR_RELUS:
                 nc.scalar.activation(y[:, lo * P : hi * P], y_acc[:], RELU)
-        for y_cols, y_acc in y_accs[-VECTOR_RELUS:]:
+        for c in VECTOR_RELUS:
+            y_cols, y_acc = y_accs[Z_ORDER.index(c)]
             nc.vector.tensor_scalar_max(y_cols, y_acc[:], 0.0)
 
         ident = keep.tile([P, P], F32, name="ident")
@@ -191,8 +192,8 @@ def tile_picked_devox_relu_p_kernel(
 
         groups = [(0, V - P), (V - P, V)]
         turned = [psum.tile([P, P], F32, name=f"turned{b}", tag=f"bank{3 + b}") for b in range(V // P)]
-        for lo, hi in groups:
-            for d in range(D - 1):
+        for d, lo, hi in [(0, 0, V)] + [(d, lo, hi) for lo, hi in groups for d in range(1, D - 1)]:
+            if True:
                 term = gather_term(d, lo, hi)
                 for b in range(lo // P, hi // P):
                     nc.tensor.matmul(
@@ -211,8 +212,9 @@ def tile_picked_devox_relu_p_kernel(
                 nc.scalar.copy(turned_sb[:], turned[b][:])
                 nc.tensor.transpose(back[:, b * P - lo : (b + 1) * P - lo], turned_sb[:], ident[:])
             partial.append(back)
-        last_terms = [gather_term(D - 1, lo, hi) for lo, hi in groups]
-        for a, (lo, hi) in enumerate(groups):
-            res = keep.tile([P, hi - lo], F32, name=f"res{a}")
-            nc.vector.tensor_tensor(res[:], partial[a][:], last_terms[a][:], ADD)
-            nc.sync.dma_start(out[:, lo:hi], res[:])
+        last_terms = [gather_term(D - 1, lo, hi) for lo, hi in ((0, 2 * P), (2 * P, V))]
+        for a, lo, hi, queue in ((0, 0, 2 * P, nc.sync), (0, 2 * P, 3 * P, nc.scalar), (1, 3 * P, V, nc.sync)):
+            res = keep.tile([P, hi - lo], F32, name=f"res{lo}")
+            cols = slice(lo - groups[a][0], hi - groups[a][0])
+            nc.vector.tensor_tensor(res[:], partial[a][:, cols], last_terms[lo // HALF_V][:, lo % HALF_V : lo % HALF_V + hi - lo], ADD)
+            queue.dma_start(out[:, lo:hi], res[:])

@@ -24,7 +24,7 @@ PER_COLUMN = 16
 QUADRANT = 32
 BANKS = 8
 HALF_S = S // 2
-HALF_V = V // 2
+WIDE = V - P
 
 H_PIECES = [(0, 0, P), (1, 0, P), (0, P, S), (1, P, S), (2, 0, S), (3, 0, S)]
 Z_CHUNKS = [(0, 1), (1, 3), (3, 5), (5, 6), (6, 8)]
@@ -190,20 +190,19 @@ def tile_picked_devox_relu_p_kernel(
             nc.vector.tensor_tensor(term[:], y[:].indirect(entries(pos_t[d], lo, hi)), gate_t[:, d, lo:hi], MULT)
             return term
 
-        groups = [(0, V - P), (V - P, V)]
+        groups = [(0, WIDE), (WIDE, V)]
         turned = [psum.tile([P, P], F32, name=f"turned{b}", tag=f"bank{3 + b}") for b in range(V // P)]
         for d, lo, hi in [(0, 0, V)] + [(d, lo, hi) for lo, hi in groups for d in range(1, D - 1)]:
-            if True:
-                term = gather_term(d, lo, hi)
-                for b in range(lo // P, hi // P):
-                    nc.tensor.matmul(
-                        turned[b][:],
-                        term[:, b * P - lo : (b + 1) * P - lo],
-                        ident[:],
-                        start=(d == 0),
-                        stop=(d == D - 2),
-                        is_transpose=True,
-                    )
+            term = gather_term(d, lo, hi)
+            for b in range(lo // P, hi // P):
+                nc.tensor.matmul(
+                    turned[b][:],
+                    term[:, b * P - lo : (b + 1) * P - lo],
+                    ident[:],
+                    start=(d == 0),
+                    stop=(d == D - 2),
+                    is_transpose=True,
+                )
         partial = []
         for a, (lo, hi) in enumerate(groups):
             back = psum.tile([P, hi - lo], F32, name=f"back{a}", tag=f"bank{1 + a}")
@@ -212,9 +211,9 @@ def tile_picked_devox_relu_p_kernel(
                 nc.scalar.copy(turned_sb[:], turned[b][:])
                 nc.tensor.transpose(back[:, b * P - lo : (b + 1) * P - lo], turned_sb[:], ident[:])
             partial.append(back)
-        last_terms = [gather_term(D - 1, lo, hi) for lo, hi in ((0, 2 * P), (2 * P, V))]
-        for a, lo, hi, queue in ((0, 0, 2 * P, nc.sync), (0, 2 * P, 3 * P, nc.scalar), (1, 3 * P, V, nc.sync)):
-            res = keep.tile([P, hi - lo], F32, name=f"res{lo}")
-            cols = slice(lo - groups[a][0], hi - groups[a][0])
-            nc.vector.tensor_tensor(res[:], partial[a][:, cols], last_terms[lo // HALF_V][:, lo % HALF_V : lo % HALF_V + hi - lo], ADD)
-            queue.dma_start(out[:, lo:hi], res[:])
+
+        last_terms = [gather_term(D - 1, lo, hi) for lo, hi in groups]
+        for a, (lo, hi) in enumerate(groups):
+            res = keep.tile([P, hi - lo], F32, name=f"res{a}")
+            nc.vector.tensor_tensor(res[:], partial[a][:], last_terms[a][:], ADD)
+            nc.sync.dma_start(out[:, lo:hi], res[:])

@@ -213,7 +213,7 @@ def tile_picked_devox_relu_p_kernel(
             partial.append(back)
 
         last_terms = [gather_term(D - 1, lo, hi) for lo, hi in groups]
+        res = keep.tile([P, V], F32, name="res")
         for a, (lo, hi) in enumerate(groups):
-            res = keep.tile([P, hi - lo], F32, name=f"res{a}")
-            nc.vector.tensor_tensor(res[:], partial[a][:], last_terms[a][:], ADD)
-            nc.sync.dma_start(out[:, lo:hi], res[:])
+            nc.vector.tensor_tensor(res[:, lo:hi], partial[a][:], last_terms[a][:], ADD)
+        nc.sync.dma_start(out, res[:])

@@ -24,9 +24,9 @@ PER_COLUMN = 16
 QUADRANT = 32
 BANKS = 8
 HALF_S = S // 2
+HALF_P = P // 2
 WIDE = V - P
 
-H_PIECES = [(0, 0, P), (1, 0, P), (0, P, S), (1, P, S), (2, 0, S), (3, 0, S)]
 Z_CHUNKS = [(0, 1), (1, 3), (3, 5), (5, 6), (6, 8)]
 SCALAR_CHUNKS = 4
 LAST_ADDS = [(0, 1), (1, 3), (6, 8), (3, 6)]
@@ -61,43 +61,53 @@ def tile_picked_devox_relu_p_kernel(
         xs_all = keep.tile([P, T], U8, name="xs_all", align_bytes=64)
         nc.gpsimd.memset(xs_all[:].bitcast(I32), 0)
         w1_rows = w1.rearrange("(p j) c -> p j c", j=PACK)
-        w1_lo = keep.tile([P, 2, H], F32, name="w1_lo")
-        nc.sync.dma_start(w1_lo[:], w1_rows[:, 0:2, :])
+        w1_left = keep.tile([P, PACK, H // 2], F32, name="w1_left")
+        nc.sync.dma_start(w1_left[:], w1_rows[:, :, 0 : H // 2])
         offs_t = load_list("offs_t", offs)
         load_scale_rows(xs_all, x_scales)
-        w1_hi = keep.tile([P, 2, H], F32, name="w1_hi", tag="stage1")
-        nc.sync.dma_start(w1_hi[:], w1_rows[:, 2:4, :])
         xw_all = keep.tile([P, T], U32, name="xw_all", tag="stage2")
         nc.sync.dma_start(xw_all[:].bitcast(I32), x_words[0].rearrange("p n t -> p (n t)").bitcast(I32))
         cell_t = load_list("cell_t", cell)
+        w1_right = keep.tile([P, PACK, H // 2], F32, name="w1_right", tag="right")
+        nc.sync.dma_start(w1_right[:], w1_rows[:, :, H // 2 : H])
+        emb_rows = emb.rearrange("(p t) c -> p t c", t=PACK)
+        emb01 = keep.tile([P, 2, U], F32, name="emb01", tag="stage1")
+        nc.sync.dma_start(emb01[:], emb_rows[:, 0:2, :])
 
         windows = []
-        for t in range(PACK - 1):
+        for t in range(4):
             window = keep.tile([P, U], F32, name=f"window{t}")
-            nc.vector.memset(window[:], 0.0)
+            (nc.vector if t < 2 else nc.gpsimd).memset(window[:], 0.0)
             windows.append(window)
-        windows.append(windows[0])
+        ident = keep.tile([P, P], F32, name="ident")
+        make_identity(nc, ident[:])
 
-        w1_bf = keep.tile([P, PACK, P, PACK], BF16, name="w1_bf", align_bytes=64)
-        dealt = w1_bf[:].rearrange("p t (g e) j -> p g j e t", e=2)
-        nc.scalar.copy(dealt[:, :, 0:2], w1_lo[:].rearrange("p j (g e t) -> p g j e t", e=2, t=PACK))
+        def deal(copy, dst, src, t0, t1):
+            copy(
+                dst.rearrange("p t (g e) j -> p g j e t", e=2),
+                src.rearrange("p j (g e t) -> p g j e t", e=2, t=PACK)[:, :, :, :, t0:t1],
+            )
+
+        def quantize(codes, scales, src):
+            nc.vector.quantize_mx(out=codes.bitcast(FP8X4), scales=scales, in_=src.rearrange("p t m j -> p (t m j)"))
+
+        w1_codes = [keep.tile([P, P], U32, name=f"w1_codes{i}", align_bytes=64) for i in range(PACK)]
+        w1_scales = [keep.tile([P, P], U8, name=f"w1_scales{i}", align_bytes=64) for i in range(PACK)]
+        lower_bf = keep.tile([P, 2, HALF_P, PACK], BF16, name="lower_bf", align_bytes=64)
+        deal(nc.scalar.copy, lower_bf[:], w1_left[:], 0, 2)
+        left_bf = keep.tile([P, 2, HALF_P, PACK], BF16, name="left_bf", align_bytes=64)
+        deal(nc.vector.tensor_copy, left_bf[:], w1_left[:], 2, PACK)
         xs_picked = keep.tile([P, S], U8, name="xs_picked", align_bytes=64)
         nc.vector.tensor_copy(xs_picked[:], xs_all[:].indirect(offs_t[:]))
-        nc.vector.tensor_copy(dealt[:, :, 2:4], w1_hi[:].rearrange("p j (g e t) -> p g j e t", e=2, t=PACK))
-        w1_codes = keep.tile([P, H], U32, name="w1_codes", align_bytes=64)
-        w1_scales = keep.tile([P, H], U8, name="w1_scales", align_bytes=64)
-        nc.vector.quantize_mx(
-            out=w1_codes[:].bitcast(FP8X4), scales=w1_scales[:], in_=w1_bf[:].rearrange("p t m j -> p (t m j)")
-        )
+        quantize(w1_codes[0][:], w1_scales[0][:], lower_bf[:])
+        for t in (2, 3):
+            quantize(w1_codes[t][:, 0:HALF_P], w1_scales[t][:, 0:HALF_P], left_bf[:, t - 2 : t - 1])
         xw_picked = [keep.tile([P, HALF_S], U32, name=f"xw_picked{a}", align_bytes=64) for a in range(2)]
         for a in range(2):
             nc.vector.tensor_copy(xw_picked[a][:], xw_all[:].indirect(entries(offs_t, a * HALF_S, (a + 1) * HALF_S)))
 
-        emb_rows = emb.rearrange("(p t) c -> p t c", t=PACK)
-        emb01 = keep.tile([P, 2, U], F32, name="emb01", tag="stage1")
-        nc.sync.dma_start(emb01[:], emb_rows[:, 0:2, :])
-        emb23 = keep.tile([P, 2, U], F32, name="emb23", tag="stage2")
-        nc.sync.dma_start(emb23[:], emb_rows[:, 2:4, :])
+        emb2 = keep.tile([P, U], F32, name="emb2", tag="stage2")
+        nc.sync.dma_start(emb2[:], emb_rows[:, 2, :])
         pos_t = [load_list(f"pos{d}_t", src) for d, src in enumerate((pos1, pos2, pos3, pos4))]
         w2_codes = keep.tile([P, 2 * N], U8, name="w2_codes", align_bytes=64)
         nc.sync.dma_start(w2_codes[:].bitcast(I32), w2_words[0].bitcast(I32))
@@ -105,45 +115,96 @@ def tile_picked_devox_relu_p_kernel(
         nc.vector.memset(w2_plane[:].bitcast(I32), 0)
         load_scale_rows(w2_plane, w2_scales)
 
-        window_b = [window[:].rearrange("p (b c) -> p b c", c=P) for window in windows]
-        emb_b = [pair[:, e, :].rearrange("p (b c) -> p b c", c=P) for pair in (emb01, emb23) for e in range(2)]
-        z01_row = keep.tile([P, 2 * U], BF16, name="z01_row")
-        z01 = z01_row[:].rearrange("p (b e c) -> p b e c", e=2, c=P)
-
-        for i, (t, lo, hi) in enumerate(H_PIECES):
-            h_acc = psum.tile([P, hi - lo], F32, name=f"h_acc{i}", tag=f"bank{i}")
+        def product(i, tile_no, lo, hi, bank):
+            h_acc = psum.tile([P, hi - lo], F32, name=f"h_acc{i}", tag=f"bank{bank}")
             for a in range(lo // HALF_S, (hi - 1) // HALF_S + 1):
                 c0, c1 = max(lo, a * HALF_S), min(hi, (a + 1) * HALF_S)
                 nc.tensor.matmul_mx(
                     out=h_acc[:, c0 - lo : c1 - lo],
-                    lhsT=w1_codes[:, t * P : (t + 1) * P].bitcast(FP8X4),
-                    lhsT_scale=w1_scales[:, t * P : (t + 1) * P],
+                    lhsT=w1_codes[tile_no][:].bitcast(FP8X4),
+                    lhsT_scale=w1_scales[tile_no][:],
                     rhs=xw_picked[a][:, c0 - a * HALF_S : c1 - a * HALF_S].bitcast(FP8X4),
                     rhs_scale=xs_picked[:, c0:c1],
                     start=True,
                     stop=True,
                 )
-            h = keep.tile([P, hi - lo], F32, name=f"h{i}")
-            if i == 0:
-                nc.vector.tensor_scalar_max(h[:], h_acc[:], 0.0)
-            else:
-                nc.scalar.activation(h[:], h_acc[:], RELU)
-            nc.vector.tensor_copy(windows[t][:].indirect(entries(cell_t, lo, hi)), h[:])
-            if hi == S and t == 0:
-                nc.gpsimd.tensor_tensor(z01[:, :, 0, :], window_b[0], emb_b[0], ADD)
-            if hi == S and t == 1:
-                for blocks in (slice(0, U // P // 2), slice(U // P // 2, U // P)):
-                    nc.gpsimd.tensor_tensor(z01[:, blocks, 1, :], window_b[1][:, blocks], emb_b[1][:, blocks], ADD)
+            return h_acc
+
+        def scatter(window, lo, hi, h):
+            nc.vector.tensor_copy(window[:].indirect(entries(cell_t, lo, hi)), h)
+
+        acc0 = product(0, 0, 0, P, 4)
+        h0 = keep.tile([P, P], F32, name="h0")
+        nc.vector.tensor_scalar_max(h0[:], acc0[:], 0.0)
+        scatter(windows[0], 0, P, h0[:])
+        acc1 = product(1, 0, P, HALF_S, 5)
+        h1 = keep.tile([P, P], F32, name="h1")
+        nc.scalar.activation(h1[:], acc1[:], RELU)
+        scatter(windows[1], P, HALF_S, h1[:])
+        acc2 = product(2, 0, HALF_S, S, 6)
+        upper_bf = keep.tile([P, 2, HALF_P, PACK], BF16, name="upper_bf", align_bytes=64)
+        deal(nc.scalar.copy, upper_bf[:], w1_right[:], 0, 2)
+        right_bf = keep.tile([P, 2, HALF_P, PACK], BF16, name="right_bf", align_bytes=64)
+        deal(nc.scalar.copy, right_bf[:], w1_right[:], 2, PACK)
+        quantize(w1_codes[1][:], w1_scales[1][:], upper_bf[:])
+        h2 = keep.tile([P, HALF_S], F32, name="h2", tag="right")
+        nc.scalar.activation(h2[:], acc2[:], RELU)
+        for t in (2, 3):
+            quantize(w1_codes[t][:, HALF_P:P], w1_scales[t][:, HALF_P:P], right_bf[:, t - 2 : t - 1])
+        scatter(windows[0], HALF_S, S, h2[:])
+        whole = []
+        for i, bank in ((1, 7), (2, 4), (3, 5)):
+            acc = product(2 + i, i, 0, S, bank)
+            h = keep.tile([P, S], F32, name=f"h{2 + i}")
+            nc.scalar.activation(h[:], acc[:], RELU)
+            whole.append(h)
+        scatter(windows[2], 0, S, whole[0][:])
+
+        sums = [psum.tile([P, 2, 2, P], F32, name=f"sums{k}", tag=f"bank{k}") for k in range(4)]
+
+        def turn_into(dst, src, start, stop):
+            nc.tensor.matmul(dst, src, ident[:], start=start, stop=stop, is_transpose=True)
+
+        for b in range(U // P):
+            for e in range(2):
+                turn_into(sums[b // 2][:, b % 2, e, :], emb01[:, e, b * P : (b + 1) * P], b % 2 == 0 and e == 0, False)
+        for w, half in ((1, 0), (0, 0), (2, 1)):
+            for b in range(U // P):
+                turn_into(
+                    sums[b // 2][:, b % 2, :, half * HALF_P : (half + 1) * HALF_P],
+                    windows[w][:, b * P : (b + 1) * P],
+                    False,
+                    w == 2 and b % 2 == 1,
+                )
+        z_row = keep.tile([P, PACK * U], BF16, name="z_row", align_bytes=64)
+        z_bf = z_row[:].rearrange("p (b c a e) -> p b c a e", c=P, a=2, e=2)
+        z_words = z_row[:].bitcast(F32).rearrange("p (c a) -> p c a", a=2)
+        backs = [psum.tile([P, U // 2], F32, name=f"pairs{k}", tag=f"bank{6 + k}") for k in range(2)]
+        for k in range(4):
+            turned_z = keep.tile([P, 2 * 2 * P], BF16, name=f"turned_z{k}", tag=f"turned_z{k}")
+            nc.scalar.copy(
+                turned_z[:].rearrange("c (b p e) -> c b p e", b=2, e=2), sums[k][:].rearrange("c b e p -> c b p e")
+            )
+            for b2 in range(2):
+                b = 2 * k + b2
+                nc.tensor.transpose(
+                    backs[b // 4][:, (b % 4) * P : (b % 4 + 1) * P],
+                    turned_z[:].bitcast(F32)[:, b2 * P : (b2 + 1) * P],
+                    ident[:],
+                )
+        for k in range(2):
+            nc.scalar.copy(z_words[:, k * U // 2 : (k + 1) * U // 2, 0], backs[k][:])
+
+        scatter(windows[3], 0, S, whole[1][:])
+        scatter(windows[2], 0, S, whole[2][:])
+        window_b = {t: windows[{2: 3, 3: 2}[t]][:].rearrange("p (b c) -> p b c", c=P) for t in (2, 3)}
+        emb3 = keep.tile([P, U], F32, name="emb3", tag="turned_z1")
+        nc.sync.dma_start(emb3[:], emb_rows[:, 3, :])
+        emb_b = {t: e[:].rearrange("p (b c) -> p b c", c=P) for t, e in ((2, emb2), (3, emb3))}
 
         gate_t = keep.tile([P, D, V], F32, name="gate_t", tag="stage1")
         nc.sync.dma_start(gate_t[:], gate.rearrange("d p v -> p d v"))
 
-        z_bf = [
-            keep.tile([P, hi - lo, P, 2, 2], BF16, name=f"z_bf{c}", align_bytes=64)
-            for c, (lo, hi) in enumerate(Z_CHUNKS)
-        ]
-        for c, (lo, hi) in enumerate(Z_CHUNKS):
-            nc.scalar.copy(z_bf[c][:, :, :, 0, :], z01[:, lo:hi].rearrange("p b e c -> p b c e"))
         z23_row = keep.tile([P, 2 * U], BF16, name="z23_row")
         z23 = z23_row[:].rearrange("p (b e c) -> p b e c", e=2, c=P)
         nc.gpsimd.tensor_tensor(z23[:, :, 0, :], window_b[2], emb_b[2], ADD)
@@ -151,7 +212,7 @@ def tile_picked_devox_relu_p_kernel(
             nc.vector.tensor_tensor(z23[:, lo:hi, 1, :], window_b[3][:, lo:hi], emb_b[3][:, lo:hi], ADD)
         for c, (lo, hi) in enumerate(Z_CHUNKS):
             copy = nc.scalar.copy if c < SCALAR_CHUNKS else nc.vector.tensor_copy
-            copy(z_bf[c][:, :, :, 1, :], z23[:, lo:hi].rearrange("p b e c -> p b c e"))
+            copy(z_bf[:, lo:hi, :, 1, :], z23[:, lo:hi].rearrange("p b e c -> p b c e"))
 
         y = keep.tile([P, U], F32, name="y")
         y_accs = []
@@ -163,9 +224,9 @@ def tile_picked_devox_relu_p_kernel(
             nc.vector.quantize_mx(
                 out=z_codes[:].bitcast(FP8X4),
                 scales=z_scales[:],
-                in_=z_bf[c][:].rearrange("p b c a e -> p (b c a e)"),
+                in_=z_row[:, lo * P * PACK : hi * P * PACK],
             )
-            y_acc = psum.tile([P, width], F32, name=f"y_acc{c}", tag=f"bank{(len(H_PIECES) + i) % BANKS}")
+            y_acc = psum.tile([P, width], F32, name=f"y_acc{c}", tag=f"bank{i}")
             nc.tensor.matmul_mx(
                 out=y_acc[:],
                 lhsT=w2_codes[:].bitcast(FP4X4),
@@ -182,8 +243,6 @@ def tile_picked_devox_relu_p_kernel(
             y_cols, y_acc = y_accs[Z_ORDER.index(c)]
             nc.vector.tensor_scalar_max(y_cols, y_acc[:], 0.0)
 
-        ident = keep.tile([P, P], F32, name="ident")
-        make_identity(nc, ident[:])
 
         def gather_term(d, lo, hi):
             term = keep.tile([P, hi - lo], F32, name=f"term{d}_{lo}")
@@ -191,7 +250,7 @@ def tile_picked_devox_relu_p_kernel(
             return term
 
         groups = [(0, WIDE), (WIDE, V)]
-        turned = [psum.tile([P, P], F32, name=f"turned{b}", tag=f"bank{3 + b}") for b in range(V // P)]
+        turned = [psum.tile([P, P], F32, name=f"turned{b}", tag=f"bank{4 + b}") for b in range(V // P)]
         for d, lo, hi in [(0, 0, V)] + [(d, lo, hi) for lo, hi in groups for d in range(1, D - 1)]:
             term = gather_term(d, lo, hi)
             for b in range(lo // P, hi // P):
@@ -205,7 +264,7 @@ def tile_picked_devox_relu_p_kernel(
                 )
         partial = []
         for a, (lo, hi) in enumerate(groups):
-            back = psum.tile([P, hi - lo], F32, name=f"back{a}", tag=f"bank{1 + a}")
+            back = psum.tile([P, hi - lo], F32, name=f"back{a}", tag=f"bank{a}")
             for b in range(lo // P, hi // P):
                 turned_sb = keep.tile([P, P], F32, name=f"turned_sb{b}")
                 nc.scalar.copy(turned_sb[:], turned[b][:])

@@ -75,9 +75,9 @@ def tile_picked_devox_relu_p_kernel(
         nc.sync.dma_start(emb01[:], emb_rows[:, 0:2, :])
 
         windows = []
-        for t in range(4):
+        for t in range(3):
             window = keep.tile([P, U], F32, name=f"window{t}")
-            (nc.vector if t < 2 else nc.gpsimd).memset(window[:], 0.0)
+            nc.vector.memset(window[:], 0.0)
             windows.append(window)
         ident = keep.tile([P, P], F32, name="ident")
         make_identity(nc, ident[:])
@@ -93,15 +93,15 @@ def tile_picked_devox_relu_p_kernel(
 
         w1_codes = [keep.tile([P, P], U32, name=f"w1_codes{i}", align_bytes=64) for i in range(PACK)]
         w1_scales = [keep.tile([P, P], U8, name=f"w1_scales{i}", align_bytes=64) for i in range(PACK)]
-        lower_bf = keep.tile([P, 2, HALF_P, PACK], BF16, name="lower_bf", align_bytes=64)
+        lower_bf = keep.tile([P, 2, HALF_P, PACK], BF16, name="lower_bf", tag="lower", align_bytes=64)
         deal(nc.scalar.copy, lower_bf[:], w1_left[:], 0, 2)
         left_bf = keep.tile([P, 2, HALF_P, PACK], BF16, name="left_bf", align_bytes=64)
         deal(nc.vector.tensor_copy, left_bf[:], w1_left[:], 2, PACK)
-        xs_picked = keep.tile([P, S], U8, name="xs_picked", align_bytes=64)
-        nc.vector.tensor_copy(xs_picked[:], xs_all[:].indirect(offs_t[:]))
-        quantize(w1_codes[0][:], w1_scales[0][:], lower_bf[:])
         for t in (2, 3):
             quantize(w1_codes[t][:, 0:HALF_P], w1_scales[t][:, 0:HALF_P], left_bf[:, t - 2 : t - 1])
+        quantize(w1_codes[0][:], w1_scales[0][:], lower_bf[:])
+        xs_picked = keep.tile([P, S], U8, name="xs_picked", tag="lower", align_bytes=64)
+        nc.vector.tensor_copy(xs_picked[:], xs_all[:].indirect(offs_t[:]))
         xw_picked = [keep.tile([P, HALF_S], U32, name=f"xw_picked{a}", align_bytes=64) for a in range(2)]
         for a in range(2):
             nc.vector.tensor_copy(xw_picked[a][:], xw_all[:].indirect(entries(offs_t, a * HALF_S, (a + 1) * HALF_S)))
@@ -195,10 +195,10 @@ def tile_picked_devox_relu_p_kernel(
         for k in range(2):
             nc.scalar.copy(z_words[:, k * U // 2 : (k + 1) * U // 2, 0], backs[k][:])
 
-        scatter(windows[3], 0, S, whole[1][:])
+        scatter(windows[1], 0, S, whole[1][:])
         scatter(windows[2], 0, S, whole[2][:])
-        window_b = {t: windows[{2: 3, 3: 2}[t]][:].rearrange("p (b c) -> p b c", c=P) for t in (2, 3)}
-        emb3 = keep.tile([P, U], F32, name="emb3", tag="turned_z1")
+        window_b = {t: windows[{2: 1, 3: 2}[t]][:].rearrange("p (b c) -> p b c", c=P) for t in (2, 3)}
+        emb3 = keep.tile([P, U], F32, name="emb3", tag="turned_z0")
         nc.sync.dma_start(emb3[:], emb_rows[:, 3, :])
         emb_b = {t: e[:].rearrange("p (b c) -> p b c", c=P) for t, e in ((2, emb2), (3, emb3))}
 

@@ -27,11 +27,12 @@ HALF_S = S // 2
 HALF_P = P // 2
 WIDE = V - P
 
-Z_CHUNKS = [(0, 1), (1, 3), (3, 5), (5, 6), (6, 8)]
-SCALAR_CHUNKS = 4
-LAST_ADDS = [(0, 1), (1, 3), (6, 8), (3, 6)]
-Z_ORDER = [0, 4, 1, 2, 3]
-VECTOR_RELUS = (0, 4, 1, 3)
+Z_CHUNKS = [(0, 1), (1, 3), (3, 4), (4, 6), (6, 8)]
+SCALAR_CHUNKS = 3
+DIRECT = 6
+LAST_ADDS = [(0, 1), (1, 3), (3, 6)]
+Z_ORDER = [0, 4, 3, 1, 2]
+VECTOR_RELUS = (1, 2)
 
 
 def tile_picked_devox_relu_p_kernel(
@@ -52,27 +53,30 @@ def tile_picked_devox_relu_p_kernel(
             return list_tile[:, lo // PER_COLUMN : hi // PER_COLUMN]
 
         def load_scale_rows(plane, src):
-            for q in range(P // QUADRANT):
-                nc.sync.dma_start(
-                    plane[QUADRANT * q : QUADRANT * q + PACK, :].bitcast(I32),
-                    src[0, PACK * q : PACK * (q + 1), :].bitcast(I32),
-                )
+            for r in range(PACK):
+                nc.sync.dma_start(plane[r:P:QUADRANT, :].bitcast(I32), src[0, r : PACK * PACK : PACK, :].bitcast(I32))
 
         xs_all = keep.tile([P, T], U8, name="xs_all", align_bytes=64)
         nc.gpsimd.memset(xs_all[:].bitcast(I32), 0)
         w1_rows = w1.rearrange("(p j) c -> p j c", j=PACK)
-        w1_left = keep.tile([P, PACK, H // 2], F32, name="w1_left")
-        nc.sync.dma_start(w1_left[:], w1_rows[:, :, 0 : H // 2])
+        w1_left = [keep.tile([P, 2, H // 2], F32, name=f"w1_left{a}") for a in range(2)]
+        nc.sync.dma_start(w1_left[0][:], w1_rows[:, 0:2, 0 : H // 2])
         offs_t = load_list("offs_t", offs)
         load_scale_rows(xs_all, x_scales)
+        nc.sync.dma_start(w1_left[1][:], w1_rows[:, 2:4, 0 : H // 2])
         xw_all = keep.tile([P, T], U32, name="xw_all", tag="stage2")
         nc.sync.dma_start(xw_all[:].bitcast(I32), x_words[0].rearrange("p n t -> p (n t)").bitcast(I32))
         cell_t = load_list("cell_t", cell)
         w1_right = keep.tile([P, PACK, H // 2], F32, name="w1_right", tag="right")
         nc.sync.dma_start(w1_right[:], w1_rows[:, :, H // 2 : H])
         emb_rows = emb.rearrange("(p t) c -> p t c", t=PACK)
-        emb01 = keep.tile([P, 2, U], F32, name="emb01", tag="stage1")
-        nc.sync.dma_start(emb01[:], emb_rows[:, 0:2, :])
+        emb_pair = [keep.tile([P, U], F32, name=f"emb_pair{half}", tag=f"pair{half}") for half in range(2)]
+        for e in range(2):
+            nc.sync.dma_start(emb_pair[0][e:P:2, :], emb_rows[0:HALF_P, e, :])
+        emb3 = keep.tile([P, U], F32, name="emb3")
+        nc.sync.dma_start(emb3[:], emb_rows[:, 3, :])
+        for e in range(2):
+            nc.sync.dma_start(emb_pair[1][e:P:2, :], emb_rows[HALF_P:P, e, :])
 
         windows = []
         for t in range(3):
@@ -88,20 +92,24 @@ def tile_picked_devox_relu_p_kernel(
                 src.rearrange("p j (g e t) -> p g j e t", e=2, t=PACK)[:, :, :, :, t0:t1],
             )
 
+        def deal_pair(copy, dst, src):
+            copy(dst.rearrange("p m e j -> p m j e"), src.rearrange("p j (m t) -> p m j t", t=PACK)[:, :, :, 0:2])
+
         def quantize(codes, scales, src):
             nc.vector.quantize_mx(out=codes.bitcast(FP8X4), scales=scales, in_=src.rearrange("p t m j -> p (t m j)"))
 
         w1_codes = [keep.tile([P, P], U32, name=f"w1_codes{i}", align_bytes=64) for i in range(PACK)]
         w1_scales = [keep.tile([P, P], U8, name=f"w1_scales{i}", align_bytes=64) for i in range(PACK)]
-        lower_bf = keep.tile([P, 2, HALF_P, PACK], BF16, name="lower_bf", tag="lower", align_bytes=64)
-        deal(nc.scalar.copy, lower_bf[:], w1_left[:], 0, 2)
+        xs_picked = keep.tile([P, S], U8, name="xs_picked", align_bytes=64)
+        nc.vector.tensor_copy(xs_picked[:], xs_all[:].indirect(offs_t[:]))
+        lower_bf = keep.tile([P, HALF_P, 2, PACK], BF16, name="lower_bf", align_bytes=64)
         left_bf = keep.tile([P, 2, HALF_P, PACK], BF16, name="left_bf", align_bytes=64)
-        deal(nc.vector.tensor_copy, left_bf[:], w1_left[:], 2, PACK)
+        for a, copy in enumerate((nc.scalar.copy, nc.vector.tensor_copy)):
+            deal_pair(copy, lower_bf[:, :, :, 2 * a : 2 * a + 2], w1_left[a][:])
+            deal(copy, left_bf[:, :, :, 2 * a : 2 * a + 2], w1_left[a][:], 2, PACK)
+        quantize(w1_codes[0][:], w1_scales[0][:], lower_bf[:])
         for t in (2, 3):
             quantize(w1_codes[t][:, 0:HALF_P], w1_scales[t][:, 0:HALF_P], left_bf[:, t - 2 : t - 1])
-        quantize(w1_codes[0][:], w1_scales[0][:], lower_bf[:])
-        xs_picked = keep.tile([P, S], U8, name="xs_picked", tag="lower", align_bytes=64)
-        nc.vector.tensor_copy(xs_picked[:], xs_all[:].indirect(offs_t[:]))
         xw_picked = [keep.tile([P, HALF_S], U32, name=f"xw_picked{a}", align_bytes=64) for a in range(2)]
         for a in range(2):
             nc.vector.tensor_copy(xw_picked[a][:], xw_all[:].indirect(entries(offs_t, a * HALF_S, (a + 1) * HALF_S)))
@@ -142,8 +150,8 @@ def tile_picked_devox_relu_p_kernel(
         nc.scalar.activation(h1[:], acc1[:], RELU)
         scatter(windows[1], P, HALF_S, h1[:])
         acc2 = product(2, 0, HALF_S, S, 6)
-        upper_bf = keep.tile([P, 2, HALF_P, PACK], BF16, name="upper_bf", align_bytes=64)
-        deal(nc.scalar.copy, upper_bf[:], w1_right[:], 0, 2)
+        upper_bf = keep.tile([P, HALF_P, 2, PACK], BF16, name="upper_bf", align_bytes=64)
+        deal_pair(nc.scalar.copy, upper_bf[:], w1_right[:])
         right_bf = keep.tile([P, 2, HALF_P, PACK], BF16, name="right_bf", align_bytes=64)
         deal(nc.scalar.copy, right_bf[:], w1_right[:], 2, PACK)
         quantize(w1_codes[1][:], w1_scales[1][:], upper_bf[:])
@@ -160,57 +168,71 @@ def tile_picked_devox_relu_p_kernel(
             whole.append(h)
         scatter(windows[2], 0, S, whole[0][:])
 
-        sums = [psum.tile([P, 2, 2, P], F32, name=f"sums{k}", tag=f"bank{k}") for k in range(4)]
-
-        def turn_into(dst, src, start, stop):
-            nc.tensor.matmul(dst, src, ident[:], start=start, stop=stop, is_transpose=True)
-
-        for b in range(U // P):
-            for e in range(2):
-                turn_into(sums[b // 2][:, b % 2, e, :], emb01[:, e, b * P : (b + 1) * P], b % 2 == 0 and e == 0, False)
-        for w, half in ((1, 0), (0, 0), (2, 1)):
-            for b in range(U // P):
-                turn_into(
-                    sums[b // 2][:, b % 2, :, half * HALF_P : (half + 1) * HALF_P],
-                    windows[w][:, b * P : (b + 1) * P],
-                    False,
-                    w == 2 and b % 2 == 1,
+        emb3_turned = []
+        for k in range(2):
+            fwd = psum.tile([P, 3 * P], F32, name=f"emb3_fwd{k}", tag=f"bank{4 + k}")
+            for b in range(3):
+                nc.tensor.transpose(
+                    fwd[:, b * P : (b + 1) * P], emb3[:, (3 * k + b) * P : (3 * k + b + 1) * P], ident[:]
                 )
+            turned_e = keep.tile([P, 3 * P], F32, name=f"emb3_turned{k}")
+            nc.scalar.copy(turned_e[:], fwd[:])
+            emb3_turned.append(turned_e)
+
+        turned_z = [keep.tile([P, 4, 2, P], BF16, name=f"turned_z{k}") for k in range(2)]
+        for half, sources in enumerate(((windows[1], windows[0]), (windows[2],))):
+            sums = [psum.tile([P, 4, P], F32, name=f"sums{half}_{k}", tag=f"bank{2 * half + k}") for k in range(2)]
+            terms = (emb_pair[half],) + sources
+            for i, src in enumerate(terms):
+                for b in range(U // P):
+                    nc.tensor.matmul(
+                        sums[b // 4][:, b % 4, :],
+                        src[:, b * P : (b + 1) * P],
+                        ident[:],
+                        start=(i == 0 and b % 4 == 0),
+                        stop=(i == len(terms) - 1 and b % 4 == 3),
+                        is_transpose=True,
+                    )
+            for k in range(2):
+                nc.scalar.copy(turned_z[k][:, :, half, :], sums[k][:])
         z_row = keep.tile([P, PACK * U], BF16, name="z_row", align_bytes=64)
         z_bf = z_row[:].rearrange("p (b c a e) -> p b c a e", c=P, a=2, e=2)
         z_words = z_row[:].bitcast(F32).rearrange("p (c a) -> p c a", a=2)
         backs = [psum.tile([P, U // 2], F32, name=f"pairs{k}", tag=f"bank{6 + k}") for k in range(2)]
-        for k in range(4):
-            turned_z = keep.tile([P, 2 * 2 * P], BF16, name=f"turned_z{k}", tag=f"turned_z{k}")
-            nc.scalar.copy(
-                turned_z[:].rearrange("c (b p e) -> c b p e", b=2, e=2), sums[k][:].rearrange("c b e p -> c b p e")
-            )
-            for b2 in range(2):
-                b = 2 * k + b2
-                nc.tensor.transpose(
-                    backs[b // 4][:, (b % 4) * P : (b % 4 + 1) * P],
-                    turned_z[:].bitcast(F32)[:, b2 * P : (b2 + 1) * P],
-                    ident[:],
-                )
+        for k in range(2):
+            words = turned_z[k][:].rearrange("c b h q -> c (b h q)").bitcast(F32)
+            for b in range(4):
+                nc.tensor.transpose(backs[k][:, b * P : (b + 1) * P], words[:, b * P : (b + 1) * P], ident[:])
         for k in range(2):
             nc.scalar.copy(z_words[:, k * U // 2 : (k + 1) * U // 2, 0], backs[k][:])
+
+        emb3_psum = []
+        for k in range(2):
+            held = psum.tile([P, 3, P], F32, name=f"emb3_psum{k}", tag=f"bank{3 - k}")
+            for b in range(3):
+                nc.tensor.transpose(held[:, b, :], emb3_turned[k][:, b * P : (b + 1) * P], ident[:])
+            emb3_psum.append(held)
 
         scatter(windows[1], 0, S, whole[1][:])
         scatter(windows[2], 0, S, whole[2][:])
         window_b = {t: windows[{2: 1, 3: 2}[t]][:].rearrange("p (b c) -> p b c", c=P) for t in (2, 3)}
-        emb3 = keep.tile([P, U], F32, name="emb3", tag="turned_z0")
-        nc.sync.dma_start(emb3[:], emb_rows[:, 3, :])
-        emb_b = {t: e[:].rearrange("p (b c) -> p b c", c=P) for t, e in ((2, emb2), (3, emb3))}
+        emb_b = {t: e.rearrange("p (b c) -> p b c", c=P) for t, e in ((2, emb2[:]), (3, emb3[:]))}
 
-        gate_t = keep.tile([P, D, V], F32, name="gate_t", tag="stage1")
+        gate_t = keep.tile([P, D, V], F32, name="gate_t", tag="pair1")
         nc.sync.dma_start(gate_t[:], gate.rearrange("d p v -> p d v"))
 
         z23_row = keep.tile([P, 2 * U], BF16, name="z23_row")
         z23 = z23_row[:].rearrange("p (b e c) -> p b e c", e=2, c=P)
-        nc.gpsimd.tensor_tensor(z23[:, :, 0, :], window_b[2], emb_b[2], ADD)
+        own = slice(0, DIRECT)
+        direct = slice(DIRECT, U // P)
+        nc.gpsimd.tensor_tensor(z23[:, own, 0, :], window_b[2][:, own], emb_b[2][:, own], ADD)
+        nc.gpsimd.tensor_tensor(z_bf[:, direct, :, 1, 0], window_b[2][:, direct], emb_b[2][:, direct], ADD)
+        nc.gpsimd.tensor_tensor(z_bf[:, direct, :, 1, 1], window_b[3][:, direct], emb_b[3][:, direct], ADD)
         for lo, hi in LAST_ADDS:
-            nc.vector.tensor_tensor(z23[:, lo:hi, 1, :], window_b[3][:, lo:hi], emb_b[3][:, lo:hi], ADD)
-        for c, (lo, hi) in enumerate(Z_CHUNKS):
+            nc.vector.tensor_tensor(
+                z23[:, lo:hi, 1, :], window_b[3][:, lo:hi], emb3_psum[lo // 3][:, lo % 3 : lo % 3 + hi - lo], ADD
+            )
+        for c, (lo, hi) in enumerate(Z_CHUNKS[:-1]):
             copy = nc.scalar.copy if c < SCALAR_CHUNKS else nc.vector.tensor_copy
             copy(z_bf[:, lo:hi, :, 1, :], z23[:, lo:hi].rearrange("p b e c -> p b c e"))
 

@@ -27,12 +27,11 @@ HALF_S = S // 2
 HALF_P = P // 2
 WIDE = V - P
 
-Z_CHUNKS = [(0, 1), (1, 3), (3, 4), (4, 6), (6, 8)]
-SCALAR_CHUNKS = 3
-DIRECT = 6
-LAST_ADDS = [(0, 1), (1, 3), (3, 6)]
-Z_ORDER = [0, 4, 3, 1, 2]
-VECTOR_RELUS = (1, 2)
+Z_CHUNKS = [(0, 1), (1, 3), (3, 5), (5, 6), (6, 8)]
+SCALAR_CHUNKS = 4
+LAST_ADDS = [(0, 1), (1, 3), (6, 8), (3, 6)]
+Z_ORDER = [0, 4, 1, 2, 3]
+VECTOR_RELUS = (0, 4, 1, 3)
 
 
 def tile_picked_devox_relu_p_kernel(
@@ -53,17 +52,19 @@ def tile_picked_devox_relu_p_kernel(
             return list_tile[:, lo // PER_COLUMN : hi // PER_COLUMN]
 
         def load_scale_rows(plane, src):
-            for r in range(PACK):
-                nc.sync.dma_start(plane[r:P:QUADRANT, :].bitcast(I32), src[0, r : PACK * PACK : PACK, :].bitcast(I32))
+            for q in range(P // QUADRANT):
+                nc.sync.dma_start(
+                    plane[QUADRANT * q : QUADRANT * q + PACK, :].bitcast(I32),
+                    src[0, PACK * q : PACK * (q + 1), :].bitcast(I32),
+                )
 
-        xs_all = keep.tile([P, T], U8, name="xs_all", align_bytes=64)
+        xs_all = keep.tile([P, T], U8, name="xs_all", tag="scales", align_bytes=64)
         nc.gpsimd.memset(xs_all[:].bitcast(I32), 0)
         w1_rows = w1.rearrange("(p j) c -> p j c", j=PACK)
-        w1_left = [keep.tile([P, 2, H // 2], F32, name=f"w1_left{a}") for a in range(2)]
-        nc.sync.dma_start(w1_left[0][:], w1_rows[:, 0:2, 0 : H // 2])
+        w1_left = keep.tile([P, PACK, H // 2], F32, name="w1_left")
+        nc.sync.dma_start(w1_left[:], w1_rows[:, :, 0 : H // 2])
         offs_t = load_list("offs_t", offs)
         load_scale_rows(xs_all, x_scales)
-        nc.sync.dma_start(w1_left[1][:], w1_rows[:, 2:4, 0 : H // 2])
         xw_all = keep.tile([P, T], U32, name="xw_all", tag="stage2")
         nc.sync.dma_start(xw_all[:].bitcast(I32), x_words[0].rearrange("p n t -> p (n t)").bitcast(I32))
         cell_t = load_list("cell_t", cell)
@@ -73,8 +74,6 @@ def tile_picked_devox_relu_p_kernel(
         emb_pair = [keep.tile([P, U], F32, name=f"emb_pair{half}", tag=f"pair{half}") for half in range(2)]
         for e in range(2):
             nc.sync.dma_start(emb_pair[0][e:P:2, :], emb_rows[0:HALF_P, e, :])
-        emb3 = keep.tile([P, U], F32, name="emb3")
-        nc.sync.dma_start(emb3[:], emb_rows[:, 3, :])
         for e in range(2):
             nc.sync.dma_start(emb_pair[1][e:P:2, :], emb_rows[HALF_P:P, e, :])
 
@@ -100,16 +99,15 @@ def tile_picked_devox_relu_p_kernel(
 
         w1_codes = [keep.tile([P, P], U32, name=f"w1_codes{i}", align_bytes=64) for i in range(PACK)]
         w1_scales = [keep.tile([P, P], U8, name=f"w1_scales{i}", align_bytes=64) for i in range(PACK)]
-        xs_picked = keep.tile([P, S], U8, name="xs_picked", align_bytes=64)
-        nc.vector.tensor_copy(xs_picked[:], xs_all[:].indirect(offs_t[:]))
-        lower_bf = keep.tile([P, HALF_P, 2, PACK], BF16, name="lower_bf", align_bytes=64)
+        lower_bf = keep.tile([P, HALF_P, 2, PACK], BF16, name="lower_bf", tag="lower", align_bytes=64)
+        deal_pair(nc.scalar.copy, lower_bf[:], w1_left[:])
         left_bf = keep.tile([P, 2, HALF_P, PACK], BF16, name="left_bf", align_bytes=64)
-        for a, copy in enumerate((nc.scalar.copy, nc.vector.tensor_copy)):
-            deal_pair(copy, lower_bf[:, :, :, 2 * a : 2 * a + 2], w1_left[a][:])
-            deal(copy, left_bf[:, :, :, 2 * a : 2 * a + 2], w1_left[a][:], 2, PACK)
-        quantize(w1_codes[0][:], w1_scales[0][:], lower_bf[:])
+        deal(nc.vector.tensor_copy, left_bf[:], w1_left[:], 2, PACK)
         for t in (2, 3):
             quantize(w1_codes[t][:, 0:HALF_P], w1_scales[t][:, 0:HALF_P], left_bf[:, t - 2 : t - 1])
+        quantize(w1_codes[0][:], w1_scales[0][:], lower_bf[:])
+        xs_picked = keep.tile([P, S], U8, name="xs_picked", tag="lower", align_bytes=64)
+        nc.vector.tensor_copy(xs_picked[:], xs_all[:].indirect(offs_t[:]))
         xw_picked = [keep.tile([P, HALF_S], U32, name=f"xw_picked{a}", align_bytes=64) for a in range(2)]
         for a in range(2):
             nc.vector.tensor_copy(xw_picked[a][:], xw_all[:].indirect(entries(offs_t, a * HALF_S, (a + 1) * HALF_S)))
@@ -156,31 +154,27 @@ def tile_picked_devox_relu_p_kernel(
         deal(nc.scalar.copy, right_bf[:], w1_right[:], 2, PACK)
         quantize(w1_codes[1][:], w1_scales[1][:], upper_bf[:])
         h2 = keep.tile([P, HALF_S], F32, name="h2", tag="right")
-        nc.scalar.activation(h2[:], acc2[:], RELU)
+        for a in range(2):
+            nc.scalar.activation(h2[:, a * P : (a + 1) * P], acc2[:, a * P : (a + 1) * P], RELU)
         for t in (2, 3):
             quantize(w1_codes[t][:, HALF_P:P], w1_scales[t][:, HALF_P:P], right_bf[:, t - 2 : t - 1])
-        scatter(windows[0], HALF_S, S, h2[:])
-        whole = []
-        for i, bank in ((1, 7), (2, 4), (3, 5)):
-            acc = product(2 + i, i, 0, S, bank)
-            h = keep.tile([P, S], F32, name=f"h{2 + i}")
+        for a in range(2):
+            scatter(windows[a], HALF_S + a * P, HALF_S + (a + 1) * P, h2[:, a * P : (a + 1) * P])
+        window3 = keep.tile([P, U], F32, name="window3", tag="scales", align_bytes=64)
+        nc.gpsimd.memset(window3[:], 0.0)
+        windows.append(window3)
+        later = []
+        for i, (tile_no, lo, hi, bank) in enumerate(((1, 0, HALF_S, 7), (1, HALF_S, S, 4), (2, 0, S, 5), (3, 0, S, 6))):
+            acc = product(3 + i, tile_no, lo, hi, bank)
+            h = keep.tile([P, hi - lo], F32, name=f"h{3 + i}")
             nc.scalar.activation(h[:], acc[:], RELU)
-            whole.append(h)
-        scatter(windows[2], 0, S, whole[0][:])
+            later.append(h)
+        scatter(windows[2], 0, HALF_S, later[0][:])
+        scatter(windows[3], HALF_S, S, later[1][:])
+        whole = later[1:]
 
-        emb3_turned = []
-        for k in range(2):
-            fwd = psum.tile([P, 3 * P], F32, name=f"emb3_fwd{k}", tag=f"bank{4 + k}")
-            for b in range(3):
-                nc.tensor.transpose(
-                    fwd[:, b * P : (b + 1) * P], emb3[:, (3 * k + b) * P : (3 * k + b + 1) * P], ident[:]
-                )
-            turned_e = keep.tile([P, 3 * P], F32, name=f"emb3_turned{k}")
-            nc.scalar.copy(turned_e[:], fwd[:])
-            emb3_turned.append(turned_e)
-
-        turned_z = [keep.tile([P, 4, 2, P], BF16, name=f"turned_z{k}") for k in range(2)]
-        for half, sources in enumerate(((windows[1], windows[0]), (windows[2],))):
+        turned_z = [keep.tile([P, 4, 2, P], BF16, name=f"turned_z{k}", tag=f"turned_z{k}") for k in range(2)]
+        for half, sources in enumerate(((windows[0], windows[1]), (windows[2], windows[3]))):
             sums = [psum.tile([P, 4, P], F32, name=f"sums{half}_{k}", tag=f"bank{2 * half + k}") for k in range(2)]
             terms = (emb_pair[half],) + sources
             for i, src in enumerate(terms):
@@ -206,16 +200,11 @@ def tile_picked_devox_relu_p_kernel(
         for k in range(2):
             nc.scalar.copy(z_words[:, k * U // 2 : (k + 1) * U // 2, 0], backs[k][:])
 
-        emb3_psum = []
-        for k in range(2):
-            held = psum.tile([P, 3, P], F32, name=f"emb3_psum{k}", tag=f"bank{3 - k}")
-            for b in range(3):
-                nc.tensor.transpose(held[:, b, :], emb3_turned[k][:, b * P : (b + 1) * P], ident[:])
-            emb3_psum.append(held)
-
-        scatter(windows[1], 0, S, whole[1][:])
-        scatter(windows[2], 0, S, whole[2][:])
-        window_b = {t: windows[{2: 1, 3: 2}[t]][:].rearrange("p (b c) -> p b c", c=P) for t in (2, 3)}
+        scatter(windows[0], 0, S, whole[1][:])
+        scatter(windows[3], 0, S, whole[2][:])
+        window_b = {t: windows[{2: 0, 3: 3}[t]][:].rearrange("p (b c) -> p b c", c=P) for t in (2, 3)}
+        emb3 = keep.tile([P, U], F32, name="emb3", tag="turned_z0")
+        nc.sync.dma_start(emb3[:], emb_rows[:, 3, :])
         emb_b = {t: e.rearrange("p (b c) -> p b c", c=P) for t, e in ((2, emb2[:]), (3, emb3[:]))}
 
         gate_t = keep.tile([P, D, V], F32, name="gate_t", tag="pair1")
@@ -223,16 +212,10 @@ def tile_picked_devox_relu_p_kernel(
 
         z23_row = keep.tile([P, 2 * U], BF16, name="z23_row")
         z23 = z23_row[:].rearrange("p (b e c) -> p b e c", e=2, c=P)
-        own = slice(0, DIRECT)
-        direct = slice(DIRECT, U // P)
-        nc.gpsimd.tensor_tensor(z23[:, own, 0, :], window_b[2][:, own], emb_b[2][:, own], ADD)
-        nc.gpsimd.tensor_tensor(z_bf[:, direct, :, 1, 0], window_b[2][:, direct], emb_b[2][:, direct], ADD)
-        nc.gpsimd.tensor_tensor(z_bf[:, direct, :, 1, 1], window_b[3][:, direct], emb_b[3][:, direct], ADD)
+        nc.gpsimd.tensor_tensor(z23[:, :, 0, :], window_b[2], emb_b[2], ADD)
         for lo, hi in LAST_ADDS:
-            nc.vector.tensor_tensor(
-                z23[:, lo:hi, 1, :], window_b[3][:, lo:hi], emb3_psum[lo // 3][:, lo % 3 : lo % 3 + hi - lo], ADD
-            )
-        for c, (lo, hi) in enumerate(Z_CHUNKS[:-1]):
+            nc.vector.tensor_tensor(z23[:, lo:hi, 1, :], window_b[3][:, lo:hi], emb_b[3][:, lo:hi], ADD)
+        for c, (lo, hi) in enumerate(Z_CHUNKS):
             copy = nc.scalar.copy if c < SCALAR_CHUNKS else nc.vector.tensor_copy
             copy(z_bf[:, lo:hi, :, 1, :], z23[:, lo:hi].rearrange("p b e c -> p b c e"))
 

@@ -71,11 +71,8 @@ def tile_picked_devox_relu_p_kernel(
         w1_right = keep.tile([P, PACK, H // 2], F32, name="w1_right", tag="right")
         nc.sync.dma_start(w1_right[:], w1_rows[:, :, H // 2 : H])
         emb_rows = emb.rearrange("(p t) c -> p t c", t=PACK)
-        emb_pair = [keep.tile([P, U], F32, name=f"emb_pair{half}", tag=f"pair{half}") for half in range(2)]
-        for e in range(2):
-            nc.sync.dma_start(emb_pair[0][e:P:2, :], emb_rows[0:HALF_P, e, :])
-        for e in range(2):
-            nc.sync.dma_start(emb_pair[1][e:P:2, :], emb_rows[HALF_P:P, e, :])
+        emb01 = keep.tile([P, 2, U], F32, name="emb01", tag="pair1")
+        nc.sync.dma_start(emb01[:], emb_rows[:, 0:2, :])
 
         windows = []
         for t in range(3):
@@ -91,16 +88,13 @@ def tile_picked_devox_relu_p_kernel(
                 src.rearrange("p j (g e t) -> p g j e t", e=2, t=PACK)[:, :, :, :, t0:t1],
             )
 
-        def deal_pair(copy, dst, src):
-            copy(dst.rearrange("p m e j -> p m j e"), src.rearrange("p j (m t) -> p m j t", t=PACK)[:, :, :, 0:2])
-
         def quantize(codes, scales, src):
             nc.vector.quantize_mx(out=codes.bitcast(FP8X4), scales=scales, in_=src.rearrange("p t m j -> p (t m j)"))
 
         w1_codes = [keep.tile([P, P], U32, name=f"w1_codes{i}", align_bytes=64) for i in range(PACK)]
         w1_scales = [keep.tile([P, P], U8, name=f"w1_scales{i}", align_bytes=64) for i in range(PACK)]
-        lower_bf = keep.tile([P, HALF_P, 2, PACK], BF16, name="lower_bf", tag="lower", align_bytes=64)
-        deal_pair(nc.scalar.copy, lower_bf[:], w1_left[:])
+        lower_bf = keep.tile([P, 2, HALF_P, PACK], BF16, name="lower_bf", tag="lower", align_bytes=64)
+        deal(nc.scalar.copy, lower_bf[:], w1_left[:], 0, 2)
         left_bf = keep.tile([P, 2, HALF_P, PACK], BF16, name="left_bf", align_bytes=64)
         deal(nc.vector.tensor_copy, left_bf[:], w1_left[:], 2, PACK)
         for t in (2, 3):
@@ -148,8 +142,8 @@ def tile_picked_devox_relu_p_kernel(
         nc.scalar.activation(h1[:], acc1[:], RELU)
         scatter(windows[1], P, HALF_S, h1[:])
         acc2 = product(2, 0, HALF_S, S, 6)
-        upper_bf = keep.tile([P, HALF_P, 2, PACK], BF16, name="upper_bf", align_bytes=64)
-        deal_pair(nc.scalar.copy, upper_bf[:], w1_right[:])
+        upper_bf = keep.tile([P, 2, HALF_P, PACK], BF16, name="upper_bf", align_bytes=64)
+        deal(nc.scalar.copy, upper_bf[:], w1_right[:], 0, 2)
         right_bf = keep.tile([P, 2, HALF_P, PACK], BF16, name="right_bf", align_bytes=64)
         deal(nc.scalar.copy, right_bf[:], w1_right[:], 2, PACK)
         quantize(w1_codes[1][:], w1_scales[1][:], upper_bf[:])
@@ -173,30 +167,38 @@ def tile_picked_devox_relu_p_kernel(
         scatter(windows[3], HALF_S, S, later[1][:])
         whole = later[1:]
 
-        turned_z = [keep.tile([P, 4, 2, P], BF16, name=f"turned_z{k}", tag=f"turned_z{k}") for k in range(2)]
-        for half, sources in enumerate(((windows[0], windows[1]), (windows[2], windows[3]))):
-            sums = [psum.tile([P, 4, P], F32, name=f"sums{half}_{k}", tag=f"bank{2 * half + k}") for k in range(2)]
-            terms = (emb_pair[half],) + sources
-            for i, src in enumerate(terms):
-                for b in range(U // P):
-                    nc.tensor.matmul(
-                        sums[b // 4][:, b % 4, :],
-                        src[:, b * P : (b + 1) * P],
-                        ident[:],
-                        start=(i == 0 and b % 4 == 0),
-                        stop=(i == len(terms) - 1 and b % 4 == 3),
-                        is_transpose=True,
-                    )
-            for k in range(2):
-                nc.scalar.copy(turned_z[k][:, :, half, :], sums[k][:])
+        sums = [psum.tile([P, 2, 2, P], F32, name=f"sums{k}", tag=f"bank{k}") for k in range(4)]
+
+        def turn_into(dst, src, start, stop):
+            nc.tensor.matmul(dst, src, ident[:], start=start, stop=stop, is_transpose=True)
+
+        for b in range(U // P):
+            for e in range(2):
+                turn_into(sums[b // 2][:, b % 2, e, :], emb01[:, e, b * P : (b + 1) * P], b % 2 == 0 and e == 0, False)
+        for w, half in ((0, 0), (1, 0), (2, 1), (3, 1)):
+            for b in range(U // P):
+                turn_into(
+                    sums[b // 2][:, b % 2, :, half * HALF_P : (half + 1) * HALF_P],
+                    windows[w][:, b * P : (b + 1) * P],
+                    False,
+                    w == 3 and b % 2 == 1,
+                )
         z_row = keep.tile([P, PACK * U], BF16, name="z_row", align_bytes=64)
         z_bf = z_row[:].rearrange("p (b c a e) -> p b c a e", c=P, a=2, e=2)
         z_words = z_row[:].bitcast(F32).rearrange("p (c a) -> p c a", a=2)
         backs = [psum.tile([P, U // 2], F32, name=f"pairs{k}", tag=f"bank{6 + k}") for k in range(2)]
-        for k in range(2):
-            words = turned_z[k][:].rearrange("c b h q -> c (b h q)").bitcast(F32)
-            for b in range(4):
-                nc.tensor.transpose(backs[k][:, b * P : (b + 1) * P], words[:, b * P : (b + 1) * P], ident[:])
+        for k in range(4):
+            turned_z = keep.tile([P, 2 * 2 * P], BF16, name=f"turned_z{k}", tag=f"turned_z{k}")
+            nc.scalar.copy(
+                turned_z[:].rearrange("c (b p e) -> c b p e", b=2, e=2), sums[k][:].rearrange("c b e p -> c b p e")
+            )
+            for b2 in range(2):
+                b = 2 * k + b2
+                nc.tensor.transpose(
+                    backs[b // 4][:, (b % 4) * P : (b % 4 + 1) * P],
+                    turned_z[:].bitcast(F32)[:, b2 * P : (b2 + 1) * P],
+                    ident[:],
+                )
         for k in range(2):
             nc.scalar.copy(z_words[:, k * U // 2 : (k + 1) * U // 2, 0], backs[k][:])
 

@@ -142,16 +142,14 @@ def tile_picked_devox_relu_p_kernel(
         nc.scalar.activation(h1[:], acc1[:], RELU)
         scatter(windows[1], P, HALF_S, h1[:])
         acc2 = product(2, 0, HALF_S, S, 6)
-        upper_bf = keep.tile([P, 2, HALF_P, PACK], BF16, name="upper_bf", align_bytes=64)
-        deal(nc.scalar.copy, upper_bf[:], w1_right[:], 0, 2)
-        right_bf = keep.tile([P, 2, HALF_P, PACK], BF16, name="right_bf", align_bytes=64)
-        deal(nc.scalar.copy, right_bf[:], w1_right[:], 2, PACK)
-        quantize(w1_codes[1][:], w1_scales[1][:], upper_bf[:])
+        right_bf = keep.tile([P, PACK, HALF_P, PACK], BF16, name="right_bf", align_bytes=64)
+        deal(nc.scalar.copy, right_bf[:], w1_right[:], 0, PACK)
+        quantize(w1_codes[1][:], w1_scales[1][:], right_bf[:, 0:2])
         h2 = keep.tile([P, HALF_S], F32, name="h2", tag="right")
         for a in range(2):
             nc.scalar.activation(h2[:, a * P : (a + 1) * P], acc2[:, a * P : (a + 1) * P], RELU)
         for t in (2, 3):
-            quantize(w1_codes[t][:, HALF_P:P], w1_scales[t][:, HALF_P:P], right_bf[:, t - 2 : t - 1])
+            quantize(w1_codes[t][:, HALF_P:P], w1_scales[t][:, HALF_P:P], right_bf[:, t : t + 1])
         for a in range(2):
             scatter(windows[a], HALF_S + a * P, HALF_S + (a + 1) * P, h2[:, a * P : (a + 1) * P])
         window3 = keep.tile([P, U], F32, name="window3", tag="scales", align_bytes=64)

@@ -65,7 +65,7 @@ def tile_picked_devox_relu_p_kernel(
         nc.sync.dma_start(w1_left[:], w1_rows[:, :, 0 : H // 2])
         offs_t = load_list("offs_t", offs)
         load_scale_rows(xs_all, x_scales)
-        xw_all = keep.tile([P, T], U32, name="xw_all", tag="stage2")
+        xw_all = keep.tile([P, T], U32, name="xw_all", tag="stage2", align_bytes=64)
         nc.sync.dma_start(xw_all[:].bitcast(I32), x_words[0].rearrange("p n t -> p (n t)").bitcast(I32))
         cell_t = load_list("cell_t", cell)
         w1_right = keep.tile([P, PACK, H // 2], F32, name="w1_right", tag="right")
@@ -91,23 +91,24 @@ def tile_picked_devox_relu_p_kernel(
         def quantize(codes, scales, src):
             nc.vector.quantize_mx(out=codes.bitcast(FP8X4), scales=scales, in_=src.rearrange("p t m j -> p (t m j)"))
 
-        w1_codes = [keep.tile([P, P], U32, name=f"w1_codes{i}", align_bytes=64) for i in range(PACK)]
+        pair_codes = [keep.tile([P, P], U32, name=f"pair_codes{i}", align_bytes=64) for i in range(2)]
         w1_scales = [keep.tile([P, P], U8, name=f"w1_scales{i}", align_bytes=64) for i in range(PACK)]
         lower_bf = keep.tile([P, 2, HALF_P, PACK], BF16, name="lower_bf", tag="lower", align_bytes=64)
-        deal(nc.scalar.copy, lower_bf[:], w1_left[:], 0, 2)
+        deal(nc.scalar.copy, lower_bf[:, :, 0 : HALF_P // 2], w1_left[:, :, 0:P], 0, 2)
+        deal(nc.vector.tensor_copy, lower_bf[:, :, HALF_P // 2 : HALF_P], w1_left[:, :, P : 2 * P], 0, 2)
         left_bf = keep.tile([P, 2, HALF_P, PACK], BF16, name="left_bf", align_bytes=64)
-        deal(nc.vector.tensor_copy, left_bf[:], w1_left[:], 2, PACK)
-        for t in (2, 3):
-            quantize(w1_codes[t][:, 0:HALF_P], w1_scales[t][:, 0:HALF_P], left_bf[:, t - 2 : t - 1])
-        quantize(w1_codes[0][:], w1_scales[0][:], lower_bf[:])
+        deal(nc.scalar.copy, left_bf[:], w1_left[:], 2, PACK)
+        quantize(pair_codes[0][:], w1_scales[0][:], lower_bf[:])
         xs_picked = keep.tile([P, S], U8, name="xs_picked", tag="lower", align_bytes=64)
         nc.vector.tensor_copy(xs_picked[:], xs_all[:].indirect(offs_t[:]))
         xw_picked = [keep.tile([P, HALF_S], U32, name=f"xw_picked{a}", align_bytes=64) for a in range(2)]
         for a in range(2):
             nc.vector.tensor_copy(xw_picked[a][:], xw_all[:].indirect(entries(offs_t, a * HALF_S, (a + 1) * HALF_S)))
+        plane_codes = keep.tile([P, 2 * P], U32, name="plane_codes", tag="stage2", align_bytes=64)
+        w1_codes = [pair_codes[0][:], pair_codes[1][:], plane_codes[:, 0:P], plane_codes[:, P : 2 * P]]
+        for t in (2, 3):
+            quantize(w1_codes[t][:, 0:HALF_P], w1_scales[t][:, 0:HALF_P], left_bf[:, t - 2 : t - 1])
 
-        emb2 = keep.tile([P, U], F32, name="emb2", tag="stage2")
-        nc.sync.dma_start(emb2[:], emb_rows[:, 2, :])
         pos_t = [load_list(f"pos{d}_t", src) for d, src in enumerate((pos1, pos2, pos3, pos4))]
         w2_codes = keep.tile([P, 2 * N], U8, name="w2_codes", align_bytes=64)
         nc.sync.dma_start(w2_codes[:].bitcast(I32), w2_words[0].bitcast(I32))
@@ -121,7 +122,7 @@ def tile_picked_devox_relu_p_kernel(
                 c0, c1 = max(lo, a * HALF_S), min(hi, (a + 1) * HALF_S)
                 nc.tensor.matmul_mx(
                     out=h_acc[:, c0 - lo : c1 - lo],
-                    lhsT=w1_codes[tile_no][:].bitcast(FP8X4),
+                    lhsT=w1_codes[tile_no].bitcast(FP8X4),
                     lhsT_scale=w1_scales[tile_no][:],
                     rhs=xw_picked[a][:, c0 - a * HALF_S : c1 - a * HALF_S].bitcast(FP8X4),
                     rhs_scale=xs_picked[:, c0:c1],
@@ -135,7 +136,7 @@ def tile_picked_devox_relu_p_kernel(
 
         acc0 = product(0, 0, 0, P, 4)
         h0 = keep.tile([P, P], F32, name="h0")
-        nc.vector.tensor_scalar_max(h0[:], acc0[:], 0.0)
+        nc.scalar.activation(h0[:], acc0[:], RELU)
         scatter(windows[0], 0, P, h0[:])
         acc1 = product(1, 0, P, HALF_S, 5)
         h1 = keep.tile([P, P], F32, name="h1")
@@ -144,7 +145,7 @@ def tile_picked_devox_relu_p_kernel(
         acc2 = product(2, 0, HALF_S, S, 6)
         right_bf = keep.tile([P, PACK, HALF_P, PACK], BF16, name="right_bf", align_bytes=64)
         deal(nc.scalar.copy, right_bf[:], w1_right[:], 0, PACK)
-        quantize(w1_codes[1][:], w1_scales[1][:], right_bf[:, 0:2])
+        quantize(w1_codes[1], w1_scales[1][:], right_bf[:, 0:2])
         h2 = keep.tile([P, HALF_S], F32, name="h2", tag="right")
         for a in range(2):
             nc.scalar.activation(h2[:, a * P : (a + 1) * P], acc2[:, a * P : (a + 1) * P], RELU)
@@ -164,6 +165,9 @@ def tile_picked_devox_relu_p_kernel(
         scatter(windows[2], 0, HALF_S, later[0][:])
         scatter(windows[3], HALF_S, S, later[1][:])
         whole = later[1:]
+
+        emb2 = keep.tile([P, U], F32, name="emb2", tag="stage2", align_bytes=64)
+        nc.sync.dma_start(emb2[:], emb_rows[:, 2, :])
 
         sums = [psum.tile([P, 2, 2, P], F32, name=f"sums{k}", tag=f"bank{k}") for k in range(4)]
 

@@ -27,11 +27,11 @@ HALF_S = S // 2
 HALF_P = P // 2
 WIDE = V - P
 
-Z_CHUNKS = [(0, 1), (1, 3), (3, 5), (5, 6), (6, 8)]
+Z_CHUNKS = [(0, 1), (1, 3), (3, 4), (4, 5), (5, 7), (7, 8)]
 SCALAR_CHUNKS = 4
-LAST_ADDS = [(0, 1), (1, 3), (6, 8), (3, 6)]
-Z_ORDER = [0, 4, 1, 2, 3]
-VECTOR_RELUS = (0, 4, 1, 3)
+LAST_ADDS = [(0, 1), (1, 3), (5, 8), (3, 5)]
+Z_ORDER = [0, 4, 5, 1, 2, 3]
+VECTOR_RELUS = (2, 3)
 
 
 def tile_picked_devox_relu_p_kernel(

@@ -25,13 +25,14 @@ QUADRANT = 32
 BANKS = 8
 HALF_S = S // 2
 HALF_P = P // 2
+FIRST = 128
 WIDE = V - P
 
-Z_CHUNKS = [(0, 1), (1, 3), (3, 4), (4, 5), (5, 7), (7, 8)]
-SCALAR_CHUNKS = 4
-LAST_ADDS = [(0, 1), (1, 3), (5, 8), (3, 5)]
-Z_ORDER = [0, 4, 5, 1, 2, 3]
-VECTOR_RELUS = (2, 3)
+COPY = mybir.ActivationFunctionType.Copy
+CHUNKS = [(0, 256), (256, 512), (512, 768), (768, 896), (896, 1024)]
+PAIR_TILES = [(0, 512), (512, 1024)]
+VECTOR_WEAVES = (2, 3, 4)
+VECTOR_RELUS = ()
 
 
 def tile_picked_devox_relu_p_kernel(
@@ -71,13 +72,20 @@ def tile_picked_devox_relu_p_kernel(
         w1_right = keep.tile([P, PACK, H // 2], F32, name="w1_right", tag="right")
         nc.sync.dma_start(w1_right[:], w1_rows[:, :, H // 2 : H])
         emb_rows = emb.rearrange("(p t) c -> p t c", t=PACK)
+        pairs = [keep.tile([P, 2, hi - lo], F32, name=f"pairs{c}") for c, (lo, hi) in enumerate(PAIR_TILES)]
+        for c, (lo, hi) in enumerate(PAIR_TILES):
+            nc.sync.dma_start(pairs[c][:, 1, :], emb_rows[:, 2, lo:hi])
         emb01 = keep.tile([P, 2, U], F32, name="emb01", tag="pair1")
         nc.sync.dma_start(emb01[:], emb_rows[:, 0:2, :])
+        emb3 = keep.tile([P, U], F32, name="emb3")
+        nc.sync.dma_start(emb3[:], emb_rows[:, 3, :])
+        gate_t = keep.tile([P, D, V], F32, name="gate_t")
+        nc.sync.dma_start(gate_t[:], gate.rearrange("d p v -> p d v"))
 
         windows = []
-        for t in range(3):
-            window = keep.tile([P, U], F32, name=f"window{t}")
-            nc.vector.memset(window[:], 0.0)
+        for t in range(4):
+            window = keep.tile([P, U], F32, name=f"window{t}", tag=f"window{t}")
+            (nc.gpsimd if t == 3 else nc.vector).memset(window[:].bitcast(I32), 0)
             windows.append(window)
         ident = keep.tile([P, P], F32, name="ident")
         make_identity(nc, ident[:])
@@ -134,40 +142,47 @@ def tile_picked_devox_relu_p_kernel(
         def scatter(window, lo, hi, h):
             nc.vector.tensor_copy(window[:].indirect(entries(cell_t, lo, hi)), h)
 
+        def scatter_on_scalar(window, lo, hi, h):
+            nc.scalar.activation(window[:].indirect(entries(cell_t, lo, hi)), h, COPY)
+
+        right_bf = keep.tile([P, PACK, HALF_P, PACK], BF16, name="right_bf", align_bytes=64)
+        for t in (2, 0, 1, 3):
+            nc.gpsimd.tensor_scalar(
+                right_bf[:, t], w1_right[:].rearrange("p j (m t) -> p t m j", t=PACK)[:, t], 1.0, 0.0, MULT, ADD
+            )
+
         acc0 = product(0, 0, 0, P, 4)
+        acc1 = product(1, 0, P, HALF_S, 5)
+        acc2 = product(2, 0, HALF_S, S, 6)
         h0 = keep.tile([P, P], F32, name="h0")
         nc.scalar.activation(h0[:], acc0[:], RELU)
         scatter(windows[0], 0, P, h0[:])
-        acc1 = product(1, 0, P, HALF_S, 5)
-        h1 = keep.tile([P, P], F32, name="h1")
-        nc.scalar.activation(h1[:], acc1[:], RELU)
-        scatter(windows[1], P, HALF_S, h1[:])
-        acc2 = product(2, 0, HALF_S, S, 6)
-        right_bf = keep.tile([P, PACK, HALF_P, PACK], BF16, name="right_bf", align_bytes=64)
-        deal(nc.scalar.copy, right_bf[:], w1_right[:], 0, PACK)
+        h2 = keep.tile([P, HALF_S], F32, name="h2")
+        nc.scalar.activation(h2[:], acc2[:], RELU)
+        scatter_on_scalar(windows[1], HALF_S, S, h2[:])
+        quantize(w1_codes[2][:, HALF_P:P], w1_scales[2][:, HALF_P:P], right_bf[:, 2:3])
+        h1 = keep.tile([P, P], F32, name="h1", tag="right")
+        nc.vector.tensor_scalar_max(h1[:], acc1[:], 0.0)
         quantize(w1_codes[1], w1_scales[1][:], right_bf[:, 0:2])
-        h2 = keep.tile([P, HALF_S], F32, name="h2", tag="right")
-        for a in range(2):
-            nc.scalar.activation(h2[:, a * P : (a + 1) * P], acc2[:, a * P : (a + 1) * P], RELU)
-        for t in (2, 3):
-            quantize(w1_codes[t][:, HALF_P:P], w1_scales[t][:, HALF_P:P], right_bf[:, t : t + 1])
-        for a in range(2):
-            scatter(windows[a], HALF_S + a * P, HALF_S + (a + 1) * P, h2[:, a * P : (a + 1) * P])
-        window3 = keep.tile([P, U], F32, name="window3", tag="scales", align_bytes=64)
-        nc.gpsimd.memset(window3[:], 0.0)
-        windows.append(window3)
-        later = []
-        for i, (tile_no, lo, hi, bank) in enumerate(((1, 0, HALF_S, 7), (1, HALF_S, S, 4), (2, 0, S, 5), (3, 0, S, 6))):
-            acc = product(3 + i, tile_no, lo, hi, bank)
-            h = keep.tile([P, hi - lo], F32, name=f"h{3 + i}")
-            nc.scalar.activation(h[:], acc[:], RELU)
-            later.append(h)
-        scatter(windows[2], 0, HALF_S, later[0][:])
-        scatter(windows[3], HALF_S, S, later[1][:])
-        whole = later[1:]
+        quantize(w1_codes[3][:, HALF_P:P], w1_scales[3][:, HALF_P:P], right_bf[:, 3:4])
+        scatter(windows[0], P, HALF_S, h1[:])
+        window4 = keep.tile([P, U], F32, name="window4", tag="scales", align_bytes=64)
+        nc.gpsimd.memset(window4[:], 0.0)
+        windows.append(window4)
 
-        emb2 = keep.tile([P, U], F32, name="emb2", tag="stage2", align_bytes=64)
-        nc.sync.dma_start(emb2[:], emb_rows[:, 2, :])
+        acc_p2 = product(3, 2, 0, S, 7)
+        h_p2 = keep.tile([P, S], F32, name="h_p2")
+        nc.scalar.activation(h_p2[:], acc_p2[:], RELU)
+        scatter(windows[3], 0, S, h_p2[:])
+        acc_up = product(4, 1, 0, S, 4)
+        acc_p3 = product(5, 3, 0, S, 6)
+        h_up = keep.tile([P, S], F32, name="h_up")
+        nc.scalar.activation(h_up[:], acc_up[:], RELU)
+        h_p3 = keep.tile([P, S], F32, name="h_p3")
+        scatter_on_scalar(windows[2], 0, HALF_S, h_up[:, 0:HALF_S])
+        nc.scalar.activation(h_p3[:], acc_p3[:], RELU)
+        scatter_on_scalar(windows[2], HALF_S, S, h_up[:, HALF_S:S])
+        scatter(windows[4], 0, S, h_p3[:])
 
         sums = [psum.tile([P, 2, 2, P], F32, name=f"sums{k}", tag=f"bank{k}") for k in range(4)]
 
@@ -177,20 +192,28 @@ def tile_picked_devox_relu_p_kernel(
         for b in range(U // P):
             for e in range(2):
                 turn_into(sums[b // 2][:, b % 2, e, :], emb01[:, e, b * P : (b + 1) * P], b % 2 == 0 and e == 0, False)
-        for w, half in ((0, 0), (1, 0), (2, 1), (3, 1)):
+        for w, half in ((0, 0), (1, 0), (2, 1)):
             for b in range(U // P):
                 turn_into(
                     sums[b // 2][:, b % 2, :, half * HALF_P : (half + 1) * HALF_P],
                     windows[w][:, b * P : (b + 1) * P],
                     False,
-                    w == 3 and b % 2 == 1,
+                    w == 2 and b % 2 == 1,
                 )
-        z_row = keep.tile([P, PACK * U], BF16, name="z_row", align_bytes=64)
-        z_bf = z_row[:].rearrange("p (b c a e) -> p b c a e", c=P, a=2, e=2)
-        z_words = z_row[:].bitcast(F32).rearrange("p (c a) -> p c a", a=2)
-        backs = [psum.tile([P, U // 2], F32, name=f"pairs{k}", tag=f"bank{6 + k}") for k in range(2)]
+
+        def words_of(lo, hi):
+            c = lo // (U // 2)
+            return pairs[c][:, :, lo - c * U // 2 : hi - c * U // 2]
+
+        def plane_of(lo, hi, e):
+            return words_of(lo, hi)[:, 1, :].bitcast(BF16).rearrange("p (c e) -> p c e", e=2)[:, :, e]
+
+        for lo, hi in PAIR_TILES:
+            nc.gpsimd.tensor_tensor(plane_of(lo, hi, 0), windows[3][:, lo:hi], words_of(lo, hi)[:, 1, :], ADD)
+
+        backs = [psum.tile([P, U // 2], F32, name=f"backs{k}", tag=f"bank{6 + k}") for k in range(2)]
         for k in range(4):
-            turned_z = keep.tile([P, 2 * 2 * P], BF16, name=f"turned_z{k}", tag=f"turned_z{k}")
+            turned_z = keep.tile([P, 2 * 2 * P], BF16, name=f"turned_z{k}")
             nc.scalar.copy(
                 turned_z[:].rearrange("c (b p e) -> c b p e", b=2, e=2), sums[k][:].rearrange("c b e p -> c b p e")
             )
@@ -201,41 +224,24 @@ def tile_picked_devox_relu_p_kernel(
                     turned_z[:].bitcast(F32)[:, b2 * P : (b2 + 1) * P],
                     ident[:],
                 )
-        for k in range(2):
-            nc.scalar.copy(z_words[:, k * U // 2 : (k + 1) * U // 2, 0], backs[k][:])
-
-        scatter(windows[0], 0, S, whole[1][:])
-        scatter(windows[3], 0, S, whole[2][:])
-        window_b = {t: windows[{2: 0, 3: 3}[t]][:].rearrange("p (b c) -> p b c", c=P) for t in (2, 3)}
-        emb3 = keep.tile([P, U], F32, name="emb3", tag="turned_z0")
-        nc.sync.dma_start(emb3[:], emb_rows[:, 3, :])
-        emb_b = {t: e.rearrange("p (b c) -> p b c", c=P) for t, e in ((2, emb2[:]), (3, emb3[:]))}
-
-        gate_t = keep.tile([P, D, V], F32, name="gate_t", tag="pair1")
-        nc.sync.dma_start(gate_t[:], gate.rearrange("d p v -> p d v"))
-
-        z23_row = keep.tile([P, 2 * U], BF16, name="z23_row")
-        z23 = z23_row[:].rearrange("p (b e c) -> p b e c", e=2, c=P)
-        nc.gpsimd.tensor_tensor(z23[:, :, 0, :], window_b[2], emb_b[2], ADD)
-        for lo, hi in LAST_ADDS:
-            nc.vector.tensor_tensor(z23[:, lo:hi, 1, :], window_b[3][:, lo:hi], emb_b[3][:, lo:hi], ADD)
-        for c, (lo, hi) in enumerate(Z_CHUNKS):
-            copy = nc.scalar.copy if c < SCALAR_CHUNKS else nc.vector.tensor_copy
-            copy(z_bf[:, lo:hi, :, 1, :], z23[:, lo:hi].rearrange("p b e c -> p b c e"))
+            if k % 2 == 1:
+                nc.scalar.copy(pairs[k // 2][:, 0, :], backs[k // 2][:])
+        for lo, hi in CHUNKS:
+            nc.vector.tensor_tensor(plane_of(lo, hi, 1), windows[4][:, lo:hi], emb3[:, lo:hi], ADD)
+        z_bf = []
+        for c, (lo, hi) in enumerate(CHUNKS):
+            z = keep.tile([P, PACK * (hi - lo)], BF16, name=f"z_bf{c}", align_bytes=64)
+            copy = nc.vector.tensor_copy if c in VECTOR_WEAVES else nc.scalar.copy
+            copy(z[:].bitcast(F32).rearrange("p (c a) -> p c a", a=2), words_of(lo, hi).rearrange("p a c -> p c a"))
+            z_bf.append(z)
 
         y = keep.tile([P, U], F32, name="y")
-        y_accs = []
-        for i, c in enumerate(Z_ORDER):
-            lo, hi = Z_CHUNKS[c]
-            width = (hi - lo) * P
+        for c, (lo, hi) in enumerate(CHUNKS):
+            width = hi - lo
             z_codes = keep.tile([P, width], U32, name=f"z_codes{c}", align_bytes=64)
             z_scales = keep.tile([P, width], U8, name=f"z_scales{c}", align_bytes=64)
-            nc.vector.quantize_mx(
-                out=z_codes[:].bitcast(FP8X4),
-                scales=z_scales[:],
-                in_=z_row[:, lo * P * PACK : hi * P * PACK],
-            )
-            y_acc = psum.tile([P, width], F32, name=f"y_acc{c}", tag=f"bank{i}")
+            nc.vector.quantize_mx(out=z_codes[:].bitcast(FP8X4), scales=z_scales[:], in_=z_bf[c][:])
+            y_acc = psum.tile([P, width], F32, name=f"y_acc{c}", tag=f"bank{c}")
             nc.tensor.matmul_mx(
                 out=y_acc[:],
                 lhsT=w2_codes[:].bitcast(FP4X4),
@@ -245,12 +251,10 @@ def tile_picked_devox_relu_p_kernel(
                 start=True,
                 stop=True,
             )
-            y_accs.append((y[:, lo * P : hi * P], y_acc))
-            if c not in VECTOR_RELUS:
-                nc.scalar.activation(y[:, lo * P : hi * P], y_acc[:], RELU)
-        for c in VECTOR_RELUS:
-            y_cols, y_acc = y_accs[Z_ORDER.index(c)]
-            nc.vector.tensor_scalar_max(y_cols, y_acc[:], 0.0)
+            if c in VECTOR_RELUS:
+                nc.vector.tensor_scalar_max(y[:, lo:hi], y_acc[:], 0.0)
+            else:
+                nc.scalar.activation(y[:, lo:hi], y_acc[:], RELU)
 
 
         def gather_term(d, lo, hi):

@@ -25,14 +25,14 @@ QUADRANT = 32
 BANKS = 8
 HALF_S = S // 2
 HALF_P = P // 2
-FIRST = 128
-WIDE = V - P
+LAST = 384
+WIDE = V // 2
 
 COPY = mybir.ActivationFunctionType.Copy
-CHUNKS = [(0, 256), (256, 512), (512, 768), (768, 896), (896, 1024)]
+CHUNKS = [(512, 768), (0, 256), (768, 1024), (256, 512)]
 PAIR_TILES = [(0, 512), (512, 1024)]
-VECTOR_WEAVES = (2, 3, 4)
-VECTOR_RELUS = ()
+VECTOR_WEAVES = (1, 3)
+VECTOR_RELUS = (2,)
 
 
 def tile_picked_devox_relu_p_kernel(
@@ -79,8 +79,8 @@ def tile_picked_devox_relu_p_kernel(
         nc.sync.dma_start(emb01[:], emb_rows[:, 0:2, :])
         emb3 = keep.tile([P, U], F32, name="emb3")
         nc.sync.dma_start(emb3[:], emb_rows[:, 3, :])
-        gate_t = keep.tile([P, D, V], F32, name="gate_t")
-        nc.sync.dma_start(gate_t[:], gate.rearrange("d p v -> p d v"))
+        gate_t = keep.tile([P, D - 1, V], F32, name="gate_t")
+        nc.sync.dma_start(gate_t[:], gate[0 : D - 1].rearrange("d p v -> p d v"))
 
         windows = []
         for t in range(4):
@@ -124,10 +124,15 @@ def tile_picked_devox_relu_p_kernel(
         nc.vector.memset(w2_plane[:].bitcast(I32), 0)
         load_scale_rows(w2_plane, w2_scales)
 
+        gate_col = keep.tile([P, V // P], F32, name="gate_col")
+        with nc.allow_non_contiguous_dma(reason="one gate value a partition"):
+            nc.sync.dma_start(gate_col[:], gate[D - 1, 0, :].rearrange("(b p) -> p b", p=P))
+
         def product(i, tile_no, lo, hi, bank):
             h_acc = psum.tile([P, hi - lo], F32, name=f"h_acc{i}", tag=f"bank{bank}")
-            for a in range(lo // HALF_S, (hi - 1) // HALF_S + 1):
-                c0, c1 = max(lo, a * HALF_S), min(hi, (a + 1) * HALF_S)
+            cuts = sorted({lo, hi} | {c for c in (P, HALF_S) if lo < c < hi and (c == HALF_S or hi < HALF_S)})
+            for c0, c1 in zip(cuts, cuts[1:]):
+                a = c0 // HALF_S
                 nc.tensor.matmul_mx(
                     out=h_acc[:, c0 - lo : c1 - lo],
                     lhsT=w1_codes[tile_no].bitcast(FP8X4),
@@ -145,44 +150,40 @@ def tile_picked_devox_relu_p_kernel(
         def scatter_on_scalar(window, lo, hi, h):
             nc.scalar.activation(window[:].indirect(entries(cell_t, lo, hi)), h, COPY)
 
+        acc0 = product(0, 0, 0, HALF_S, 4)
+        acc1 = product(1, 0, HALF_S, LAST, 5)
+        acc2 = product(2, 0, LAST, S, 6)
+        for a, (acc, lo, hi) in enumerate(((acc0, 0, HALF_S), (acc1, HALF_S, LAST))):
+            h = keep.tile([P, hi - lo], F32, name=f"h_low{a}")
+            nc.scalar.activation(h[:], acc[:], RELU)
+            scatter_on_scalar(windows[1], lo, hi, h[:])
         right_bf = keep.tile([P, PACK, HALF_P, PACK], BF16, name="right_bf", align_bytes=64)
-        for t in (2, 0, 1, 3):
-            nc.gpsimd.tensor_scalar(
-                right_bf[:, t], w1_right[:].rearrange("p j (m t) -> p t m j", t=PACK)[:, t], 1.0, 0.0, MULT, ADD
-            )
-
-        acc0 = product(0, 0, 0, P, 4)
-        acc1 = product(1, 0, P, HALF_S, 5)
-        acc2 = product(2, 0, HALF_S, S, 6)
-        h0 = keep.tile([P, P], F32, name="h0")
-        nc.scalar.activation(h0[:], acc0[:], RELU)
-        scatter(windows[0], 0, P, h0[:])
-        h2 = keep.tile([P, HALF_S], F32, name="h2")
-        nc.scalar.activation(h2[:], acc2[:], RELU)
-        scatter_on_scalar(windows[1], HALF_S, S, h2[:])
+        deal(nc.vector.tensor_copy, right_bf[:], w1_right[:], 0, PACK)
+        h0 = keep.tile([P, S - LAST], F32, name="h0", tag="right")
+        nc.vector.tensor_scalar_max(h0[:], acc2[:], 0.0)
         quantize(w1_codes[2][:, HALF_P:P], w1_scales[2][:, HALF_P:P], right_bf[:, 2:3])
-        h1 = keep.tile([P, P], F32, name="h1", tag="right")
-        nc.vector.tensor_scalar_max(h1[:], acc1[:], 0.0)
         quantize(w1_codes[1], w1_scales[1][:], right_bf[:, 0:2])
         quantize(w1_codes[3][:, HALF_P:P], w1_scales[3][:, HALF_P:P], right_bf[:, 3:4])
-        scatter(windows[0], P, HALF_S, h1[:])
+        scatter(windows[0], LAST, S, h0[:])
         window4 = keep.tile([P, U], F32, name="window4", tag="scales", align_bytes=64)
         nc.gpsimd.memset(window4[:], 0.0)
         windows.append(window4)
 
         acc_p2 = product(3, 2, 0, S, 7)
         h_p2 = keep.tile([P, S], F32, name="h_p2")
-        nc.scalar.activation(h_p2[:], acc_p2[:], RELU)
+        nc.vector.tensor_scalar_max(h_p2[:], acc_p2[:], 0.0)
         scatter(windows[3], 0, S, h_p2[:])
         acc_up = product(4, 1, 0, S, 4)
-        acc_p3 = product(5, 3, 0, S, 6)
+        acc_p3 = [product(5 + a, 3, a * HALF_S, (a + 1) * HALF_S, 5 + a) for a in range(2)]
         h_up = keep.tile([P, S], F32, name="h_up")
         nc.scalar.activation(h_up[:], acc_up[:], RELU)
         h_p3 = keep.tile([P, S], F32, name="h_p3")
         scatter_on_scalar(windows[2], 0, HALF_S, h_up[:, 0:HALF_S])
-        nc.scalar.activation(h_p3[:], acc_p3[:], RELU)
+        nc.scalar.activation(h_p3[:, 0:HALF_S], acc_p3[0][:], RELU)
         scatter_on_scalar(windows[2], HALF_S, S, h_up[:, HALF_S:S])
-        scatter(windows[4], 0, S, h_p3[:])
+        scatter(windows[4], 0, HALF_S, h_p3[:, 0:HALF_S])
+        nc.scalar.activation(h_p3[:, HALF_S:S], acc_p3[1][:], RELU)
+        scatter(windows[4], HALF_S, S, h_p3[:, HALF_S:S])
 
         sums = [psum.tile([P, 2, 2, P], F32, name=f"sums{k}", tag=f"bank{k}") for k in range(4)]
 
@@ -213,7 +214,7 @@ def tile_picked_devox_relu_p_kernel(
 
         backs = [psum.tile([P, U // 2], F32, name=f"backs{k}", tag=f"bank{6 + k}") for k in range(2)]
         for k in range(4):
-            turned_z = keep.tile([P, 2 * 2 * P], BF16, name=f"turned_z{k}")
+            turned_z = keep.tile([P, 2 * 2 * P], BF16, name=f"turned_z{k}", tag=f"turned_z{k}", align_bytes=64)
             nc.scalar.copy(
                 turned_z[:].rearrange("c (b p e) -> c b p e", b=2, e=2), sums[k][:].rearrange("c b e p -> c b p e")
             )
@@ -224,9 +225,9 @@ def tile_picked_devox_relu_p_kernel(
                     turned_z[:].bitcast(F32)[:, b2 * P : (b2 + 1) * P],
                     ident[:],
                 )
-            if k % 2 == 1:
-                nc.scalar.copy(pairs[k // 2][:, 0, :], backs[k // 2][:])
-        for lo, hi in CHUNKS:
+        for k in range(2):
+            nc.scalar.copy(pairs[k][:, 0, :], backs[k][:])
+        for lo, hi in reversed(PAIR_TILES):
             nc.vector.tensor_tensor(plane_of(lo, hi, 1), windows[4][:, lo:hi], emb3[:, lo:hi], ADD)
         z_bf = []
         for c, (lo, hi) in enumerate(CHUNKS):
@@ -256,36 +257,48 @@ def tile_picked_devox_relu_p_kernel(
             else:
                 nc.scalar.activation(y[:, lo:hi], y_acc[:], RELU)
 
-
         def gather_term(d, lo, hi):
             term = keep.tile([P, hi - lo], F32, name=f"term{d}_{lo}")
             nc.vector.tensor_tensor(term[:], y[:].indirect(entries(pos_t[d], lo, hi)), gate_t[:, d, lo:hi], MULT)
             return term
 
+        blocks = V // P
+        plain = keep.tile([P, V], F32, name="plain")
+        nc.scalar.activation(plain[:], y[:].indirect(pos_t[D - 1][:]), COPY)
+        turned_plain = psum.tile([P, V], F32, name="turned_plain", tag="bank5")
+        for b in range(blocks):
+            nc.tensor.transpose(turned_plain[:, b * P : (b + 1) * P], plain[:, b * P : (b + 1) * P], ident[:])
+        scaled = keep.tile([P, V], F32, name="scaled")
+        for b in range(blocks):
+            nc.scalar.activation(
+                scaled[:, b * P : (b + 1) * P], turned_plain[:, b * P : (b + 1) * P], COPY, scale=gate_col[:, b : b + 1]
+            )
         groups = [(0, WIDE), (WIDE, V)]
-        turned = [psum.tile([P, P], F32, name=f"turned{b}", tag=f"bank{4 + b}") for b in range(V // P)]
-        for d, lo, hi in [(0, 0, V)] + [(d, lo, hi) for lo, hi in groups for d in range(1, D - 1)]:
+        turned = [psum.tile([P, hi - lo], F32, name=f"turned{a}", tag=f"bank{6 + a}") for a, (lo, hi) in enumerate(groups)]
+        for d, lo, hi in [(0, 0, V)] + [(1, lo, hi) for lo, hi in groups]:
             term = gather_term(d, lo, hi)
             for b in range(lo // P, hi // P):
-                nc.tensor.matmul(
-                    turned[b][:],
+                a = 0 if b * P < WIDE else 1
+                c0 = b * P - groups[a][0]
+                turn_into(
+                    turned[a][:, c0 : c0 + P],
                     term[:, b * P - lo : (b + 1) * P - lo],
-                    ident[:],
-                    start=(d == 0),
-                    stop=(d == D - 2),
-                    is_transpose=True,
+                    d == 0 and c0 == 0,
+                    d == 1 and (b + 1) * P == groups[a][1],
                 )
-        partial = []
+        backs_out = [psum.tile([P, hi - lo], F32, name=f"back{a}", tag=f"bank{a}") for a, (lo, hi) in enumerate(groups)]
         for a, (lo, hi) in enumerate(groups):
-            back = psum.tile([P, hi - lo], F32, name=f"back{a}", tag=f"bank{a}")
             for b in range(lo // P, hi // P):
-                turned_sb = keep.tile([P, P], F32, name=f"turned_sb{b}")
-                nc.scalar.copy(turned_sb[:], turned[b][:])
-                nc.tensor.transpose(back[:, b * P - lo : (b + 1) * P - lo], turned_sb[:], ident[:])
-            partial.append(back)
+                turn_into(backs_out[a][:, b * P - lo : (b + 1) * P - lo], scaled[:, b * P : (b + 1) * P], b * P == lo, False)
+        for a, (lo, hi) in enumerate(groups):
+            turned_sb = keep.tile([P, hi - lo], F32, name=f"turned_sb{a}")
+            nc.scalar.copy(turned_sb[:], turned[a][:])
+            for b in range(lo // P, hi // P):
+                cols = slice(b * P - lo, (b + 1) * P - lo)
+                turn_into(backs_out[a][:, cols], turned_sb[:, cols], False, (b + 1) * P == hi)
 
-        last_terms = [gather_term(D - 1, lo, hi) for lo, hi in groups]
+        last_terms = [gather_term(D - 2, lo, hi) for lo, hi in groups]
         res = keep.tile([P, V], F32, name="res")
         for a, (lo, hi) in enumerate(groups):
-            nc.vector.tensor_tensor(res[:, lo:hi], partial[a][:], last_terms[a][:], ADD)
+            nc.vector.tensor_tensor(res[:, lo:hi], backs_out[a][:], last_terms[a][:], ADD)
         nc.sync.dma_start(out, res[:])

@@ -25,14 +25,13 @@ QUADRANT = 32
 BANKS = 8
 HALF_S = S // 2
 HALF_P = P // 2
-LAST = 384
-WIDE = V // 2
+GROUPS = [(0, 256), (256, 384), (384, 512)]
 
 COPY = mybir.ActivationFunctionType.Copy
-CHUNKS = [(512, 768), (0, 256), (768, 1024), (256, 512)]
+CHUNKS = [(512, 768), (0, 256), (768, 896), (256, 512), (896, 1024)]
 PAIR_TILES = [(0, 512), (512, 1024)]
 VECTOR_WEAVES = (1, 3)
-VECTOR_RELUS = (2,)
+VECTOR_RELUS = (4,)
 
 
 def tile_picked_devox_relu_p_kernel(
@@ -72,23 +71,26 @@ def tile_picked_devox_relu_p_kernel(
         w1_right = keep.tile([P, PACK, H // 2], F32, name="w1_right", tag="right")
         nc.sync.dma_start(w1_right[:], w1_rows[:, :, H // 2 : H])
         emb_rows = emb.rearrange("(p t) c -> p t c", t=PACK)
+        emb01 = keep.tile([P, 2, U], F32, name="emb01")
+        for e in range(2):
+            nc.sync.dma_start(emb01[e:P:2], emb.rearrange("(h m t) c -> t m h c", h=2, t=PACK)[e])
         pairs = [keep.tile([P, 2, hi - lo], F32, name=f"pairs{c}") for c, (lo, hi) in enumerate(PAIR_TILES)]
         for c, (lo, hi) in enumerate(PAIR_TILES):
             nc.sync.dma_start(pairs[c][:, 1, :], emb_rows[:, 2, lo:hi])
-        emb01 = keep.tile([P, 2, U], F32, name="emb01", tag="pair1")
-        nc.sync.dma_start(emb01[:], emb_rows[:, 0:2, :])
         emb3 = keep.tile([P, U], F32, name="emb3")
         nc.sync.dma_start(emb3[:], emb_rows[:, 3, :])
         gate_t = keep.tile([P, D - 1, V], F32, name="gate_t")
         nc.sync.dma_start(gate_t[:], gate[0 : D - 1].rearrange("d p v -> p d v"))
 
         windows = []
-        for t in range(4):
+        for t in range(3):
             window = keep.tile([P, U], F32, name=f"window{t}", tag=f"window{t}")
-            (nc.gpsimd if t == 3 else nc.vector).memset(window[:].bitcast(I32), 0)
+            nc.vector.memset(window[:].bitcast(I32), 0)
             windows.append(window)
         ident = keep.tile([P, P], F32, name="ident")
         make_identity(nc, ident[:])
+        ident_bf = keep.tile([P, P], BF16, name="ident_bf")
+        make_identity(nc, ident_bf[:])
 
         def deal(copy, dst, src, t0, t1):
             copy(
@@ -96,16 +98,19 @@ def tile_picked_devox_relu_p_kernel(
                 src.rearrange("p j (g e t) -> p g j e t", e=2, t=PACK)[:, :, :, :, t0:t1],
             )
 
+        def deal_pair(copy, dst, src):
+            copy(dst.rearrange("p m e j -> p m j e"), src.rearrange("p j (m t) -> p m j t", t=PACK)[:, :, :, 0:2])
+
         def quantize(codes, scales, src):
             nc.vector.quantize_mx(out=codes.bitcast(FP8X4), scales=scales, in_=src.rearrange("p t m j -> p (t m j)"))
 
         pair_codes = [keep.tile([P, P], U32, name=f"pair_codes{i}", align_bytes=64) for i in range(2)]
         w1_scales = [keep.tile([P, P], U8, name=f"w1_scales{i}", align_bytes=64) for i in range(PACK)]
-        lower_bf = keep.tile([P, 2, HALF_P, PACK], BF16, name="lower_bf", tag="lower", align_bytes=64)
-        deal(nc.scalar.copy, lower_bf[:, :, 0 : HALF_P // 2], w1_left[:, :, 0:P], 0, 2)
-        deal(nc.vector.tensor_copy, lower_bf[:, :, HALF_P // 2 : HALF_P], w1_left[:, :, P : 2 * P], 0, 2)
-        left_bf = keep.tile([P, 2, HALF_P, PACK], BF16, name="left_bf", align_bytes=64)
-        deal(nc.scalar.copy, left_bf[:], w1_left[:], 2, PACK)
+        lower_bf = keep.tile([P, HALF_P, 2, PACK], BF16, name="lower_bf", tag="lower", align_bytes=64)
+        deal_pair(nc.scalar.copy, lower_bf[:, 0 : HALF_P // 2], w1_left[:, :, 0:P])
+        deal_pair(nc.vector.tensor_copy, lower_bf[:, HALF_P // 2 : HALF_P], w1_left[:, :, P : 2 * P])
+        planes_bf = keep.tile([P, 2, P, PACK], BF16, name="planes_bf", align_bytes=64)
+        deal(nc.scalar.copy, planes_bf[:, :, 0:HALF_P], w1_left[:], 2, PACK)
         quantize(pair_codes[0][:], w1_scales[0][:], lower_bf[:])
         xs_picked = keep.tile([P, S], U8, name="xs_picked", tag="lower", align_bytes=64)
         nc.vector.tensor_copy(xs_picked[:], xs_all[:].indirect(offs_t[:]))
@@ -114,8 +119,6 @@ def tile_picked_devox_relu_p_kernel(
             nc.vector.tensor_copy(xw_picked[a][:], xw_all[:].indirect(entries(offs_t, a * HALF_S, (a + 1) * HALF_S)))
         plane_codes = keep.tile([P, 2 * P], U32, name="plane_codes", tag="stage2", align_bytes=64)
         w1_codes = [pair_codes[0][:], pair_codes[1][:], plane_codes[:, 0:P], plane_codes[:, P : 2 * P]]
-        for t in (2, 3):
-            quantize(w1_codes[t][:, 0:HALF_P], w1_scales[t][:, 0:HALF_P], left_bf[:, t - 2 : t - 1])
 
         pos_t = [load_list(f"pos{d}_t", src) for d, src in enumerate((pos1, pos2, pos3, pos4))]
         w2_codes = keep.tile([P, 2 * N], U8, name="w2_codes", align_bytes=64)
@@ -150,57 +153,55 @@ def tile_picked_devox_relu_p_kernel(
         def scatter_on_scalar(window, lo, hi, h):
             nc.scalar.activation(window[:].indirect(entries(cell_t, lo, hi)), h, COPY)
 
-        acc0 = product(0, 0, 0, HALF_S, 4)
-        acc1 = product(1, 0, HALF_S, LAST, 5)
-        acc2 = product(2, 0, LAST, S, 6)
-        for a, (acc, lo, hi) in enumerate(((acc0, 0, HALF_S), (acc1, HALF_S, LAST))):
-            h = keep.tile([P, hi - lo], F32, name=f"h_low{a}")
-            nc.scalar.activation(h[:], acc[:], RELU)
-            scatter_on_scalar(windows[1], lo, hi, h[:])
-        right_bf = keep.tile([P, PACK, HALF_P, PACK], BF16, name="right_bf", align_bytes=64)
-        deal(nc.vector.tensor_copy, right_bf[:], w1_right[:], 0, PACK)
-        h0 = keep.tile([P, S - LAST], F32, name="h0", tag="right")
-        nc.vector.tensor_scalar_max(h0[:], acc2[:], 0.0)
-        quantize(w1_codes[2][:, HALF_P:P], w1_scales[2][:, HALF_P:P], right_bf[:, 2:3])
-        quantize(w1_codes[1], w1_scales[1][:], right_bf[:, 0:2])
-        quantize(w1_codes[3][:, HALF_P:P], w1_scales[3][:, HALF_P:P], right_bf[:, 3:4])
-        scatter(windows[0], LAST, S, h0[:])
-        window4 = keep.tile([P, U], F32, name="window4", tag="scales", align_bytes=64)
-        nc.gpsimd.memset(window4[:], 0.0)
-        windows.append(window4)
+        acc_low = [product(a, 0, a * HALF_S, (a + 1) * HALF_S, 4 + a) for a in range(2)]
+        h_low0 = keep.tile([P, HALF_S], F32, name="h_low0")
+        nc.scalar.activation(h_low0[:], acc_low[0][:], RELU)
+        scatter_on_scalar(windows[0], 0, HALF_S, h_low0[:])
+        deal(nc.vector.tensor_copy, planes_bf[:, :, HALF_P:P], w1_right[:], 2, PACK)
+        upper_bf = keep.tile([P, HALF_P, 2, PACK], BF16, name="upper_bf", align_bytes=64)
+        quantize(w1_codes[2], w1_scales[2][:], planes_bf[:, 0:1])
+        deal_pair(nc.vector.tensor_copy, upper_bf[:], w1_right[:])
+        h_low1 = keep.tile([P, HALF_S], F32, name="h_low1", tag="right")
+        nc.vector.tensor_scalar_max(h_low1[:], acc_low[1][:], 0.0)
+        scatter_on_scalar(windows[0], HALF_S, S, h_low1[:])
+        quantize(w1_codes[1], w1_scales[1][:], upper_bf[:])
+        quantize(w1_codes[3], w1_scales[3][:], planes_bf[:, 1:2])
+        window3 = keep.tile([P, U], F32, name="window3", tag="scales", align_bytes=64)
+        nc.gpsimd.memset(window3[:], 0.0)
+        windows.append(window3)
 
         acc_p2 = product(3, 2, 0, S, 7)
-        h_p2 = keep.tile([P, S], F32, name="h_p2")
+        h_p2 = keep.tile([P, S], F32, name="h_p2", tag="h_plane")
         nc.vector.tensor_scalar_max(h_p2[:], acc_p2[:], 0.0)
-        scatter(windows[3], 0, S, h_p2[:])
-        acc_up = product(4, 1, 0, S, 4)
-        acc_p3 = [product(5 + a, 3, a * HALF_S, (a + 1) * HALF_S, 5 + a) for a in range(2)]
-        h_up = keep.tile([P, S], F32, name="h_up")
+        scatter(windows[2], 0, S, h_p2[:])
+        acc_up = product(4, 1, 0, S, 6)
+        acc_p3 = product(5, 3, 0, S, 4)
+        h_up = keep.tile([P, S], F32, name="h_up", tag="h_up")
         nc.scalar.activation(h_up[:], acc_up[:], RELU)
-        h_p3 = keep.tile([P, S], F32, name="h_p3")
-        scatter_on_scalar(windows[2], 0, HALF_S, h_up[:, 0:HALF_S])
-        nc.scalar.activation(h_p3[:, 0:HALF_S], acc_p3[0][:], RELU)
-        scatter_on_scalar(windows[2], HALF_S, S, h_up[:, HALF_S:S])
-        scatter(windows[4], 0, HALF_S, h_p3[:, 0:HALF_S])
-        nc.scalar.activation(h_p3[:, HALF_S:S], acc_p3[1][:], RELU)
-        scatter(windows[4], HALF_S, S, h_p3[:, HALF_S:S])
-
-        sums = [psum.tile([P, 2, 2, P], F32, name=f"sums{k}", tag=f"bank{k}") for k in range(4)]
+        scatter_on_scalar(windows[1], 0, HALF_S, h_up[:, 0:HALF_S])
+        scatter_on_scalar(windows[1], HALF_S, S, h_up[:, HALF_S:S])
+        h_p3 = keep.tile([P, S], F32, name="h_p3", tag="h_plane")
+        nc.vector.tensor_scalar_max(h_p3[:], acc_p3[:], 0.0)
+        scatter(windows[3], 0, S, h_p3[:])
 
         def turn_into(dst, src, start, stop):
             nc.tensor.matmul(dst, src, ident[:], start=start, stop=stop, is_transpose=True)
 
-        for b in range(U // P):
-            for e in range(2):
-                turn_into(sums[b // 2][:, b % 2, e, :], emb01[:, e, b * P : (b + 1) * P], b % 2 == 0 and e == 0, False)
-        for w, half in ((0, 0), (1, 0), (2, 1)):
-            for b in range(U // P):
-                turn_into(
-                    sums[b // 2][:, b % 2, :, half * HALF_P : (half + 1) * HALF_P],
-                    windows[w][:, b * P : (b + 1) * P],
-                    False,
-                    w == 2 and b % 2 == 1,
-                )
+        half_u = U // 2
+        lower_z = keep.tile([P, U], BF16, name="lower_z")
+        lower_turned = [psum.tile([P, half_u], BF16, name=f"lower_turned{k}", tag=f"bank{k}") for k in range(2)]
+        upper_turned = [psum.tile([P, half_u], F32, name=f"upper_turned{k}", tag=f"bank{7 - k}") for k in range(2)]
+        for c0 in range(0, U, P):
+            at = c0 % half_u
+            turn_into(upper_turned[c0 // half_u][:, at : at + P], emb01[:, 1, c0 : c0 + P], at == 0, False)
+        for lo, hi in PAIR_TILES:
+            nc.gpsimd.tensor_tensor(lower_z[:, lo:hi], windows[0][:, lo:hi], emb01[:, 0, lo:hi], ADD)
+        for c0 in range(0, U, P):
+            at = c0 % half_u
+            nc.tensor.transpose(lower_turned[c0 // half_u][:, at : at + P], lower_z[:, c0 : c0 + P], ident_bf[:])
+        for c0 in range(0, U, P):
+            at = c0 % half_u
+            turn_into(upper_turned[c0 // half_u][:, at : at + P], windows[1][:, c0 : c0 + P], False, at + P == half_u)
 
         def words_of(lo, hi):
             c = lo // (U // 2)
@@ -210,25 +211,21 @@ def tile_picked_devox_relu_p_kernel(
             return words_of(lo, hi)[:, 1, :].bitcast(BF16).rearrange("p (c e) -> p c e", e=2)[:, :, e]
 
         for lo, hi in PAIR_TILES:
-            nc.gpsimd.tensor_tensor(plane_of(lo, hi, 0), windows[3][:, lo:hi], words_of(lo, hi)[:, 1, :], ADD)
+            nc.gpsimd.tensor_tensor(plane_of(lo, hi, 0), windows[2][:, lo:hi], words_of(lo, hi)[:, 1, :], ADD)
 
-        backs = [psum.tile([P, U // 2], F32, name=f"backs{k}", tag=f"bank{6 + k}") for k in range(2)]
-        for k in range(4):
-            turned_z = keep.tile([P, 2 * 2 * P], BF16, name=f"turned_z{k}", tag=f"turned_z{k}", align_bytes=64)
-            nc.scalar.copy(
-                turned_z[:].rearrange("c (b p e) -> c b p e", b=2, e=2), sums[k][:].rearrange("c b e p -> c b p e")
-            )
-            for b2 in range(2):
-                b = 2 * k + b2
-                nc.tensor.transpose(
-                    backs[b // 4][:, (b % 4) * P : (b % 4 + 1) * P],
-                    turned_z[:].bitcast(F32)[:, b2 * P : (b2 + 1) * P],
-                    ident[:],
-                )
+        backs = [psum.tile([P, U // 2], F32, name=f"backs{k}", tag=f"bank{4 + k}") for k in range(2)]
+        turned_z = [keep.tile([P, half_u // P, 2, P], BF16, name=f"turned_z{k}", tag=("h_up", "turned_z")[k]) for k in range(2)]
+        for half, banks in enumerate((lower_turned, upper_turned)):
+            for k in range(2):
+                nc.scalar.copy(turned_z[k][:, :, half, :], banks[k][:].rearrange("c (b q) -> c b q", q=P))
+        for k in range(2):
+            words = turned_z[k][:].rearrange("c b h q -> c (b h q)").bitcast(F32)
+            for c0 in range(0, half_u, P):
+                nc.tensor.transpose(backs[k][:, c0 : c0 + P], words[:, c0 : c0 + P], ident[:])
         for k in range(2):
             nc.scalar.copy(pairs[k][:, 0, :], backs[k][:])
         for lo, hi in reversed(PAIR_TILES):
-            nc.vector.tensor_tensor(plane_of(lo, hi, 1), windows[4][:, lo:hi], emb3[:, lo:hi], ADD)
+            nc.vector.tensor_tensor(plane_of(lo, hi, 1), windows[3][:, lo:hi], emb3[:, lo:hi], ADD)
         z_bf = []
         for c, (lo, hi) in enumerate(CHUNKS):
             z = keep.tile([P, PACK * (hi - lo)], BF16, name=f"z_bf{c}", align_bytes=64)
@@ -242,7 +239,7 @@ def tile_picked_devox_relu_p_kernel(
             z_codes = keep.tile([P, width], U32, name=f"z_codes{c}", align_bytes=64)
             z_scales = keep.tile([P, width], U8, name=f"z_scales{c}", align_bytes=64)
             nc.vector.quantize_mx(out=z_codes[:].bitcast(FP8X4), scales=z_scales[:], in_=z_bf[c][:])
-            y_acc = psum.tile([P, width], F32, name=f"y_acc{c}", tag=f"bank{c}")
+            y_acc = psum.tile([P, width], F32, name=f"y_acc{c}", tag=f"bank{(c + 7) % BANKS}")
             nc.tensor.matmul_mx(
                 out=y_acc[:],
                 lhsT=w2_codes[:].bitcast(FP4X4),
@@ -262,43 +259,49 @@ def tile_picked_devox_relu_p_kernel(
             nc.vector.tensor_tensor(term[:], y[:].indirect(entries(pos_t[d], lo, hi)), gate_t[:, d, lo:hi], MULT)
             return term
 
-        blocks = V // P
-        plain = keep.tile([P, V], F32, name="plain")
-        nc.scalar.activation(plain[:], y[:].indirect(pos_t[D - 1][:]), COPY)
-        turned_plain = psum.tile([P, V], F32, name="turned_plain", tag="bank5")
-        for b in range(blocks):
-            nc.tensor.transpose(turned_plain[:, b * P : (b + 1) * P], plain[:, b * P : (b + 1) * P], ident[:])
+        half_v = V // 2
+        halves = [(0, half_v), (half_v, V)]
         scaled = keep.tile([P, V], F32, name="scaled")
-        for b in range(blocks):
+        turned_plain = []
+        for a, (lo, hi) in enumerate(halves):
+            plain = keep.tile([P, half_v], F32, name=f"plain{a}")
+            nc.scalar.activation(plain[:], y[:].indirect(entries(pos_t[D - 1], lo, hi)), COPY)
+            bank = psum.tile([P, half_v], F32, name=f"turned_plain{a}", tag=f"bank{a}")
+            for c0 in range(0, half_v, P):
+                nc.tensor.transpose(bank[:, c0 : c0 + P], plain[:, c0 : c0 + P], ident[:])
+            turned_plain.append(bank)
+        for b in range(V // P):
+            c0 = b * P % half_v
             nc.scalar.activation(
-                scaled[:, b * P : (b + 1) * P], turned_plain[:, b * P : (b + 1) * P], COPY, scale=gate_col[:, b : b + 1]
+                scaled[:, b * P : (b + 1) * P],
+                turned_plain[b * P // half_v][:, c0 : c0 + P],
+                COPY,
+                scale=gate_col[:, b : b + 1],
             )
-        groups = [(0, WIDE), (WIDE, V)]
-        turned = [psum.tile([P, hi - lo], F32, name=f"turned{a}", tag=f"bank{6 + a}") for a, (lo, hi) in enumerate(groups)]
-        for d, lo, hi in [(0, 0, V)] + [(1, lo, hi) for lo, hi in groups]:
-            term = gather_term(d, lo, hi)
-            for b in range(lo // P, hi // P):
-                a = 0 if b * P < WIDE else 1
-                c0 = b * P - groups[a][0]
-                turn_into(
-                    turned[a][:, c0 : c0 + P],
-                    term[:, b * P - lo : (b + 1) * P - lo],
-                    d == 0 and c0 == 0,
-                    d == 1 and (b + 1) * P == groups[a][1],
-                )
-        backs_out = [psum.tile([P, hi - lo], F32, name=f"back{a}", tag=f"bank{a}") for a, (lo, hi) in enumerate(groups)]
-        for a, (lo, hi) in enumerate(groups):
-            for b in range(lo // P, hi // P):
-                turn_into(backs_out[a][:, b * P - lo : (b + 1) * P - lo], scaled[:, b * P : (b + 1) * P], b * P == lo, False)
-        for a, (lo, hi) in enumerate(groups):
+        turned = [psum.tile([P, hi - lo], F32, name=f"turned{a}", tag=f"bank{2 + a}") for a, (lo, hi) in enumerate(GROUPS)]
+        first_term = gather_term(0, 0, V)
+        for a, (lo, hi) in enumerate(GROUPS):
+            for c0 in range(lo, hi, P):
+                turn_into(turned[a][:, c0 - lo : c0 - lo + P], first_term[:, c0 : c0 + P], c0 == lo, False)
+        for a, (lo, hi) in enumerate(GROUPS):
+            term = gather_term(1, lo, hi)
+            for c0 in range(0, hi - lo, P):
+                turn_into(turned[a][:, c0 : c0 + P], term[:, c0 : c0 + P], False, c0 + P == hi - lo)
+        partial = [psum.tile([P, half_v], F32, name=f"partial{a}", tag=f"bank{5 + a}") for a in range(2)]
+        for c0 in range(0, V, P):
+            at = c0 % half_v
+            turn_into(partial[c0 // half_v][:, at : at + P], scaled[:, c0 : c0 + P], at == 0, False)
+        for a, (lo, hi) in enumerate(GROUPS):
             turned_sb = keep.tile([P, hi - lo], F32, name=f"turned_sb{a}")
             nc.scalar.copy(turned_sb[:], turned[a][:])
-            for b in range(lo // P, hi // P):
-                cols = slice(b * P - lo, (b + 1) * P - lo)
-                turn_into(backs_out[a][:, cols], turned_sb[:, cols], False, (b + 1) * P == hi)
+            for c0 in range(lo, hi, P):
+                at = c0 % half_v
+                turn_into(
+                    partial[c0 // half_v][:, at : at + P], turned_sb[:, c0 - lo : c0 - lo + P], False, at + P == half_v
+                )
 
-        last_terms = [gather_term(D - 2, lo, hi) for lo, hi in groups]
+        last_term = gather_term(D - 2, 0, V)
         res = keep.tile([P, V], F32, name="res")
-        for a, (lo, hi) in enumerate(groups):
-            nc.vector.tensor_tensor(res[:, lo:hi], backs_out[a][:], last_terms[a][:], ADD)
+        for a, (lo, hi) in enumerate(halves):
+            nc.vector.tensor_tensor(res[:, lo:hi], partial[a][:], last_term[:, lo:hi], ADD)
         nc.sync.dma_start(out, res[:])

@@ -71,12 +71,17 @@ def tile_picked_devox_relu_p_kernel(
         w1_right = keep.tile([P, PACK, H // 2], F32, name="w1_right", tag="right")
         nc.sync.dma_start(w1_right[:], w1_rows[:, :, H // 2 : H])
         emb_rows = emb.rearrange("(p t) c -> p t c", t=PACK)
-        emb01 = keep.tile([P, 2, U], F32, name="emb01")
-        for e in range(2):
-            nc.sync.dma_start(emb01[e:P:2], emb.rearrange("(h m t) c -> t m h c", h=2, t=PACK)[e])
+        def load_pair_rows(half):
+            rows = keep.tile([P, U], F32, name=f"emb_pair{half}")
+            for e in range(2):
+                nc.sync.dma_start(rows[e:P:2, :], emb.rearrange("(h m t) c -> h t m c", h=2, t=PACK)[half, e])
+            return rows
+
+        emb_lower = load_pair_rows(0)
         pairs = [keep.tile([P, 2, hi - lo], F32, name=f"pairs{c}") for c, (lo, hi) in enumerate(PAIR_TILES)]
         for c, (lo, hi) in enumerate(PAIR_TILES):
             nc.sync.dma_start(pairs[c][:, 1, :], emb_rows[:, 2, lo:hi])
+        emb_upper = load_pair_rows(1)
         emb3 = keep.tile([P, U], F32, name="emb3")
         nc.sync.dma_start(emb3[:], emb_rows[:, 3, :])
         gate_t = keep.tile([P, D - 1, V], F32, name="gate_t")
@@ -159,49 +164,55 @@ def tile_picked_devox_relu_p_kernel(
         scatter_on_scalar(windows[0], 0, HALF_S, h_low0[:])
         deal(nc.vector.tensor_copy, planes_bf[:, :, HALF_P:P], w1_right[:], 2, PACK)
         upper_bf = keep.tile([P, HALF_P, 2, PACK], BF16, name="upper_bf", align_bytes=64)
-        quantize(w1_codes[2], w1_scales[2][:], planes_bf[:, 0:1])
+        for t in (2, 3):
+            quantize(w1_codes[t], w1_scales[t][:], planes_bf[:, t - 2 : t - 1])
         deal_pair(nc.vector.tensor_copy, upper_bf[:], w1_right[:])
+        quantize(w1_codes[1], w1_scales[1][:], upper_bf[:])
         h_low1 = keep.tile([P, HALF_S], F32, name="h_low1", tag="right")
         nc.vector.tensor_scalar_max(h_low1[:], acc_low[1][:], 0.0)
         scatter_on_scalar(windows[0], HALF_S, S, h_low1[:])
-        quantize(w1_codes[1], w1_scales[1][:], upper_bf[:])
-        quantize(w1_codes[3], w1_scales[3][:], planes_bf[:, 1:2])
         window3 = keep.tile([P, U], F32, name="window3", tag="scales", align_bytes=64)
         nc.gpsimd.memset(window3[:], 0.0)
         windows.append(window3)
 
-        acc_p2 = product(3, 2, 0, S, 7)
-        h_p2 = keep.tile([P, S], F32, name="h_p2", tag="h_plane")
-        nc.vector.tensor_scalar_max(h_p2[:], acc_p2[:], 0.0)
-        scatter(windows[2], 0, S, h_p2[:])
-        acc_up = product(4, 1, 0, S, 6)
-        acc_p3 = product(5, 3, 0, S, 4)
-        h_up = keep.tile([P, S], F32, name="h_up", tag="h_up")
-        nc.scalar.activation(h_up[:], acc_up[:], RELU)
+        acc_planes = [product(3 + a, 2 + a, 0, S, (7, 3)[a]) for a in range(2)]
+        acc_up = [product(5 + a, 1, a * HALF_S, (a + 1) * HALF_S, (6, 2)[a]) for a in range(2)]
+        h_planes = [keep.tile([P, S], F32, name=f"h_plane{a}") for a in range(2)]
+        h_up = keep.tile([P, HALF_S], F32, name="h_up")
+        for a in range(2):
+            nc.vector.tensor_scalar_max(h_planes[a][:], acc_planes[a][:], 0.0)
+        nc.vector.tensor_scalar_max(h_up[:, 0:HALF_S], acc_up[0][:], 0.0)
+        for a in range(2):
+            scatter(windows[2 + a], 0, S, h_planes[a][:])
         scatter_on_scalar(windows[1], 0, HALF_S, h_up[:, 0:HALF_S])
-        scatter_on_scalar(windows[1], HALF_S, S, h_up[:, HALF_S:S])
-        h_p3 = keep.tile([P, S], F32, name="h_p3", tag="h_plane")
-        nc.vector.tensor_scalar_max(h_p3[:], acc_p3[:], 0.0)
-        scatter(windows[3], 0, S, h_p3[:])
 
         def turn_into(dst, src, start, stop):
             nc.tensor.matmul(dst, src, ident[:], start=start, stop=stop, is_transpose=True)
 
         half_u = U // 2
-        lower_z = keep.tile([P, U], BF16, name="lower_z")
-        lower_turned = [psum.tile([P, half_u], BF16, name=f"lower_turned{k}", tag=f"bank{k}") for k in range(2)]
+        lower_z = keep.tile([P, half_u], BF16, name="lower_z")
+        lower_turned = [
+            psum.tile([P, half_u], (BF16, F32)[k], name=f"lower_turned{k}", tag=f"bank{3 * k}") for k in range(2)
+        ]
         upper_turned = [psum.tile([P, half_u], F32, name=f"upper_turned{k}", tag=f"bank{7 - k}") for k in range(2)]
-        for c0 in range(0, U, P):
-            at = c0 % half_u
-            turn_into(upper_turned[c0 // half_u][:, at : at + P], emb01[:, 1, c0 : c0 + P], at == 0, False)
-        for lo, hi in PAIR_TILES:
-            nc.gpsimd.tensor_tensor(lower_z[:, lo:hi], windows[0][:, lo:hi], emb01[:, 0, lo:hi], ADD)
-        for c0 in range(0, U, P):
-            at = c0 % half_u
-            nc.tensor.transpose(lower_turned[c0 // half_u][:, at : at + P], lower_z[:, c0 : c0 + P], ident_bf[:])
-        for c0 in range(0, U, P):
-            at = c0 % half_u
-            turn_into(upper_turned[c0 // half_u][:, at : at + P], windows[1][:, c0 : c0 + P], False, at + P == half_u)
+
+        def turn_half(bank, src, k, first):
+            for at in range(0, half_u, P):
+                c0 = k * half_u + at
+                turn_into(bank[:, at : at + P], src[:, c0 : c0 + P], first and at == 0, not first and at + P == half_u)
+
+        turn_half(lower_turned[1], emb_lower, 1, True)
+        turn_half(lower_turned[1], windows[0], 1, False)
+        for k in range(2):
+            turn_half(upper_turned[k], emb_upper, k, True)
+        nc.gpsimd.tensor_tensor(lower_z[:], windows[0][:, 0:half_u], emb_lower[:, 0:half_u], ADD)
+        for at in range(0, half_u, P):
+            nc.tensor.transpose(lower_turned[0][:, at : at + P], lower_z[:, at : at + P], ident_bf[:])
+        h_up1 = keep.tile([P, HALF_S], F32, name="h_up1", tag="window0")
+        nc.scalar.activation(h_up1[:], acc_up[1][:], RELU)
+        scatter_on_scalar(windows[1], HALF_S, S, h_up1[:])
+        for k in range(2):
+            turn_half(upper_turned[k], windows[1], k, False)
 
         def words_of(lo, hi):
             c = lo // (U // 2)
@@ -214,7 +225,7 @@ def tile_picked_devox_relu_p_kernel(
             nc.gpsimd.tensor_tensor(plane_of(lo, hi, 0), windows[2][:, lo:hi], words_of(lo, hi)[:, 1, :], ADD)
 
         backs = [psum.tile([P, U // 2], F32, name=f"backs{k}", tag=f"bank{4 + k}") for k in range(2)]
-        turned_z = [keep.tile([P, half_u // P, 2, P], BF16, name=f"turned_z{k}", tag=("h_up", "turned_z")[k]) for k in range(2)]
+        turned_z = [keep.tile([P, half_u // P, 2, P], BF16, name=f"turned_z{k}", tag=("window0", "turned_z")[k]) for k in range(2)]
         for half, banks in enumerate((lower_turned, upper_turned)):
             for k in range(2):
                 nc.scalar.copy(turned_z[k][:, :, half, :], banks[k][:].rearrange("c (b q) -> c b q", q=P))

@@ -28,10 +28,10 @@ HALF_P = P // 2
 GROUPS = [(0, 256), (256, 384), (384, 512)]
 
 COPY = mybir.ActivationFunctionType.Copy
-CHUNKS = [(512, 768), (0, 256), (768, 896), (256, 512), (896, 1024)]
+EARLY_CHUNKS = [(0, 256), (256, 512)]
+LATE_CHUNKS = [(512, 768), (768, 896), (896, 1024)]
+LATE_ORDER = [LATE_CHUNKS[0], LATE_CHUNKS[2], LATE_CHUNKS[1]]
 PAIR_TILES = [(0, 512), (512, 1024)]
-VECTOR_WEAVES = (1, 3)
-VECTOR_RELUS = (4,)
 
 
 def tile_picked_devox_relu_p_kernel(
@@ -110,13 +110,15 @@ def tile_picked_devox_relu_p_kernel(
             nc.vector.quantize_mx(out=codes.bitcast(FP8X4), scales=scales, in_=src.rearrange("p t m j -> p (t m j)"))
 
         pair_codes = [keep.tile([P, P], U32, name=f"pair_codes{i}", align_bytes=64) for i in range(2)]
-        w1_scales = [keep.tile([P, P], U8, name=f"w1_scales{i}", align_bytes=64) for i in range(PACK)]
+        pair_scales = [keep.tile([P, P], U8, name=f"pair_scales{i}", align_bytes=64) for i in range(2)]
+        plane_scales = keep.tile([P, 2 * P], U8, name="plane_scales", align_bytes=64)
+        w1_scales = [pair_scales[0][:], pair_scales[1][:], plane_scales[:, 0:P], plane_scales[:, P : 2 * P]]
         lower_bf = keep.tile([P, HALF_P, 2, PACK], BF16, name="lower_bf", tag="lower", align_bytes=64)
         deal_pair(nc.scalar.copy, lower_bf[:, 0 : HALF_P // 2], w1_left[:, :, 0:P])
         deal_pair(nc.vector.tensor_copy, lower_bf[:, HALF_P // 2 : HALF_P], w1_left[:, :, P : 2 * P])
         planes_bf = keep.tile([P, 2, P, PACK], BF16, name="planes_bf", align_bytes=64)
         deal(nc.scalar.copy, planes_bf[:, :, 0:HALF_P], w1_left[:], 2, PACK)
-        quantize(pair_codes[0][:], w1_scales[0][:], lower_bf[:])
+        quantize(pair_codes[0][:], w1_scales[0], lower_bf[:])
         xs_picked = keep.tile([P, S], U8, name="xs_picked", tag="lower", align_bytes=64)
         nc.vector.tensor_copy(xs_picked[:], xs_all[:].indirect(offs_t[:]))
         xw_picked = [keep.tile([P, HALF_S], U32, name=f"xw_picked{a}", align_bytes=64) for a in range(2)]
@@ -144,7 +146,7 @@ def tile_picked_devox_relu_p_kernel(
                 nc.tensor.matmul_mx(
                     out=h_acc[:, c0 - lo : c1 - lo],
                     lhsT=w1_codes[tile_no].bitcast(FP8X4),
-                    lhsT_scale=w1_scales[tile_no][:],
+                    lhsT_scale=w1_scales[tile_no],
                     rhs=xw_picked[a][:, c0 - a * HALF_S : c1 - a * HALF_S].bitcast(FP8X4),
                     rhs_scale=xs_picked[:, c0:c1],
                     start=True,
@@ -164,10 +166,9 @@ def tile_picked_devox_relu_p_kernel(
         scatter_on_scalar(windows[0], 0, HALF_S, h_low0[:])
         deal(nc.vector.tensor_copy, planes_bf[:, :, HALF_P:P], w1_right[:], 2, PACK)
         upper_bf = keep.tile([P, HALF_P, 2, PACK], BF16, name="upper_bf", align_bytes=64)
-        for t in (2, 3):
-            quantize(w1_codes[t], w1_scales[t][:], planes_bf[:, t - 2 : t - 1])
+        quantize(plane_codes[:], plane_scales[:], planes_bf[:])
         deal_pair(nc.vector.tensor_copy, upper_bf[:], w1_right[:])
-        quantize(w1_codes[1], w1_scales[1][:], upper_bf[:])
+        quantize(w1_codes[1], w1_scales[1], upper_bf[:])
         h_low1 = keep.tile([P, HALF_S], F32, name="h_low1", tag="right")
         nc.vector.tensor_scalar_max(h_low1[:], acc_low[1][:], 0.0)
         scatter_on_scalar(windows[0], HALF_S, S, h_low1[:])
@@ -237,20 +238,20 @@ def tile_picked_devox_relu_p_kernel(
             nc.scalar.copy(pairs[k][:, 0, :], backs[k][:])
         for lo, hi in reversed(PAIR_TILES):
             nc.vector.tensor_tensor(plane_of(lo, hi, 1), windows[3][:, lo:hi], emb3[:, lo:hi], ADD)
-        z_bf = []
-        for c, (lo, hi) in enumerate(CHUNKS):
-            z = keep.tile([P, PACK * (hi - lo)], BF16, name=f"z_bf{c}", align_bytes=64)
-            copy = nc.vector.tensor_copy if c in VECTOR_WEAVES else nc.scalar.copy
+
+        def weave(copy, lo, hi):
+            z = keep.tile([P, PACK * (hi - lo)], BF16, name=f"z_bf{lo}", align_bytes=64)
             copy(z[:].bitcast(F32).rearrange("p (c a) -> p c a", a=2), words_of(lo, hi).rearrange("p a c -> p c a"))
-            z_bf.append(z)
+            return z
 
         y = keep.tile([P, U], F32, name="y")
-        for c, (lo, hi) in enumerate(CHUNKS):
+
+        def second_product(z, lo, hi, bank):
             width = hi - lo
-            z_codes = keep.tile([P, width], U32, name=f"z_codes{c}", align_bytes=64)
-            z_scales = keep.tile([P, width], U8, name=f"z_scales{c}", align_bytes=64)
-            nc.vector.quantize_mx(out=z_codes[:].bitcast(FP8X4), scales=z_scales[:], in_=z_bf[c][:])
-            y_acc = psum.tile([P, width], F32, name=f"y_acc{c}", tag=f"bank{(c + 7) % BANKS}")
+            z_codes = keep.tile([P, width], U32, name=f"z_codes{lo}", align_bytes=64)
+            z_scales = keep.tile([P, width], U8, name=f"z_scales{lo}", align_bytes=64)
+            nc.vector.quantize_mx(out=z_codes[:].bitcast(FP8X4), scales=z_scales[:], in_=z[:])
+            y_acc = psum.tile([P, width], F32, name=f"y_acc{lo}", tag=f"bank{bank}")
             nc.tensor.matmul_mx(
                 out=y_acc[:],
                 lhsT=w2_codes[:].bitcast(FP4X4),
@@ -260,10 +261,19 @@ def tile_picked_devox_relu_p_kernel(
                 start=True,
                 stop=True,
             )
-            if c in VECTOR_RELUS:
-                nc.vector.tensor_scalar_max(y[:, lo:hi], y_acc[:], 0.0)
+            return y_acc
+
+        woven = {chunk: weave(nc.vector.tensor_copy, *chunk) for chunk in EARLY_CHUNKS}
+        for chunk in LATE_CHUNKS[:-1]:
+            woven[chunk] = weave(nc.scalar.copy, *chunk)
+        accs = [second_product(woven[chunk], *chunk, bank) for bank, chunk in enumerate(EARLY_CHUNKS)]
+        woven[LATE_CHUNKS[-1]] = weave(nc.vector.tensor_copy, *LATE_CHUNKS[-1])
+        accs.extend(second_product(woven[chunk], *chunk, (2, 3, 7)[i]) for i, chunk in enumerate(LATE_ORDER))
+        for i, (lo, hi) in enumerate(EARLY_CHUNKS + LATE_ORDER):
+            if i == len(accs) - 1:
+                nc.vector.tensor_scalar_max(y[:, lo:hi], accs[i][:], 0.0)
             else:
-                nc.scalar.activation(y[:, lo:hi], y_acc[:], RELU)
+                nc.scalar.activation(y[:, lo:hi], accs[i][:], RELU)
 
         def gather_term(d, lo, hi):
             term = keep.tile([P, hi - lo], F32, name=f"term{d}_{lo}")

@@ -78,10 +78,10 @@ def tile_picked_devox_relu_p_kernel(
             return rows
 
         emb_lower = load_pair_rows(0)
+        emb_upper = load_pair_rows(1)
         pairs = [keep.tile([P, 2, hi - lo], F32, name=f"pairs{c}") for c, (lo, hi) in enumerate(PAIR_TILES)]
         for c, (lo, hi) in enumerate(PAIR_TILES):
             nc.sync.dma_start(pairs[c][:, 1, :], emb_rows[:, 2, lo:hi])
-        emb_upper = load_pair_rows(1)
         emb3 = keep.tile([P, U], F32, name="emb3")
         nc.sync.dma_start(emb3[:], emb_rows[:, 3, :])
         gate_t = keep.tile([P, D - 1, V], F32, name="gate_t")
@@ -92,10 +92,6 @@ def tile_picked_devox_relu_p_kernel(
             window = keep.tile([P, U], F32, name=f"window{t}", tag=f"window{t}")
             nc.vector.memset(window[:].bitcast(I32), 0)
             windows.append(window)
-        ident = keep.tile([P, P], F32, name="ident")
-        make_identity(nc, ident[:])
-        ident_bf = keep.tile([P, P], BF16, name="ident_bf")
-        make_identity(nc, ident_bf[:])
 
         def deal(copy, dst, src, t0, t1):
             copy(
@@ -116,7 +112,7 @@ def tile_picked_devox_relu_p_kernel(
         lower_bf = keep.tile([P, HALF_P, 2, PACK], BF16, name="lower_bf", tag="lower", align_bytes=64)
         deal_pair(nc.scalar.copy, lower_bf[:, 0 : HALF_P // 2], w1_left[:, :, 0:P])
         deal_pair(nc.vector.tensor_copy, lower_bf[:, HALF_P // 2 : HALF_P], w1_left[:, :, P : 2 * P])
-        planes_bf = keep.tile([P, 2, P, PACK], BF16, name="planes_bf", align_bytes=64)
+        planes_bf = keep.tile([P, 2, P, PACK], BF16, name="planes_bf", tag="planes_bf", align_bytes=64)
         deal(nc.scalar.copy, planes_bf[:, :, 0:HALF_P], w1_left[:], 2, PACK)
         quantize(pair_codes[0][:], w1_scales[0], lower_bf[:])
         xs_picked = keep.tile([P, S], U8, name="xs_picked", tag="lower", align_bytes=64)
@@ -165,13 +161,17 @@ def tile_picked_devox_relu_p_kernel(
         nc.scalar.activation(h_low0[:], acc_low[0][:], RELU)
         scatter_on_scalar(windows[0], 0, HALF_S, h_low0[:])
         deal(nc.vector.tensor_copy, planes_bf[:, :, HALF_P:P], w1_right[:], 2, PACK)
-        upper_bf = keep.tile([P, HALF_P, 2, PACK], BF16, name="upper_bf", align_bytes=64)
+        upper_bf = keep.tile([P, HALF_P, 2, PACK], BF16, name="upper_bf", tag="upper_bf", align_bytes=64)
         quantize(plane_codes[:], plane_scales[:], planes_bf[:])
         deal_pair(nc.vector.tensor_copy, upper_bf[:], w1_right[:])
         quantize(w1_codes[1], w1_scales[1], upper_bf[:])
         h_low1 = keep.tile([P, HALF_S], F32, name="h_low1", tag="right")
         nc.vector.tensor_scalar_max(h_low1[:], acc_low[1][:], 0.0)
         scatter_on_scalar(windows[0], HALF_S, S, h_low1[:])
+        ident = keep.tile([P, P], F32, name="ident", tag="planes_bf", align_bytes=64)
+        make_identity(nc, ident[:])
+        ident_bf = keep.tile([P, P], BF16, name="ident_bf", tag="upper_bf", align_bytes=64)
+        make_identity(nc, ident_bf[:])
         window3 = keep.tile([P, U], F32, name="window3", tag="scales", align_bytes=64)
         nc.gpsimd.memset(window3[:], 0.0)
         windows.append(window3)

@@ -72,7 +72,7 @@ def tile_picked_devox_relu_p_kernel(
         nc.sync.dma_start(w1_right[:], w1_rows[:, :, H // 2 : H])
         emb_rows = emb.rearrange("(p t) c -> p t c", t=PACK)
         def load_pair_rows(half):
-            rows = keep.tile([P, U], F32, name=f"emb_pair{half}")
+            rows = keep.tile([P, U], F32, name=f"emb_pair{half}", tag=f"emb_pair{half}")
             for e in range(2):
                 nc.sync.dma_start(rows[e:P:2, :], emb.rearrange("(h m t) c -> h t m c", h=2, t=PACK)[half, e])
             return rows
@@ -164,17 +164,14 @@ def tile_picked_devox_relu_p_kernel(
         upper_bf = keep.tile([P, HALF_P, 2, PACK], BF16, name="upper_bf", tag="upper_bf", align_bytes=64)
         quantize(plane_codes[:], plane_scales[:], planes_bf[:])
         deal_pair(nc.vector.tensor_copy, upper_bf[:], w1_right[:])
-        quantize(w1_codes[1], w1_scales[1], upper_bf[:])
         h_low1 = keep.tile([P, HALF_S], F32, name="h_low1", tag="right")
         nc.vector.tensor_scalar_max(h_low1[:], acc_low[1][:], 0.0)
         scatter_on_scalar(windows[0], HALF_S, S, h_low1[:])
+        quantize(w1_codes[1], w1_scales[1], upper_bf[:])
         ident = keep.tile([P, P], F32, name="ident", tag="planes_bf", align_bytes=64)
         make_identity(nc, ident[:])
         ident_bf = keep.tile([P, P], BF16, name="ident_bf", tag="upper_bf", align_bytes=64)
         make_identity(nc, ident_bf[:])
-        window3 = keep.tile([P, U], F32, name="window3", tag="scales", align_bytes=64)
-        nc.gpsimd.memset(window3[:], 0.0)
-        windows.append(window3)
 
         acc_planes = [product(3 + a, 2 + a, 0, S, (7, 3)[a]) for a in range(2)]
         acc_up = [product(5 + a, 1, a * HALF_S, (a + 1) * HALF_S, (6, 2)[a]) for a in range(2)]
@@ -183,8 +180,7 @@ def tile_picked_devox_relu_p_kernel(
         for a in range(2):
             nc.vector.tensor_scalar_max(h_planes[a][:], acc_planes[a][:], 0.0)
         nc.vector.tensor_scalar_max(h_up[:, 0:HALF_S], acc_up[0][:], 0.0)
-        for a in range(2):
-            scatter(windows[2 + a], 0, S, h_planes[a][:])
+        scatter(windows[2], 0, S, h_planes[0][:])
         scatter_on_scalar(windows[1], 0, HALF_S, h_up[:, 0:HALF_S])
 
         def turn_into(dst, src, start, stop):
@@ -209,7 +205,8 @@ def tile_picked_devox_relu_p_kernel(
         nc.gpsimd.tensor_tensor(lower_z[:], windows[0][:, 0:half_u], emb_lower[:, 0:half_u], ADD)
         for at in range(0, half_u, P):
             nc.tensor.transpose(lower_turned[0][:, at : at + P], lower_z[:, at : at + P], ident_bf[:])
-        h_up1 = keep.tile([P, HALF_S], F32, name="h_up1", tag="window0")
+        scatter(windows[0], 0, S, h_planes[1][:])
+        h_up1 = keep.tile([P, HALF_S], F32, name="h_up1", tag="emb_pair0")
         nc.scalar.activation(h_up1[:], acc_up[1][:], RELU)
         scatter_on_scalar(windows[1], HALF_S, S, h_up1[:])
         for k in range(2):
@@ -226,7 +223,7 @@ def tile_picked_devox_relu_p_kernel(
             nc.gpsimd.tensor_tensor(plane_of(lo, hi, 0), windows[2][:, lo:hi], words_of(lo, hi)[:, 1, :], ADD)
 
         backs = [psum.tile([P, U // 2], F32, name=f"backs{k}", tag=f"bank{4 + k}") for k in range(2)]
-        turned_z = [keep.tile([P, half_u // P, 2, P], BF16, name=f"turned_z{k}", tag=("window0", "turned_z")[k]) for k in range(2)]
+        turned_z = [keep.tile([P, half_u // P, 2, P], BF16, name=f"turned_z{k}", tag=("emb_pair0", "turned_z")[k]) for k in range(2)]
         for half, banks in enumerate((lower_turned, upper_turned)):
             for k in range(2):
                 nc.scalar.copy(turned_z[k][:, :, half, :], banks[k][:].rearrange("c (b q) -> c b q", q=P))
@@ -237,7 +234,7 @@ def tile_picked_devox_relu_p_kernel(
         for k in range(2):
             nc.scalar.copy(pairs[k][:, 0, :], backs[k][:])
         for lo, hi in reversed(PAIR_TILES):
-            nc.vector.tensor_tensor(plane_of(lo, hi, 1), windows[3][:, lo:hi], emb3[:, lo:hi], ADD)
+            nc.vector.tensor_tensor(plane_of(lo, hi, 1), windows[0][:, lo:hi], emb3[:, lo:hi], ADD)
 
         def weave(copy, lo, hi):
             z = keep.tile([P, PACK * (hi - lo)], BF16, name=f"z_bf{lo}", align_bytes=64)

@@ -78,12 +78,12 @@ def tile_picked_devox_relu_p_kernel(
             return rows
 
         emb_lower = load_pair_rows(0)
-        emb_upper = load_pair_rows(1)
         pairs = [keep.tile([P, 2, hi - lo], F32, name=f"pairs{c}") for c, (lo, hi) in enumerate(PAIR_TILES)]
         for c, (lo, hi) in enumerate(PAIR_TILES):
             nc.sync.dma_start(pairs[c][:, 1, :], emb_rows[:, 2, lo:hi])
         emb3 = keep.tile([P, U], F32, name="emb3")
         nc.sync.dma_start(emb3[:], emb_rows[:, 3, :])
+        emb_upper = load_pair_rows(1)
         gate_t = keep.tile([P, D - 1, V], F32, name="gate_t")
         nc.sync.dma_start(gate_t[:], gate[0 : D - 1].rearrange("d p v -> p d v"))
 
@@ -176,7 +176,9 @@ def tile_picked_devox_relu_p_kernel(
         acc_planes = [product(3 + a, 2 + a, 0, S, (7, 3)[a]) for a in range(2)]
         acc_up = [product(5 + a, 1, a * HALF_S, (a + 1) * HALF_S, (6, 2)[a]) for a in range(2)]
         h_planes = [keep.tile([P, S], F32, name=f"h_plane{a}") for a in range(2)]
-        h_up = keep.tile([P, HALF_S], F32, name="h_up")
+        h_up = keep.tile([P, HALF_S], F32, name="h_up", tag="h_up0")
+        h_up1 = keep.tile([P, HALF_S], F32, name="h_up1", tag="h_up1")
+        nc.scalar.activation(h_up1[:], acc_up[1][:], RELU)
         for a in range(2):
             nc.vector.tensor_scalar_max(h_planes[a][:], acc_planes[a][:], 0.0)
         nc.vector.tensor_scalar_max(h_up[:, 0:HALF_S], acc_up[0][:], 0.0)
@@ -206,8 +208,6 @@ def tile_picked_devox_relu_p_kernel(
         for at in range(0, half_u, P):
             nc.tensor.transpose(lower_turned[0][:, at : at + P], lower_z[:, at : at + P], ident_bf[:])
         scatter(windows[0], 0, S, h_planes[1][:])
-        h_up1 = keep.tile([P, HALF_S], F32, name="h_up1", tag="emb_pair0")
-        nc.scalar.activation(h_up1[:], acc_up[1][:], RELU)
         scatter_on_scalar(windows[1], HALF_S, S, h_up1[:])
         for k in range(2):
             turn_half(upper_turned[k], windows[1], k, False)
@@ -223,7 +223,7 @@ def tile_picked_devox_relu_p_kernel(
             nc.gpsimd.tensor_tensor(plane_of(lo, hi, 0), windows[2][:, lo:hi], words_of(lo, hi)[:, 1, :], ADD)
 
         backs = [psum.tile([P, U // 2], F32, name=f"backs{k}", tag=f"bank{4 + k}") for k in range(2)]
-        turned_z = [keep.tile([P, half_u // P, 2, P], BF16, name=f"turned_z{k}", tag=("emb_pair0", "turned_z")[k]) for k in range(2)]
+        turned_z = [keep.tile([P, half_u // P, 2, P], BF16, name=f"turned_z{k}", tag=("h_up1", "h_up0")[k]) for k in range(2)]
         for half, banks in enumerate((lower_turned, upper_turned)):
             for k in range(2):
                 nc.scalar.copy(turned_z[k][:, :, half, :], banks[k][:].rearrange("c (b q) -> c b q", q=P))
@@ -267,7 +267,7 @@ def tile_picked_devox_relu_p_kernel(
         woven[LATE_CHUNKS[-1]] = weave(nc.vector.tensor_copy, *LATE_CHUNKS[-1])
         accs.extend(second_product(woven[chunk], *chunk, (2, 3, 7)[i]) for i, chunk in enumerate(LATE_ORDER))
         for i, (lo, hi) in enumerate(EARLY_CHUNKS + LATE_ORDER):
-            if i == len(accs) - 1:
+            if i == len(accs) - 2:
                 nc.vector.tensor_scalar_max(y[:, lo:hi], accs[i][:], 0.0)
             else:
                 nc.scalar.activation(y[:, lo:hi], accs[i][:], RELU)

@@ -267,7 +267,7 @@ def tile_picked_devox_relu_p_kernel(
         woven[LATE_CHUNKS[-1]] = weave(nc.vector.tensor_copy, *LATE_CHUNKS[-1])
         accs.extend(second_product(woven[chunk], *chunk, (2, 3, 7)[i]) for i, chunk in enumerate(LATE_ORDER))
         for i, (lo, hi) in enumerate(EARLY_CHUNKS + LATE_ORDER):
-            if i == len(accs) - 2:
+            if i == len(accs) - 3:
                 nc.vector.tensor_scalar_max(y[:, lo:hi], accs[i][:], 0.0)
             else:
                 nc.scalar.activation(y[:, lo:hi], accs[i][:], RELU)

from contextlib import ExitStack

import concourse.mybir as mybir
from concourse.masks import make_identity

K, T, S, D, V, H, N, U = 512, 2048, 512, 4, 512, 512, 128, 1024
FLOPS = 2 * K * H * S + 2 * H * N * U

F32 = mybir.dt.float32
BF16 = mybir.dt.bfloat16
I32 = mybir.dt.int32
U32 = mybir.dt.uint32
U16 = mybir.dt.uint16
U8 = mybir.dt.uint8
FP8X4 = mybir.dt.float8_e4m3fn_x4
FP4X4 = mybir.dt.float4_e2m1fn_x4
ADD = mybir.AluOpType.add
MULT = mybir.AluOpType.mult
RELU = mybir.ActivationFunctionType.Relu

P = 128
PACK = 4
PER_COLUMN = 16
QUADRANT = 32
BANKS = 8
HALF_S = S // 2
HALF_P = P // 2
GROUPS = [(0, 256), (256, 384), (384, 512)]

COPY = mybir.ActivationFunctionType.Copy
EARLY_CHUNKS = [(0, 256), (256, 512)]
LATE_CHUNKS = [(512, 768), (768, 896), (896, 1024)]
LATE_ORDER = [LATE_CHUNKS[0], LATE_CHUNKS[2], LATE_CHUNKS[1]]
PAIR_TILES = [(0, 512), (512, 1024)]


def tile_picked_devox_relu_p_kernel(
    tc, x_words, x_scales, w1, w2_words, w2_scales, gate, emb, offs, cell, pos1, pos2, pos3, pos4, out
):
    nc = tc.nc
    with ExitStack() as ctx:
        lists = ctx.enter_context(tc.tile_pool(name="lists", bufs=1))
        keep = ctx.enter_context(tc.tile_pool(name="keep", bufs=1))
        psum = ctx.enter_context(tc.psum_pool(name="psum", bufs=1))

        def load_list(name, src):
            tile = lists.tile([P, S // PER_COLUMN], U16, name=name)
            nc.sync.dma_start(tile[:], src)
            return tile

        def entries(list_tile, lo, hi):
            return list_tile[:, lo // PER_COLUMN : hi // PER_COLUMN]

        def load_scale_rows(plane, src):
            for q in range(P // QUADRANT):
                nc.sync.dma_start(
                    plane[QUADRANT * q : QUADRANT * q + PACK, :].bitcast(I32),
                    src[0, PACK * q : PACK * (q + 1), :].bitcast(I32),
                )

        xs_all = keep.tile([P, T], U8, name="xs_all", tag="scales", align_bytes=64)
        nc.gpsimd.memset(xs_all[:].bitcast(I32), 0)
        w1_rows = w1.rearrange("(p j) c -> p j c", j=PACK)
        w1_left = keep.tile([P, PACK, H // 2], F32, name="w1_left")
        nc.sync.dma_start(w1_left[:], w1_rows[:, :, 0 : H // 2])
        offs_t = load_list("offs_t", offs)
        load_scale_rows(xs_all, x_scales)
        xw_all = keep.tile([P, T], U32, name="xw_all", tag="stage2", align_bytes=64)
        nc.sync.dma_start(xw_all[:].bitcast(I32), x_words[0].rearrange("p n t -> p (n t)").bitcast(I32))
        cell_t = load_list("cell_t", cell)
        w1_right = keep.tile([P, PACK, H // 2], F32, name="w1_right", tag="right")
        nc.sync.dma_start(w1_right[:], w1_rows[:, :, H // 2 : H])
        emb_rows = emb.rearrange("(p t) c -> p t c", t=PACK)
        def load_pair_rows(half):
            rows = keep.tile([P, U], F32, name=f"emb_pair{half}", tag=f"emb_pair{half}")
            for e in range(2):
                nc.sync.dma_start(rows[e:P:2, :], emb.rearrange("(h m t) c -> h t m c", h=2, t=PACK)[half, e])
            return rows

        emb_lower = load_pair_rows(0)
        pairs = [keep.tile([P, 2, hi - lo], F32, name=f"pairs{c}") for c, (lo, hi) in enumerate(PAIR_TILES)]
        for c, (lo, hi) in enumerate(PAIR_TILES):
            nc.sync.dma_start(pairs[c][:, 1, :], emb_rows[:, 2, lo:hi])
        emb3 = keep.tile([P, U], F32, name="emb3")
        nc.sync.dma_start(emb3[:], emb_rows[:, 3, :])
        emb_upper = load_pair_rows(1)
        gate_t = keep.tile([P, D - 1, V], F32, name="gate_t")
        nc.sync.dma_start(gate_t[:], gate[0 : D - 1].rearrange("d p v -> p d v"))

        windows = []
        for t in range(3):
            window = keep.tile([P, U], F32, name=f"window{t}", tag=f"window{t}")
            nc.vector.memset(window[:].bitcast(I32), 0)
            windows.append(window)

        def deal(copy, dst, src, t0, t1):
            copy(
                dst.rearrange("p t (g e) j -> p g j e t", e=2),
                src.rearrange("p j (g e t) -> p g j e t", e=2, t=PACK)[:, :, :, :, t0:t1],
            )

        def deal_pair(copy, dst, src):
            copy(dst.rearrange("p m e j -> p m j e"), src.rearrange("p j (m t) -> p m j t", t=PACK)[:, :, :, 0:2])

        def quantize(codes, scales, src):
            nc.vector.quantize_mx(out=codes.bitcast(FP8X4), scales=scales, in_=src.rearrange("p t m j -> p (t m j)"))

        pair_codes = [keep.tile([P, P], U32, name=f"pair_codes{i}", align_bytes=64) for i in range(2)]
        pair_scales = [keep.tile([P, P], U8, name=f"pair_scales{i}", align_bytes=64) for i in range(2)]
        plane_scales = keep.tile([P, 2 * P], U8, name="plane_scales", align_bytes=64)
        w1_scales = [pair_scales[0][:], pair_scales[1][:], plane_scales[:, 0:P], plane_scales[:, P : 2 * P]]
        lower_bf = keep.tile([P, HALF_P, 2, PACK], BF16, name="lower_bf", tag="lower", align_bytes=64)
        deal_pair(nc.scalar.copy, lower_bf[:, 0 : HALF_P // 2], w1_left[:, :, 0:P])
        deal_pair(nc.vector.tensor_copy, lower_bf[:, HALF_P // 2 : HALF_P], w1_left[:, :, P : 2 * P])
        planes_bf = keep.tile([P, 2, P, PACK], BF16, name="planes_bf", tag="planes_bf", align_bytes=64)
        deal(nc.scalar.copy, planes_bf[:, :, 0:HALF_P], w1_left[:], 2, PACK)
        quantize(pair_codes[0][:], w1_scales[0], lower_bf[:])
        xs_picked = keep.tile([P, S], U8, name="xs_picked", tag="lower", align_bytes=64)
        nc.vector.tensor_copy(xs_picked[:], xs_all[:].indirect(offs_t[:]))
        xw_picked = [keep.tile([P, HALF_S], U32, name=f"xw_picked{a}", align_bytes=64) for a in range(2)]
        for a in range(2):
            nc.vector.tensor_copy(xw_picked[a][:], xw_all[:].indirect(entries(offs_t, a * HALF_S, (a + 1) * HALF_S)))
        plane_codes = keep.tile([P, 2 * P], U32, name="plane_codes", tag="stage2", align_bytes=64)
        w1_codes = [pair_codes[0][:], pair_codes[1][:], plane_codes[:, 0:P], plane_codes[:, P : 2 * P]]

        pos_t = [load_list(f"pos{d}_t", src) for d, src in enumerate((pos1, pos2, pos3, pos4))]
        w2_codes = keep.tile([P, 2 * N], U8, name="w2_codes", align_bytes=64)
        nc.sync.dma_start(w2_codes[:].bitcast(I32), w2_words[0].bitcast(I32))
        w2_plane = keep.tile([P, N], U8, name="w2_plane", align_bytes=64)
        nc.vector.memset(w2_plane[:].bitcast(I32), 0)
        load_scale_rows(w2_plane, w2_scales)

        gate_col = keep.tile([P, V // P], F32, name="gate_col")
        with nc.allow_non_contiguous_dma(reason="one gate value a partition"):
            nc.sync.dma_start(gate_col[:], gate[D - 1, 0, :].rearrange("(b p) -> p b", p=P))

        def product(i, tile_no, lo, hi, bank):
            h_acc = psum.tile([P, hi - lo], F32, name=f"h_acc{i}", tag=f"bank{bank}")
            cuts = sorted({lo, hi} | {c for c in (P, HALF_S) if lo < c < hi and (c == HALF_S or hi < HALF_S)})
            for c0, c1 in zip(cuts, cuts[1:]):
                a = c0 // HALF_S
                nc.tensor.matmul_mx(
                    out=h_acc[:, c0 - lo : c1 - lo],
                    lhsT=w1_codes[tile_no].bitcast(FP8X4),
                    lhsT_scale=w1_scales[tile_no],
                    rhs=xw_picked[a][:, c0 - a * HALF_S : c1 - a * HALF_S].bitcast(FP8X4),
                    rhs_scale=xs_picked[:, c0:c1],
                    start=True,
                    stop=True,
                )
            return h_acc

        def scatter(window, lo, hi, h):
            nc.vector.tensor_copy(window[:].indirect(entries(cell_t, lo, hi)), h)

        def scatter_on_scalar(window, lo, hi, h):
            nc.scalar.activation(window[:].indirect(entries(cell_t, lo, hi)), h, COPY)

        acc_low = [product(a, 0, a * HALF_S, (a + 1) * HALF_S, 4 + a) for a in range(2)]
        h_low0 = keep.tile([P, HALF_S], F32, name="h_low0")
        nc.scalar.activation(h_low0[:], acc_low[0][:], RELU)
        scatter_on_scalar(windows[0], 0, HALF_S, h_low0[:])
        deal(nc.vector.tensor_copy, planes_bf[:, :, HALF_P:P], w1_right[:], 2, PACK)
        upper_bf = keep.tile([P, HALF_P, 2, PACK], BF16, name="upper_bf", tag="upper_bf", align_bytes=64)
        quantize(plane_codes[:], plane_scales[:], planes_bf[:])
        deal_pair(nc.vector.tensor_copy, upper_bf[:], w1_right[:])
        h_low1 = keep.tile([P, HALF_S], F32, name="h_low1", tag="right")
        nc.vector.tensor_scalar_max(h_low1[:], acc_low[1][:], 0.0)
        scatter_on_scalar(windows[0], HALF_S, S, h_low1[:])
        quantize(w1_codes[1], w1_scales[1], upper_bf[:])
        ident = keep.tile([P, P], F32, name="ident", tag="planes_bf", align_bytes=64)
        make_identity(nc, ident[:])
        ident_bf = keep.tile([P, P], BF16, name="ident_bf", tag="upper_bf", align_bytes=64)
        make_identity(nc, ident_bf[:])

        acc_planes = [product(3 + a, 2 + a, 0, S, (7, 3)[a]) for a in range(2)]
        acc_up = [product(5 + a, 1, a * HALF_S, (a + 1) * HALF_S, (6, 2)[a]) for a in range(2)]
        h_planes = [keep.tile([P, S], F32, name=f"h_plane{a}") for a in range(2)]
        h_up = keep.tile([P, HALF_S], F32, name="h_up", tag="h_up0")
        h_up1 = keep.tile([P, HALF_S], F32, name="h_up1", tag="h_up1")
        nc.scalar.activation(h_up1[:], acc_up[1][:], RELU)
        for a in range(2):
            nc.vector.tensor_scalar_max(h_planes[a][:], acc_planes[a][:], 0.0)
        nc.vector.tensor_scalar_max(h_up[:, 0:HALF_S], acc_up[0][:], 0.0)
        scatter(windows[2], 0, S, h_planes[0][:])
        scatter_on_scalar(windows[1], 0, HALF_S, h_up[:, 0:HALF_S])

        def turn_into(dst, src, start, stop):
            nc.tensor.matmul(dst, src, ident[:], start=start, stop=stop, is_transpose=True)

        half_u = U // 2
        lower_z = keep.tile([P, half_u], BF16, name="lower_z")
        lower_turned = [
            psum.tile([P, half_u], (BF16, F32)[k], name=f"lower_turned{k}", tag=f"bank{3 * k}") for k in range(2)
        ]
        upper_turned = [psum.tile([P, half_u], F32, name=f"upper_turned{k}", tag=f"bank{7 - k}") for k in range(2)]

        def turn_half(bank, src, k, first):
            for at in range(0, half_u, P):
                c0 = k * half_u + at
                turn_into(bank[:, at : at + P], src[:, c0 : c0 + P], first and at == 0, not first and at + P == half_u)

        turn_half(lower_turned[1], emb_lower, 1, True)
        turn_half(lower_turned[1], windows[0], 1, False)
        for k in range(2):
            turn_half(upper_turned[k], emb_upper, k, True)
        nc.gpsimd.tensor_tensor(lower_z[:], windows[0][:, 0:half_u], emb_lower[:, 0:half_u], ADD)
        for at in range(0, half_u, P):
            nc.tensor.transpose(lower_turned[0][:, at : at + P], lower_z[:, at : at + P], ident_bf[:])
        scatter(windows[0], 0, S, h_planes[1][:])
        scatter_on_scalar(windows[1], HALF_S, S, h_up1[:])
        for k in range(2):
            turn_half(upper_turned[k], windows[1], k, False)

        def words_of(lo, hi):
            c = lo // (U // 2)
            return pairs[c][:, :, lo - c * U // 2 : hi - c * U // 2]

        def plane_of(lo, hi, e):
            return words_of(lo, hi)[:, 1, :].bitcast(BF16).rearrange("p (c e) -> p c e", e=2)[:, :, e]

        for lo, hi in PAIR_TILES:
            nc.gpsimd.tensor_tensor(plane_of(lo, hi, 0), windows[2][:, lo:hi], words_of(lo, hi)[:, 1, :], ADD)

        backs = [psum.tile([P, U // 2], F32, name=f"backs{k}", tag=f"bank{4 + k}") for k in range(2)]
        turned_z = [keep.tile([P, half_u // P, 2, P], BF16, name=f"turned_z{k}", tag=("h_up1", "h_up0")[k]) for k in range(2)]
        for half, banks in enumerate((lower_turned, upper_turned)):
            for k in range(2):
                nc.scalar.copy(turned_z[k][:, :, half, :], banks[k][:].rearrange("c (b q) -> c b q", q=P))
        for k in range(2):
            words = turned_z[k][:].rearrange("c b h q -> c (b h q)").bitcast(F32)
            for c0 in range(0, half_u, P):
                nc.tensor.transpose(backs[k][:, c0 : c0 + P], words[:, c0 : c0 + P], ident[:])
        for k in range(2):
            nc.scalar.copy(pairs[k][:, 0, :], backs[k][:])
        for lo, hi in reversed(PAIR_TILES):
            nc.vector.tensor_tensor(plane_of(lo, hi, 1), windows[0][:, lo:hi], emb3[:, lo:hi], ADD)

        def weave(copy, lo, hi):
            z = keep.tile([P, PACK * (hi - lo)], BF16, name=f"z_bf{lo}", align_bytes=64)
            copy(z[:].bitcast(F32).rearrange("p (c a) -> p c a", a=2), words_of(lo, hi).rearrange("p a c -> p c a"))
            return z

        y = keep.tile([P, U], F32, name="y")

        def second_product(z, lo, hi, bank):
            width = hi - lo
            z_codes = keep.tile([P, width], U32, name=f"z_codes{lo}", align_bytes=64)
            z_scales = keep.tile([P, width], U8, name=f"z_scales{lo}", align_bytes=64)
            nc.vector.quantize_mx(out=z_codes[:].bitcast(FP8X4), scales=z_scales[:], in_=z[:])
            y_acc = psum.tile([P, width], F32, name=f"y_acc{lo}", tag=f"bank{bank}")
            nc.tensor.matmul_mx(
                out=y_acc[:],
                lhsT=w2_codes[:].bitcast(FP4X4),
                lhsT_scale=w2_plane[:],
                rhs=z_codes[:].bitcast(FP8X4),
                rhs_scale=z_scales[:],
                start=True,
                stop=True,
            )
            return y_acc

        woven = {chunk: weave(nc.vector.tensor_copy, *chunk) for chunk in EARLY_CHUNKS}
        for chunk in LATE_CHUNKS[:-1]:
            woven[chunk] = weave(nc.scalar.copy, *chunk)
        accs = [second_product(woven[chunk], *chunk, bank) for bank, chunk in enumerate(EARLY_CHUNKS)]
        woven[LATE_CHUNKS[-1]] = weave(nc.vector.tensor_copy, *LATE_CHUNKS[-1])
        accs.extend(second_product(woven[chunk], *chunk, (2, 3, 7)[i]) for i, chunk in enumerate(LATE_ORDER))
        for i, (lo, hi) in enumerate(EARLY_CHUNKS + LATE_ORDER):
            if i == len(accs) - 3:
                nc.vector.tensor_scalar_max(y[:, lo:hi], accs[i][:], 0.0)
            else:
                nc.scalar.activation(y[:, lo:hi], accs[i][:], RELU)

        def gather_term(d, lo, hi):
            term = keep.tile([P, hi - lo], F32, name=f"term{d}_{lo}")
            nc.vector.tensor_tensor(term[:], y[:].indirect(entries(pos_t[d], lo, hi)), gate_t[:, d, lo:hi], MULT)
            return term

        half_v = V // 2
        halves = [(0, half_v), (half_v, V)]
        scaled = keep.tile([P, V], F32, name="scaled")
        turned_plain = []
        for a, (lo, hi) in enumerate(halves):
            plain = keep.tile([P, half_v], F32, name=f"plain{a}")
            nc.scalar.activation(plain[:], y[:].indirect(entries(pos_t[D - 1], lo, hi)), COPY)
            bank = psum.tile([P, half_v], F32, name=f"turned_plain{a}", tag=f"bank{a}")
            for c0 in range(0, half_v, P):
                nc.tensor.transpose(bank[:, c0 : c0 + P], plain[:, c0 : c0 + P], ident[:])
            turned_plain.append(bank)
        for b in range(V // P):
            c0 = b * P % half_v
            nc.scalar.activation(
                scaled[:, b * P : (b + 1) * P],
                turned_plain[b * P // half_v][:, c0 : c0 + P],
                COPY,
                scale=gate_col[:, b : b + 1],
            )
        turned = [psum.tile([P, hi - lo], F32, name=f"turned{a}", tag=f"bank{2 + a}") for a, (lo, hi) in enumerate(GROUPS)]
        first_term = gather_term(0, 0, V)
        for a, (lo, hi) in enumerate(GROUPS):
            for c0 in range(lo, hi, P):
                turn_into(turned[a][:, c0 - lo : c0 - lo + P], first_term[:, c0 : c0 + P], c0 == lo, False)
        for a, (lo, hi) in enumerate(GROUPS):
            term = gather_term(1, lo, hi)
            for c0 in range(0, hi - lo, P):
                turn_into(turned[a][:, c0 : c0 + P], term[:, c0 : c0 + P], False, c0 + P == hi - lo)
        partial = [psum.tile([P, half_v], F32, name=f"partial{a}", tag=f"bank{5 + a}") for a in range(2)]
        for c0 in range(0, V, P):
            at = c0 % half_v
            turn_into(partial[c0 // half_v][:, at : at + P], scaled[:, c0 : c0 + P], at == 0, False)
        for a, (lo, hi) in enumerate(GROUPS):
            turned_sb = keep.tile([P, hi - lo], F32, name=f"turned_sb{a}")
            nc.scalar.copy(turned_sb[:], turned[a][:])
            for c0 in range(lo, hi, P):
                at = c0 % half_v
                turn_into(
                    partial[c0 // half_v][:, at : at + P], turned_sb[:, c0 - lo : c0 - lo + P], False, at + P == half_v
                )

        last_term = gather_term(D - 2, 0, V)
        res = keep.tile([P, V], F32, name="res")
        for a, (lo, hi) in enumerate(halves):
            nc.vector.tensor_tensor(res[:, lo:hi], partial[a][:], last_term[:, lo:hi], ADD)
        nc.sync.dma_start(out, res[:])
